import numpy as np, ml_dtypes
CORES = [40,41,42,43,44,45,46,47]
N = 8
import mx_ref
BF = ml_dtypes.bfloat16
def gentries(a):
    return np.ascontiguousarray(a.reshape(8, 16, -1).transpose(0, 2, 1)).reshape(8, -1)
def gtable(e):
    e = np.asarray(e); return np.ascontiguousarray(e.reshape(8, -1, 16).transpose(0, 2, 1)).reshape(128, -1).astype(np.int32)
def gcols(t, e):
    v = np.concatenate([t.reshape(8, 16, -1, 4), np.zeros((8, 16, 1, 4), BF)], axis=2)
    return np.ascontiguousarray(np.stack([v[g][:, e[g]] for g in range(8)])).reshape(128, -1)
def tile(rs):
    return np.stack(rs, axis=2).reshape(128, -1).astype(BF)
def cut(t, i, w=512):
    return t[:, w * i:w * i + w]
def pick(q, e):
    c = np.concatenate([q[0].reshape(128, -1, 4), np.zeros((128, 1, 4), np.uint8)], axis=1); s = np.concatenate([q[1], np.ones((16, 1), np.uint8)], axis=1)
    return (np.ascontiguousarray(c[:, e].reshape(128, -1)), np.ascontiguousarray(s[:, e]))
def join(*qs):
    return (np.concatenate([q[0] for q in qs], axis=1), np.concatenate([q[1] for q in qs], axis=1))
def put(q, e, v):
    c, s = q[0].reshape(128, -1, 4).copy(), q[1].copy(); c[:, e] = v[0].reshape(128, -1, 4); s[:, e] = v[1]
    return (c.reshape(128, -1), s)
def pk(c, s):
    return (np.ascontiguousarray(c), mx_ref.live(s))
def emit(q):
    return q[0], q[1]
def packed(v, rng):
    q = [mx_ref.quantize(np.ascontiguousarray(v[r])) for r in range(N)]
    return np.stack([a for a, b in q]), np.stack([mx_ref.plane(b, rng) for a, b in q])
def values_of_codes():
    e, c = np.zeros((128, 128, 4), np.float32), np.zeros((128, 2, 4), np.uint8)
    e[np.arange(128), np.arange(128), 0] = 1
    c[:127, :, 0] = np.arange(256).reshape(2, 128).T[:127]
    return mx_ref.matmul(mx_ref.quantize(e.reshape(128, 512).astype(BF)), (c.reshape(128, 8), np.full((16, 2), 127, np.uint8))).T.reshape(-1).astype(np.float64)
CODE_VALUE, SCALE_VALUE = values_of_codes(), 2.0 ** (np.arange(256) - 127.0)
def decode(q):
    return (CODE_VALUE[q[0]].reshape(16, 8, -1, 4) * SCALE_VALUE[q[1]][:, None, :, None] + 0.0).reshape(128, -1).astype(np.float32)
def f(rng, *shape):
    return mx_ref.flush((rng.standard_normal(shape, dtype=np.float32) * np.exp2(rng.integers(-2, 3, shape[:-1] + (1,)))).astype(BF))
def wide(rng, *shape, cols=0):
    v = rng.standard_normal(shape, dtype=np.float32) * np.exp2(rng.integers(-12, 13, shape)).astype(np.float32)
    if cols: v *= np.repeat(np.exp2(rng.integers(-cols, cols + 1, shape[:-2] + (1, shape[-1] // 4))) * (rng.random(shape[:-2] + (1, shape[-1] // 4)) > 0.0625), 4, axis=-1).astype(np.float32)
    return mx_ref.flush(v.astype(BF))
C, A, R = 512, 256, 3
STEP = [1, 2, 4]
def partner(r, t):
    return r ^ STEP[t]
def big(v, k):
    v = v.astype(np.float32) * np.float32(k)
    v[np.abs(v) < np.float32(2.0 ** -16)] = 0
    return v.astype(BF)
def common(w, rng):
    c, p = packed(np.stack([w] * N), rng)
    return {"wc": c, "ws": p}
def weights(rng, q=-1):
    w = big(f(rng, 128, 2048), 1).reshape(128, 4, 128, 4)
    if q >= 0:
        w[16 * q:16 * q + 8] = 0
        for i in range(16 * q, 16 * q + 8):
            w[:, :, i] = 0
            for b in range(4): w[i, b, i, b] = 64
    return common(w.reshape(128, 2048), rng)
def numbers_of(rng):
    return {"x": big(f(rng, N, 128, 4 * C), 1), "u": np.array(f(rng, N, 128, 512)), "v": np.array(f(rng, N, 128, 512))}
def lists_of(rng):
    return {"m": np.argsort(rng.random((N, 8, C)), axis=2), "la": rng.integers(0, C, (N, 8, R * A)), "lb": rng.integers(0, C, (N, 8, R * A)),
            "ld": np.argsort(rng.random((N, 8, R, C)), axis=3)[:, :, :, :A].reshape(N, 8, R * A)}
def stored(l):
    return {k: np.stack([gtable(e) for e in l[k]]) for k in ("m", "la", "lb", "ld")}
def setup_inputs(rng):
    return {**numbers_of(rng), **stored(lists_of(rng)), **weights(rng)}
def setup_inputs_rolls(rng):
    d, l = numbers_of(rng), lists_of(rng)
    q = int(rng.integers(8))
    o = rng.permutation(N)
    back = []
    for r in range(N):
        g = rng.permutation(8)
        if o[r] % 3 == 2: g = rng.permutation(7)
        while abs(int(g[0]) - int(g[1])) < 2: g = np.roll(g, 1)
        back.append([[(0, 1), (1, 2), (2, 3)], [(0, 1), (2, 3), (0, 2)], [(0, 1), (0, 1), (0, 1)]][o[r] % 3])
        back[r] = [[int(g[i]) for i in e] for e in back[r]]
    size = np.exp2(np.array([-30.0, -12.0, 0.0, 10.0])[rng.permutation(N) % 4]).astype(np.float32)
    mark = np.zeros((27, 8, 4), np.float32)
    for k in range(9):
        for i in range(2):
            mark[k + 9 * i, :, 0] = i
            if k < 8: mark[k + 9 * i, k] = (0, 2, 0, 0)
        mark[18 + k, :, 1] = 2
        if k < 8: mark[18 + k, k] = 0
    x = d["x"].reshape(N, 8, 16, C, 4)
    u = d["u"].reshape(N, 128, 128, 4)
    u[:, :, ::16] = 0
    one = np.ones(N, np.float32)
    for r in range(N):
        if size[r] < 2.0 ** -20:
            for t in range(R): one[partner(r, t)] = 2.0 ** -30
    for g in range(8):
        u[:, 16 * q + g, 16 * g, 0] = one.astype(BF)
        u[:, 16 * q + g, 16 * g, 1] = (-one).astype(BF)
    for r in range(N):
        e = rng.permutation(C)
        written, pool = e[:A], e[A:]
        kind = rng.integers(0, 27, C)
        kind[l["m"][r, q, pool]] = np.arange(C - A) % 27
        x[r, q, :8] = (mark[kind].transpose(1, 0, 2) * size[r]).astype(BF)
        for t in range(R):
            l["ld"][r, q, A * t:A * t + A] = rng.permutation(written)
            p = back[partner(r, t)][t]
            most = o[partner(r, t)] == 2 and t == R - 1
            h = A - 1 if most else int(rng.integers(2, A // 4))
            n = np.full(8, h - 1)
            if (o[partner(r, t)] + t) % 2 == 0:
                n[min(p):] = h
                n[max(p)] = h + 1
            else:
                n[p] = h
                n[max(p) + 1:] = h
            k = np.full(2 * A, 8)
            if most: k[:A] = 26
            s = np.repeat(18 + np.arange(8), A - n) if most else np.repeat(np.arange(8), n)
            k[:len(s)] = s
            e = pool[k + 9 * rng.integers(0, 2, 2 * A) * (k < 9) + 27 * rng.integers(0, (C - A) // 27, 2 * A)]
            j = rng.permutation(A)
            l["la"][r, q, A * t:A * t + A] = e[:A][j]
            l["lb"][r, q, A * t:A * t + A] = e[A:][j]
    return {"x": x.reshape(N, 128, 4 * C), "u": u.reshape(N, 128, 512), "v": d["v"], **stored(l), **weights(rng, q)}
def setup_inputs_lists(rng):
    d, l = numbers_of(rng), lists_of(rng)
    o = rng.permutation(N)
    for r in range(N):
        if o[r] == 2:
            l["m"][r] = rng.permutation(C)[None, :]
            e = l["m"][r, 0, C - 8:]
            x = np.zeros((128, C, 4), BF)
            x[:, e] = d["x"][r].reshape(128, C, 4)[:, e]
            d["x"][r] = x.reshape(128, 4 * C)
            l["la"][r] %= C - 8
            l["lb"][r] %= C - 8
            l["ld"][r] = np.argsort(rng.random((8, R, C - 8)), axis=2)[:, :, :A].reshape(8, R * A)
        elif o[r] % 2:
            e = np.repeat(l["ld"][r, :, :1], R * A, axis=1)
            l["la"][r] = e
            l["lb"][r] = e
        else:
            e = l["ld"][r, :, :A].copy()
            l["ld"][r] = np.tile(e, (1, R))
            l["la"][r] = np.tile(e, (1, R))
            l["lb"][r] = np.tile(e[:, ::-1], (1, R))
    return {**d, **stored(l), **weights(rng)}
def setup_inputs_huge(rng):
    d, l = numbers_of(rng), lists_of(rng)
    o = rng.permutation(N)
    g = np.ones((N, 8))
    for r in range(N):
        if o[r] == 0: g[r] = -1
        if o[r] == 2: g[r, 0] = -1
        if o[r] > 2: g[r] = rng.permutation(8) % 2 * 2.0 - 1.0
    x = 2.0 ** 28 * (1.5 + 0.5 * rng.random((N, 128, 4 * C)))
    u = d["u"].reshape(N, 128, 128, 4)
    u[:, :, ::16] = (2.0 ** 30 * (0.75 + 0.25 * rng.random((N, 128, 8, 4))) * g[:, None, :, None]).astype(np.float32).astype(BF)
    w = np.zeros((128, 4, 128, 4), np.float32)
    i = np.arange(128)
    for b in range(4): w[i, b, i, b] = 32
    return {"x": x.astype(np.float32).astype(BF), "u": u.reshape(N, 128, 512), "v": d["v"], **stored(l), **common(w.reshape(128, 2048).astype(BF), rng)}
def setup_inputs_spread(rng):
    d = setup_inputs(rng)
    d["x"] = big(wide(rng, N, 128, 4 * C, cols=6), 1)
    return d
def check_inputs(d):
    b = []
    for k in ("x", "u", "v"):
        a = np.abs(d[k].astype(np.float32))
        if not (np.isfinite(a).all() and ((a == 0) | (a >= 2.0 ** -30) & (a <= 2.0 ** 30)).all()): b.append("a value of " + k)
    for r in range(N):
        if (np.sort(gentries(d["m"][r]), axis=1) != np.arange(C)).any(): b.append("m: a group's entries aren't a permutation")
        for k in ("la", "lb", "ld"):
            if ((d[k][r] < 0) | (d[k][r] >= C)).any(): b.append("an entry of " + k)
        s = np.sort(gentries(d["ld"][r]).reshape(8, R, A), axis=2)
        if (s[:, :, 1:] == s[:, :, :-1]).any(): b.append("ld: equal entries of a group in a round")
    if (d["wc"] != d["wc"][:1]).any(): b.append("wc differs between ranks")
    s = [mx_ref.live(p) for p in d["ws"]]
    if any((p != s[0]).any() for p in s): b.append("ws differs between ranks")
    return b
def reference(x, u, v, m, la, lb, ld, wc, ws):
    w = pk(wc[0], ws[0])
    qu = [mx_ref.quantize(u[r]) for r in range(N)]
    kept = [x[r] for r in range(N)]
    maps = [[gentries(m[r]).astype(np.int64)] for r in range(N)]
    for t in range(R):
        sent = []
        for r in range(N):
            now = maps[r][t]
            one = gcols(kept[r], np.take_along_axis(now, gentries(la[r])[:, A * t:A * t + A], axis=1))
            two = gcols(kept[r], np.take_along_axis(now, gentries(lb[r])[:, A * t:A * t + A], axis=1))
            q = mx_ref.quantize((one.astype(np.float32) + two.astype(np.float32)).astype(BF))
            h = tile([np.maximum(mx_ref.matmul(pick(w, np.arange(128 * b, 128 * b + 128)), q), np.float32(0.0)) * np.float32(0.015625) for b in range(4)])
            sent.append(mx_ref.quantize(h))
        came = decode(join(*sent)).astype(BF)
        for r in range(N):
            e = partner(r, t)
            yes = mx_ref.matmul(qu[r], sent[e])[::16] + np.float32(0.0) >= 0
            kept[r] = np.concatenate([kept[r], cut(came, e, 4 * A)], axis=1)
            to = gentries(ld[r])[:, A * t:A * t + A]
            new = maps[r][t].copy()
            for g in range(8): new[g, to[g][yes[g]]] = C + A * t + np.flatnonzero(yes[g])
            n = np.sum(~yes, axis=1)
            for g in np.argsort(-n, kind="stable")[:2]: new[g] = maps[r][max(t - 1, 0)][g]
            maps[r].append(new)
    y, om = np.zeros((N, 128, C), np.float32), np.zeros((N, 8, C), np.float32)
    oc, osc = np.zeros((N, 128, 4 * C), np.uint8), np.zeros((N, 16, C), np.uint8)
    for r in range(N):
        q = mx_ref.quantize(gcols(kept[r], maps[r][R]))
        y[r] = mx_ref.matmul(mx_ref.quantize(v[r]), q)
        om[r] = maps[r][R]
        oc[r], osc[r] = emit(q)
    return {"y": y, "om": om, "oc": oc, "osc": osc}

@@ -1,0 +1,507 @@
+import numpy as np
+from concourse.bass import DstId, RemoteDMATransfer
+from concourse.mybir import dt, AluOpType, AxisListType, ActivationFunctionType
+
+OP = AluOpType
+AF = ActivationFunctionType
+R = 3
+STEP = [1, 2, 4]
+GSN = 26
+
+SCRATCH = {
+    "Lst": ("sbuf", [128, 176], "int32"),
+    "X0": ("sbuf", [128, 2048], "bfloat16"),
+    "F": ("sbuf", [128, 5120], "bfloat16"),
+    "Ag": ("sbuf", [128, 1024], "bfloat16"),
+    "Z": ("sbuf", [128, 1024], "bfloat16"),
+    "Hb": ("sbuf", [128, 1024], "bfloat16"),
+    "Tt": ("sbuf", [128, 2048], "bfloat16"),
+    "uin": ("sbuf", [128, 512], "bfloat16"),
+    "vin": ("sbuf", [128, 512], "bfloat16"),
+    "ones": ("sbuf", [128, 520], "bfloat16"),
+    "ez": ("sbuf", [128, 520], "bfloat16"),
+    "vI": ("sbuf", [128, 256], "int32"),
+    "vJ": ("sbuf", [128, 256], "int32"),
+    "mask": ("sbuf", [128, 256], "bfloat16"),
+    "nmask": ("sbuf", [128, 256], "bfloat16"),
+    "idw": ("sbuf", [128, 512], "bfloat16"),
+    "m0r": ("sbuf", [128, 512], "bfloat16"),
+    "jr1": ("sbuf", [128, 256], "bfloat16"),
+    "Dd": ("sbuf", [128, 1024], "bfloat16"),
+    "Cc": ("sbuf", [128, 1024], "bfloat16"),
+    "val": ("sbuf", [128, 512], "bfloat16"),
+    "vs": ("sbuf", [128, 512], "bfloat16"),
+    "sgw": ("sbuf", [128, 3 * 272], "bfloat16"),
+    "sg2": ("sbuf", [128, 3 * 256], "bfloat16"),
+    "gx": ("sbuf", [128, 256 * GSN], "bfloat16"),
+    "gy": ("sbuf", [128, 256 * GSN], "bfloat16"),
+    "smi": ("sbuf", [128, 256], "int32"),
+    "smf": ("sbuf", [128, 3072], "float32"),
+    "smu": ("sbuf", [128, 1280], "uint16"),
+    "yo": ("sbuf", [128, 512], "float32"),
+    "ps": ("psum", [128, 4096], "float32"),
+    "wq": ("sbuf", [128, 512], "float8_e4m3fn_x4"), "wqs": ("sbuf", [128, 512], "uint8"),
+    "uq": ("sbuf", [128, 128], "float8_e4m3fn_x4"), "uqs": ("sbuf", [128, 128], "uint8"),
+    "up": ("sbuf", [128, 256], "float8_e4m3fn_x4"), "ups": ("sbuf", [128, 256], "uint8"),
+    "vq": ("sbuf", [128, 128], "float8_e4m3fn_x4"), "vqs": ("sbuf", [128, 128], "uint8"),
+    "eq": ("sbuf", [128, 512], "float8_e4m3fn_x4"), "eqs": ("sbuf", [128, 512], "uint8"),
+    "oq": ("sbuf", [128, 512], "float8_e4m3fn_x4"), "oqs": ("sbuf", [128, 512], "uint8"),
+}
+for _t in range(R):
+    for _n in ("qz", "lz", "qh"):
+        SCRATCH["%s%d" % (_n, _t)] = ("sbuf", [128, 256], "float8_e4m3fn_x4")
+        SCRATCH["%ss%d" % (_n, _t)] = ("sbuf", [128, 256], "uint8")
+ENG = {"v": "ve", "s": "ac", "t": "pe", "g": "gp"}
+LOADS = ["lm", "lx", "ll", "lu", "lw", "lv"]
+STORES = ["so0", "so1", "so2", "so3", "sy0", "sy1", "sy2", "sy3", "som", "sos"]
+SEMAPHORES = ["ve", "ac", "pe", "gp", "sent"] + ["arr%d%d" % (t, h) for t in range(R) for h in range(2)] + LOADS + STORES
+
+
+def rank_program(g, core, T, topo):
+    rank = T.rank_of(core)
+    if rank is None:
+        return
+    queue = {"v": g.vector, "s": g.scalar, "t": g.tensor, "g": g, "y": g.sync}
+    count = {}
+    known = {q: {} for q in queue}
+    writer, readers = {}, {}
+
+    def need(q, ev):
+        sem, val, snap = ev
+        k = known[q]
+        if k.get(sem, 0) < val:
+            queue[q].wait_ge(T.sem[sem], val)
+            k[sem] = val
+        for s in snap:
+            if k.get(s, 0) < snap[s]:
+                k[s] = snap[s]
+
+    def gate(q, r, w):
+        own = ENG.get(q)
+        evs = [writer[k] for k in r]
+        for k in w:
+            if k in writer and writer[k][0] != own:
+                evs.append(writer[k])
+            evs += [e for e in readers.get(k, {}).values() if e[0] != own]
+        for e in sorted(evs, key=lambda e: -e[1]):
+            need(q, e)
+
+    def note(ev, r, w):
+        for k in w:
+            writer[k] = ev
+            readers[k] = {}
+        for k in r:
+            readers.setdefault(k, {})[ev[0]] = ev
+
+    def do(q, call, r=(), w=()):
+        gate(q, r, w)
+        sem = ENG[q]
+        call(queue[q]).then_inc(T.sem[sem], 1)
+        count[sem] = count.get(sem, 0) + 1
+        note((sem, count[sem], dict(known[q])), r, w)
+
+    def dmas(q, sem, pairs, r=(), w=()):
+        gate(q, r, w)
+        for out, in_ in pairs:
+            queue[q].dma_start(out, in_).then_inc(T.sem[sem], 16)
+            count[sem] = count.get(sem, 0) + 16
+        note((sem, count[sem], dict(known[q])), r, w)
+
+    used = {"smf": 0, "smu": 0, "smi": 0, "gs": 0}
+
+    def small(n, buf="smf"):
+        a = -(-used[buf] // 32) * 32
+        used[buf] = a + n
+        return T[buf][:, a:a + n], (buf, a), a
+
+    def V(call, r=(), w=()):
+        do("v", call, r, w)
+
+    def S(call, r=(), w=()):
+        do("s", call, r, w)
+
+    def ts(out, in0, s1, s2, op0, op1, r, w):
+        if op1 is None:
+            V(lambda e: e.tensor_scalar(out, in0, s1, s2, op0), r, w)
+        else:
+            V(lambda e: e.tensor_scalar(out, in0, s1, s2, op0, op1), r, w)
+
+    def tt(out, a, b, op, r, w):
+        V(lambda e: e.tensor_tensor(out, a, b, op), r, w)
+
+    def gs_pick(win, wkeys, off, okey):
+        i = used["gs"]
+        used["gs"] = i + 1
+        tt(T.gx[:, 256 * i:256 * i + 256], win.indirect(off), T.mask[:], OP.mult, list(wkeys) + [okey, "mask"], [("gx", i)])
+        return i
+
+    def gs_scan(i):
+        V(lambda e: e.tensor_tensor_scan(T.gy[:, 256 * i:256 * i + 256], T.nmask[:], T.gx[:, 256 * i:256 * i + 256], 0.0, OP.mult, OP.add),
+          [("gx", i), "nmask"], [("gy", i)])
+        return T.gy[:, 256 * i + 15:256 * i + 256:16], [("gy", i)]
+
+    def gs(win, wkeys, off, okey):
+        return gs_scan(gs_pick(win, wkeys, off, okey))
+
+    def gs2(win, wkeys, o1, o2):
+        i = gs_pick(win, wkeys, *o1)
+        j = gs_pick(win, wkeys, *o2)
+        gs_scan(i)
+        gs_scan(j)
+        return T.gy[:, 256 * i + 15:256 * i + 512:16], [("gy", i), ("gy", j)]
+
+    L = T.Lst
+    dmas("y", "lm", [(L[:, 0:32], T.m[:])], w=["m_"])
+    dmas("s", "lm", [(L[:, 32:80], T.la[:])], w=["la_"])
+    dmas("y", "lm", [(L[:, 80:128], T.lb[:])], w=["lists"])
+    writer["lists"] = ("lm", 48, {})
+    dmas("s", "lx", [(T.X0[:], T.x[:])], w=["X0"])
+    dmas("y", "ll", [(L[:, 128:176], T.ld[:])], w=["ld_"])
+    dmas("y", "lu", [(T.uin[:], T.u[:])], w=["uin"])
+    dmas("y", "lw", [(T.wq[:].bitcast(dt.uint8), T.wc[:]), (T.wqs[:], T.ws[:])], w=["wq"])
+    dmas("y", "lv", [(T.vin[:], T.v[:])], w=["vin"])
+
+    pI, kpI, _ = small(32, "smi")
+    kI, kkI, _ = small(32, "smi")
+    do("g", lambda e: e.iota(T.vI[:], [[-1, 256]], 512, 1), w=["vI"])
+    do("g", lambda e: e.iota(pI, [[0, 32]], 0, 1), w=[kpI])
+    do("g", lambda e: e.iota(kI, [[16, 32]], 0, 0), w=[kkI])
+    do("g", lambda e: e.iota(T.idw[:], [[1, 512]], -256, 0, allow_small_or_imprecise_dtypes=True), w=["idw"])
+    do("g", lambda e: e.iota(T.jr1[:], [[1, 256]], 1, 0, allow_small_or_imprecise_dtypes=True), w=["jr1"])
+    eps, keps, _ = small(1)
+    V(lambda e: e.memset(T.Dd[:], 0.0), w=["D0", "D2"])
+    V(lambda e: e.memset(eps, 1e-37), w=[keps])
+    ts(T.vJ[:], T.vI[:], 15, None, OP.bitwise_and, None, ["vI"], ["vJ"])
+    ts(T.mask[:], T.vJ[:], 0, None, OP.is_equal, None, ["vJ"], ["mask"])
+    S(lambda e: e.activation(T.nmask[:], T.mask[:], AF.Identity, bias=1.0, scale=-1.0), ["mask"], ["nmask"])
+    V(lambda e: e.memset(T.ones[:], 1.0), w=["ones"])
+    do("g", lambda e: e.affine_select(T.ez[:], T.ones[:], [[-1, 520]], OP.is_equal, 0.0, 4, 4), ["ones"], ["ez"])
+    V(lambda e: e.memset(T.Cc[:], -1024.0), w=["C0", "C1"])
+    for t in range(R):
+        V(lambda e, t=t: e.memset(T.sgw[:, 272 * t:272 * t + 1], -1.0), w=[("pad", t)])
+    p15, kp15, _ = small(32, "smi")
+    p7, kp7, _ = small(32, "smi")
+    pg, kpg, _ = small(32, "smi")
+    idf, kidf, _ = small(32)
+    id16, kid16, _ = small(32, "smu")
+    fr8, kfr8, _ = small(32)
+    gfr, kgfr, _ = small(32)
+    U16, kU16, u0 = small(16, "smu")
+    ts(p7, pI, 7, None, OP.bitwise_and, None, [kpI], [kp7])
+    ts(p15, pI, 15, None, OP.bitwise_and, None, [kpI], [kp15])
+    ts(pg, pI, 4, None, OP.arith_shift_right, None, [kpI], [kpg])
+    tt(idf, p15, kI, OP.add, [kp15, kkI], [kidf])
+    ts(fr8, p7, 0.125, None, OP.mult, None, [kp7], [kfr8])
+    ts(gfr, pg, 0.125, None, OP.mult, None, [kpg], [kgfr])
+    V(lambda e: e.tensor_copy(id16, idf), [kidf], [kid16])
+    V(lambda e: e.tensor_copy(T.smu[:, u0:u0 + 8], T.smi[:, 32:40]), [kkI], [(kU16, 0)])
+    ts(T.smu[:, u0 + 8:u0 + 16], T.smi[:, kp7[1]:kp7[1] + 8], 16, None, OP.mult, None, [kp7], [(kU16, 1)])
+
+    L16, kL16, l0 = small(128, "smu")
+    D16, kD16, d0 = small(48, "smu")
+    Lf, kLf, lf = small(128)
+    V(lambda e: e.tensor_copy(L16, L[:, 0:128]), ["lists"], [kL16])
+
+    def la16(t):
+        return T.smu[:, l0 + 32 + 16 * t:l0 + 48 + 16 * t], kL16
+
+    def lb16(t):
+        return T.smu[:, l0 + 80 + 16 * t:l0 + 96 + 16 * t], kL16
+
+    idh = [(T.smu[:, kid16[1] + 16 * h:kid16[1] + 16 * h + 16], kid16) for h in range(2)]
+    V(lambda e: e.tensor_copy(T.m0r[:], T.idw[:].indirect(T.smu[:, l0:l0 + 32])), ["idw", kL16], ["m0r"])
+
+    zl = [small(128, "smu")[2] for _ in range(R + 1)]
+
+    def lists(t, half, src, keys, add):
+        for p in range(4):
+            a = zl[t] + 64 * half + 16 * p
+            ts(T.smu[:, a:a + 16], src, 4.0, float(4 * add + p), OP.mult, OP.add, keys, [("zl", t, half, p)])
+
+    def zoff(t, half, p, k):
+        a = zl[t] + 64 * half + 16 * p + 8 * k
+        return T.smu[:, a:a + 8]
+
+    for half, fn in ((0, la16), (1, lb16)):
+        y, ky = gs(T.m0r[:], ["m0r"], *fn(0))
+        lists(0, half, y, ky, 256)
+    m4 = []
+    for p in range(4):
+        o, ko, _ = small(32, "smu")
+        ts(o, L[:, 0:32], 4, p, OP.mult, OP.add, ["lists"], [ko])
+        m4.append((o, ko))
+
+    def fkeys(t):
+        return [("Fx", p) for p in range(4)] + [("Fn", s, h, b) for s in range(t) for h in range(2) for b in range(4)]
+
+    def operands(t):
+        win, wk = (T.X0[:], ["X0"]) if t == 0 else (T.F[:, 0:2048 + 1024 * t], fkeys(t))
+        for h in range(2):
+            for p in range(4):
+                S(lambda e, h=h, p=p: e.activation(T.Ag[:, 256 * p + 128 * h:256 * p + 128 * h + 128], win.indirect(zoff(t, 0, p, h)), AF.Copy),
+                  wk + [("zl", t, 0, p)], [("A", h, p)])
+        for h in range(2):
+            for p in range(4):
+                tt(T.Z[:, 512 * h + p:512 * h + 512:4], win.indirect(zoff(t, 1, p, h)), T.Ag[:, 256 * p + 128 * h:256 * p + 128 * h + 128],
+                   OP.add, wk + [("zl", t, 1, p), ("A", h, p)], [("Z", h, p)])
+            qz, qs = T["qz%d" % t], T["qzs%d" % t]
+            lo, hi = 128 * h, 128 * h + 128
+            V(lambda e: e.quantize_mx(qz[:, lo:hi], qs[:, lo:hi], T.Z[:, 4 * lo:4 * hi]), [("Z", h, p) for p in range(4)], [("qz", t, h)])
+            dst = T.cores[rank ^ STEP[t]]
+            rid, pid = topo.addr(dst)[:2]
+            eng = topo.engines(core, dst)
+            arr = T.sem["arr%d%d" % (t, h)]
+            gate("g", [("qz", t, h)], [])
+            m0, m1 = sum(1 << e for e in eng[0::2]), sum(1 << e for e in eng[1::2])
+            g.remote_dma(T["lz%d" % t][:, lo:hi].bitcast(dt.uint8), qz[:, lo:hi].bitcast(dt.uint8), arr, T.sem.sent, pid, rid, m0)
+            g.remote_dma(T["lzs%d" % t][:, lo:hi], qs[:, lo:hi], arr, T.sem.sent, pid, rid, m1)
+            count["sent"] = count.get("sent", 0) + len(eng)
+            count["arr%d%d" % (t, h)] = len(eng)
+            writer[("lz", t, h)] = ("arr%d%d" % (t, h), len(eng), {})
+
+    def bank(k, n=128):
+        return T.ps[:, 512 * k:512 * k + n]
+
+    def mm(k, lq, ls, rq, rs, r, n=128):
+        do("t", lambda e: e.matmul_mx(bank(k, n), lq, ls, rq, rs, True, True), r, [("bk", k)])
+
+    s1, s2 = [], []
+    for t in range(R):
+        s1.append([small(1) for _ in range(2)])
+        s2.append([small(1) for _ in range(2)])
+
+    def layer(t, h):
+        lo, hi = 128 * h, 128 * h + 128
+        for b in (0, 1, 2, 3):
+            mm(b, T.wq[:, 128 * b:128 * b + 128], T.wqs[:, 128 * b:128 * b + 128], T["lz%d" % t][:, lo:hi], T["lzs%d" % t][:, lo:hi], ["wq", ("lz", t, h)])
+        for b in (0, 1, 2, 3):
+            out = T.Hb[:, 4 * lo + b:4 * hi:4]
+            if b % 2:
+                S(lambda e: e.activation(out, bank(b), AF.Relu, scale=0.015625), [("bk", b)], [("H", h, b)])
+            else:
+                ts(out, bank(b), 0.0, 0.015625, OP.max, OP.mult, [("bk", b)], [("H", h, b)])
+        V(lambda e: e.quantize_mx(T["qh%d" % t][:, lo:hi], T["qhs%d" % t][:, lo:hi], T.Hb[:, 4 * lo:4 * hi]), [("H", h, b) for b in range(4)], [("qh", t, h)])
+
+    def scores(t, h):
+        lo, hi = 128 * h, 128 * h + 128
+        q, s = T["qh%d" % t][:, lo:hi], T["qhs%d" % t][:, lo:hi]
+        bs, bd = ((4, 5), (6, 7, 4, 5)) if h == 0 else ((6, 7), (0, 1, 2, 3))
+        for i in range(2):
+            mm(bs[i], T.up[:, 128 * i:128 * i + 128], T.ups[:, 128 * i:128 * i + 128], q, s, ["up", "ups", ("qh", t, h)])
+        out1 = T.sgw[:, 272 * t + 1 + lo:272 * t + 1 + hi]
+        out2 = T.sg2[:, 256 * t + lo:256 * t + hi]
+        S(lambda e: e.activation(out1, bank(bs[0]), AF.Sign, bias=eps, accum_out=s1[t][h][0]), [("bk", bs[0]), keps], [("sg", t, h), s1[t][h][1]])
+        S(lambda e: e.activation(out2, bank(bs[1]), AF.Sign, bias=eps, accum_out=s2[t][h][0]), [("bk", bs[1]), keps], [("sg2", t, h), s2[t][h][1]])
+        for b in range(4):
+            mm(bd[b], T.eq[:, 128 * b:128 * b + 128], T.eqs[:, 128 * b:128 * b + 128], q, s, [("eq", b), ("qh", t, h)])
+            base = 2048 + 1024 * t + 4 * lo
+            S(lambda e: e.activation(T.F[:, base + b:base + 512:4], bank(bd[b]), AF.Copy), [("bk", bd[b])], [("Fn", t, h, b)])
+
+    def value(t, h):
+        a = 256 * t + 128 * h
+        ts(T.vs[:, a:a + 128], T.sgw[:, 272 * t + 1 + 128 * h:272 * t + 129 + 128 * h], 1024.0, None, OP.mult, None, [("sg", t, h)], [("vs", t, h)])
+        tt(T.val[:, a:a + 128], T.vs[:, a:a + 128], T.jr1[:, 128 * h:128 * h + 128], OP.min, [("vs", t, h), "jr1"], [("val", t, h)])
+
+    def scatter(win, src, t, r, w):
+        V(lambda e: e.tensor_copy(win.indirect(T.smu[:, d0 + 16 * t:d0 + 16 * t + 16]), src), r + [kD16], [w])
+
+    def inverse(t, win, wk, o1, o2):
+        y, ky = gs2(win, wk, o1, o2)
+        n, kn, _ = small(32)
+        o, ko, oa = small(32, "smu")
+        ts(n, y, float(511 + 256 * t), None, OP.add, None, ky, [kn])
+        ts(o, n, float(-511 - 256 * t), None, OP.add, None, [kn], [ko])
+        return n, kn, oa, ko
+
+    own = [small(1) for _ in range(R)]
+
+    def own_half(t):
+        ts(own[t][0], s1[t][0][0], T.smf[:, kgfr[1]:kgfr[1] + 1], None, OP.add, None, [s1[t][0][1], kgfr], [own[t][1]])
+
+    keep = [small(1) for _ in range(R)]
+
+    def keep_steps(t):
+        kb, kkb, _ = small(32)
+        kt, kkt, ka = small(32)
+        c8, kc8, _ = small(8)
+        cn, kcn, _ = small(1)
+        return [
+            lambda: ts(kb, fr8, s2[t][0][0], s2[t][1][0], OP.add, OP.add, [kfr8, s2[t][0][1], s2[t][1][1]], [kkb]),
+            lambda: V(lambda e: e.transpose(kt, kb), [kkb], [kkt]),
+            lambda: ts(c8, T.smf[:, ka:ka + 8], own[t][0], s1[t][1][0], OP.subtract, OP.is_lt, [kkt, own[t][1], s1[t][1][1]], [kc8]),
+            lambda: V(lambda e: e.tensor_reduce(cn, c8, AxisListType.X, OP.add), [kc8], [kcn]),
+            lambda: ts(keep[t][0], cn, 2.0, None, OP.is_ge, None, [kcn], [keep[t][1]]),
+        ]
+
+    def bymax(a, ka, b, kb):
+        o, ko, _ = small(16)
+        tt(o, a, b, OP.max, ka + kb, [ko])
+        return o, [ko]
+
+    operands(0)
+    V(lambda e: e.tensor_copy(D16, L[:, 128:176]), ["ld_"], [kD16])
+    V(lambda e: e.quantize_mx(T.uq[:], T.uqs[:], T.uin[:]), ["uin"], ["uq"])
+    V(lambda e: e.tensor_copy(T.up[:].bitcast(dt.uint32), T.uq[:].bitcast(dt.uint32).indirect(U16)), ["uq", (kU16, 0), (kU16, 1)], ["up"])
+    for p in range(4):
+        S(lambda e, p=p: e.activation(T.F[:, p:2048:4], T.X0[:].indirect(m4[p][0]), AF.Copy), ["X0", m4[p][1]], [("Fx", p)])
+    S(lambda e: e.activation(T.ups[:], T.uqs[:].indirect(U16), AF.Copy), ["uq", (kU16, 0), (kU16, 1)], ["ups"])
+    scatter(T.Dd[:, 0:512], T.jr1[:], 0, ["jr1", "D0"], "D0")
+    for b in range(4):
+        V(lambda e, b=b: e.quantize_mx(T.eq[:, 128 * b:128 * b + 128], T.eqs[:, 128 * b:128 * b + 128], T.ez[:, 4 - b:516 - b]), ["ez"], [("eq", b)])
+    layer(0, 0)
+    np0, knp0, j0, kj0 = inverse(0, T.Dd[:, 0:512], ["D0"], la16(1), lb16(1))
+    scores(0, 0)
+    V(lambda e: e.tensor_copy(Lf, L[:, 0:128]), ["lists"], [kLf])
+    own_half(0)
+    layer(0, 1)
+    scores(0, 1)
+
+    def finish_j(t, np_, knp, ja, kj, base, kbase, after_keep):
+        npk, knpk, na = small(32)
+        win, wk = T.sgw[:, 272 * t:272 * t + 257], [("pad", t), ("sg", t, 0), ("sg", t, 1)]
+        st = keep_steps(t)
+        i = gs_pick(win, wk, T.smu[:, ja:ja + 16], kj)
+        st[0]()
+        st[1]()
+        y, ky = gs_scan(i)
+        for f in st[2:]:
+            f()
+        ts(npk, np_, keep[t][0], None, OP.mult, None, [knp, keep[t][1]], [knpk])
+        after_keep()
+        offs = []
+        for half in range(2):
+            if half:
+                y, ky = gs(win, wk, T.smu[:, ja + 16:ja + 32], kj)
+            tmp, ktmp, _ = small(16)
+            tt(tmp, y, T.smf[:, na + 16 * half:na + 16 * half + 16], OP.mult, ky + [knpk], [ktmp])
+            o, ko = bymax(tmp, [ktmp], base[half], kbase)
+            lists(t + 1, half, o, ko, 0)
+            offs.append((o, ko))
+        return offs
+
+    finish_j(0, np0, knp0, j0, kj0, [T.smf[:, lf + 48:lf + 64], T.smf[:, lf + 96:lf + 112]], [kLf], lambda: None)
+
+    def kplus(t):
+        k, kk, _ = small(1)
+        ts(k, keep[t][0], float(2511 + 256 * t), -2000.0, OP.mult, OP.add, [keep[t][1]], [kk])
+        return k, kk
+
+    operands(1)
+    kp0, kkp0 = kplus(0)
+    value(0, 0)
+    value(0, 1)
+    scatter(T.Cc[:, 0:512], T.val[:, 0:256], 0, [("val", 0, 0), ("val", 0, 1), "C0"], "C0")
+    y, ky = gs2(T.Cc[:, 0:512], ["C0"], la16(2), lb16(2))
+    ab2, kab2, aa = small(32)
+    V(lambda e: e.tensor_copy(T.smf[:, aa:aa + 16], T.smf[:, lf + 64:lf + 80]), [kLf], [(kab2, 0)])
+    V(lambda e: e.tensor_copy(T.smf[:, aa + 16:aa + 32], T.smf[:, lf + 112:lf + 128]), [kLf], [(kab2, 1)])
+    c0, kc0, _ = small(32)
+    p1, kp1, _ = small(32)
+    ts(c0, y, kp0, None, OP.add, None, ky + [kkp0], [kc0])
+    tt(p1, c0, ab2, OP.max, [kc0, (kab2, 0), (kab2, 1)], [kp1])
+    layer(1, 0)
+    scores(1, 0)
+    y, ky = gs2(T.Cc[:, 0:512], ["C0"], idh[0], idh[1])
+    c1, kc1, _ = small(32)
+    g1, kg1, _ = small(32)
+    ts(c1, y, kp0, None, OP.add, None, ky + [kkp0], [kc1])
+    tt(g1, c1, idf, OP.max, [kc1, kidf], [kg1])
+    value(1, 0)
+    own_half(1)
+    layer(1, 1)
+    scores(1, 1)
+    st = keep_steps(1)
+    value(1, 1)
+    scatter(T.Cc[:, 512:1024], T.val[:, 256:512], 1, [("val", 1, 0), ("val", 1, 1), "C1"], "C1")
+    i = gs_pick(T.Cc[:, 512:1024], ["C1"], *la16(2))
+    st[0]()
+    st[1]()
+    y, ky = gs_scan(i)
+    for fn in st[2:]:
+        fn()
+    kp1_, kkp1 = kplus(1)
+    pk, kpk, _ = small(32)
+    base, kbase, ba = small(32)
+    ts(pk, p1, keep[1][0], None, OP.mult, None, [kp1, keep[1][1]], [kpk])
+    tt(base, pk, ab2, OP.max, [kpk, (kab2, 0), (kab2, 1)], [kbase])
+    for half in range(2):
+        if half:
+            y, ky = gs(T.Cc[:, 512:1024], ["C1"], *lb16(2))
+        tmp, ktmp, _ = small(16)
+        ts(tmp, y, kp1_, None, OP.add, None, ky + [kkp1], [ktmp])
+        o, ko = bymax(tmp, [ktmp], T.smf[:, ba + 16 * half:ba + 16 * half + 16], [kbase])
+        lists(2, half, o, ko, 0)
+
+    operands(2)
+    scatter(T.Dd[:, 512:1024], T.jr1[:], 2, ["jr1", "D2"], "D2")
+    np2, knp2, j2, kj2 = inverse(2, T.Dd[:, 512:1024], ["D2"], idh[0], idh[1])
+    layer(2, 0)
+    scores(2, 0)
+    y, ky = gs2(T.Cc[:, 512:1024], ["C1"], idh[0], idh[1])
+    c2, kc2, _ = small(32)
+    g2, kg2, _ = small(32)
+    ts(c2, y, kp1_, None, OP.add, None, ky + [kkp1], [kc2])
+    tt(g2, c2, g1, OP.max, [kc2, kg1], [kg2])
+    g3, kg3, _ = small(32)
+    g4, kg4, _ = small(32)
+    ts(g3, g2, keep[1][0], None, OP.mult, None, [kg2, keep[1][1]], [kg3])
+    tt(g4, g3, idf, OP.max, [kg3, kidf], [kg4])
+    df, kdf, _ = small(32)
+    tt(df, g4, g1, OP.subtract, [kg4, kg1], [kdf])
+    V(lambda e: e.quantize_mx(T.vq[:], T.vqs[:], T.vin[:]), ["vin"], ["vq"])
+    own_half(2)
+    layer(2, 1)
+    scores(2, 1)
+    d1, kd1, _ = small(32)
+    fb, kfb, fa = small(32)
+
+    def final_base():
+        ts(d1, df, keep[2][0], None, OP.mult, None, [kdf, keep[2][1]], [kd1])
+        tt(fb, d1, g1, OP.add, [kd1, kg1], [kfb])
+
+    offs = finish_j(2, np2, knp2, j2, kj2, [T.smf[:, fa:fa + 16], T.smf[:, fa + 16:fa + 32]], [kfb], final_base)
+
+    win, wk = T.F[:], fkeys(3)
+
+    def gather_t(c, p, on_scalar):
+        out, off = T.Tt[:, 512 * c + p:512 * c + 512:4], zoff(3, c // 2, p, c % 2)
+        r, w = wk + [("zl", 3, c // 2, p)], [("T", c, p)]
+        if on_scalar:
+            S(lambda e: e.activation(out, win.indirect(off), AF.Copy), r, w)
+        else:
+            V(lambda e: e.tensor_copy(out, win.indirect(off)), r, w)
+
+    def om_out():
+        pl, kpl, pa = small(32)
+        ot, kot, oa = small(32)
+        for half in range(2):
+            o, ko = offs[half]
+            a, ka, _ = small(16)
+            b, kb, _ = small(16)
+            ts(a, o, 512.0, None, OP.is_ge, None, ko, [ka])
+            tt(b, a, o, OP.mult, ko + [ka], [kb])
+            tt(T.smf[:, pa + 16 * half:pa + 16 * half + 16], b, T.smf[:, lf + 16 * half:lf + 16 * half + 16], OP.max, [kb, kLf], [(kpl, half)])
+        V(lambda e: e.transpose(ot, pl), [(kpl, 0), (kpl, 1)], [kot])
+        dmas("y", "som", [(T.om[q:q + 1, :], T.smf[32 * (q // 2):32 * (q // 2) + 32, oa + 16 * (q % 2):oa + 16 * (q % 2) + 16]) for q in range(8)], [kot], ["om"])
+
+    def evac_y(c):
+        k = 4 + c
+        S(lambda e: e.activation(T.yo[:, 128 * c:128 * c + 128], bank(k), AF.Copy), [("bk", k)], [("yo", c)])
+        dmas("y", "sy%d" % c, [(T.y[:, 128 * c:128 * c + 128], T.yo[:, 128 * c:128 * c + 128])], [("yo", c)], [("y", c)])
+
+    for c in range(4):
+        for p in range(4):
+            gather_t(c, p, p < (3 if c == 0 else 2))
+        lo, hi = 128 * c, 128 * c + 128
+        V(lambda e: e.quantize_mx(T.oq[:, lo:hi], T.oqs[:, lo:hi], T.Tt[:, 4 * lo:4 * hi]), [("T", c, p) for p in range(4)], [("oq", c)])
+        mm(4 + c, T.vq[:], T.vqs[:], T.oq[:, lo:hi], T.oqs[:, lo:hi], ["vq", ("oq", c)])
+        if c:
+            evac_y(c - 1)
+        dmas("y", "so%d" % c, [(T.oc[:, 4 * lo:4 * hi], T.oq[:, lo:hi].bitcast(dt.uint8))], [("oq", c)], [("oc", c)])
+        if c == 1:
+            om_out()
+    evac_y(3)
+    dmas("s", "sos", [(T.osc[4 * k:4 * k + 4, :], T.oqs[32 * k:32 * k + 4, :]) for k in range(4)], [("oq", c) for c in range(4)], ["osc"])
+    for s in SEMAPHORES:
+        if known["g"].get(s, 0) < count.get(s, 0):
+            g.wait_ge(T.sem[s], count[s])

@@ -6,15 +6,19 @@ OP = AluOpType
 AF = ActivationFunctionType
 R = 3
 STEP = [1, 2, 4]
-GSN = 26
+LIFT = 2048
+BASE = 8192
+SL = 1280
+CYC, WAKE, NEAR, SEND, FLY, FIRST = 1.0, 130.0, 60.0, 600.0, 2200.0, 1000.0
+PLAN = {}
 
 SCRATCH = {
     "Lst": ("sbuf", [128, 176], "int32"),
     "X0": ("sbuf", [128, 2048], "bfloat16"),
-    "F": ("sbuf", [128, 5120], "bfloat16"),
-    "Ag": ("sbuf", [128, 1024], "bfloat16"),
-    "Z": ("sbuf", [128, 1024], "bfloat16"),
-    "Hb": ("sbuf", [128, 1024], "bfloat16"),
+    "F": ("sbuf", [128, 4 * SL], "bfloat16"),
+    "Ag": ("sbuf", [128, 3072], "bfloat16"),
+    "Z": ("sbuf", [128, 3072], "bfloat16"),
+    "Hb": ("sbuf", [128, 3072], "bfloat16"),
     "Tt": ("sbuf", [128, 2048], "bfloat16"),
     "uin": ("sbuf", [128, 512], "bfloat16"),
     "vin": ("sbuf", [128, 512], "bfloat16"),
@@ -22,21 +26,18 @@ SCRATCH = {
     "ez": ("sbuf", [128, 520], "bfloat16"),
     "vI": ("sbuf", [128, 256], "int32"),
     "vJ": ("sbuf", [128, 256], "int32"),
-    "mask": ("sbuf", [128, 256], "bfloat16"),
-    "nmask": ("sbuf", [128, 256], "bfloat16"),
+    "st": ("sbuf", [128, 1024], "bfloat16"),
     "idw": ("sbuf", [128, 512], "bfloat16"),
     "m0r": ("sbuf", [128, 512], "bfloat16"),
     "jr1": ("sbuf", [128, 256], "bfloat16"),
-    "Dd": ("sbuf", [128, 1024], "bfloat16"),
-    "Cc": ("sbuf", [128, 1024], "bfloat16"),
-    "val": ("sbuf", [128, 512], "bfloat16"),
-    "vs": ("sbuf", [128, 512], "bfloat16"),
+    "Dd": ("sbuf", [128, 1536], "bfloat16"),
     "sgw": ("sbuf", [128, 3 * 272], "bfloat16"),
     "sg2": ("sbuf", [128, 3 * 256], "bfloat16"),
-    "gx": ("sbuf", [128, 256 * GSN], "bfloat16"),
-    "gy": ("sbuf", [128, 256 * GSN], "bfloat16"),
+    "gx": ("sbuf", [128, 256 * 24], "bfloat16"),
+    "gyf": ("sbuf", [128, 256 * 16], "float32"),
+    "gyb": ("sbuf", [128, 256 * 12], "bfloat16"),
     "smi": ("sbuf", [128, 256], "int32"),
-    "smf": ("sbuf", [128, 3072], "float32"),
+    "smf": ("sbuf", [128, 4096], "float32"),
     "smu": ("sbuf", [128, 1280], "uint16"),
     "yo": ("sbuf", [128, 512], "float32"),
     "ps": ("psum", [128, 4096], "float32"),
@@ -57,6 +58,56 @@ STORES = ["so0", "so1", "so2", "so3", "sy0", "sy1", "sy2", "sy3", "som", "sos"]
 SEMAPHORES = ["ve", "ac", "pe", "gp", "sent"] + ["arr%d%d" % (t, h) for t in range(R) for h in range(2)] + LOADS + STORES
 
 
+def make_plan(ops, ready):
+    n = len(ops)
+    pred, succ, wrote, read = [[] for _ in ops], [[] for _ in ops], {}, {}
+    for i, o in enumerate(ops):
+        p = {}
+        for k in o["w"]:
+            for j in read.get(k, []) + ([wrote[k]] if k in wrote else []):
+                p[j] = False
+        for k in o["r"]:
+            if k in wrote:
+                p[wrote[k]] = True
+        for k in o["r"]:
+            read.setdefault(k, []).append(i)
+        for k in o["w"]:
+            wrote[k], read[k] = i, []
+        p.pop(i, None)
+        pred[i] = sorted(p.items())
+        for j in p:
+            succ[j].append(i)
+    rank = [0.0] * n
+    for i in range(n - 1, -1, -1):
+        o = ops[i]
+        rank[i] = min(c for _, c in o["q"].values()) + o["lag"] + max([WAKE + rank[j] for j in succ[i]] + [0.0])
+    free, fin, start, where, left = {}, [0.0] * n, [0.0] * n, [""] * n, [len(p) for p in pred]
+    cand = [i for i in range(n) if not left[i]]
+    for _ in range(n):
+        best = []
+        for i in cand:
+            o = ops[i]
+            t0 = max([ready.get(k, 0.0) for k in o["r"]] + [0.0])
+            opt = []
+            for q in o["q"]:
+                t = max(t0, free.get(q, 0.0))
+                for j, raw in pred[i]:
+                    t = max(t, fin[j] + WAKE if raw or where[j] != q else start[j])
+                opt.append((t + o["q"][q][1], t, q))
+            best.append((min(opt), i))
+        soon = min(b[0][1] for b in best)
+        pick = max((b for b in best if b[0][1] <= soon + NEAR), key=lambda b: (rank[b[1]], -b[1]))
+        (end, t, q), i = pick
+        start[i], fin[i], where[i] = t, end + ops[i]["lag"], q
+        free[q] = end
+        cand.remove(i)
+        for j in succ[i]:
+            left[j] -= 1
+            if not left[j]:
+                cand.append(j)
+    return [(i, where[i]) for i in sorted(range(n), key=lambda i: (start[i], i))]
+
+
 def rank_program(g, core, T, topo):
     rank = T.rank_of(core)
     if rank is None:
@@ -65,6 +116,7 @@ def rank_program(g, core, T, topo):
     count = {}
     known = {q: {} for q in queue}
     writer, readers = {}, {}
+    ops = []
 
     def need(q, ev):
         sem, val, snap = ev
@@ -93,13 +145,6 @@ def rank_program(g, core, T, topo):
         for k in r:
             readers.setdefault(k, {})[ev[0]] = ev
 
-    def do(q, call, r=(), w=()):
-        gate(q, r, w)
-        sem = ENG[q]
-        call(queue[q]).then_inc(T.sem[sem], 1)
-        count[sem] = count.get(sem, 0) + 1
-        note((sem, count[sem], dict(known[q])), r, w)
-
     def dmas(q, sem, pairs, r=(), w=()):
         gate(q, r, w)
         for out, in_ in pairs:
@@ -107,100 +152,129 @@ def rank_program(g, core, T, topo):
             count[sem] = count.get(sem, 0) + 16
         note((sem, count[sem], dict(known[q])), r, w)
 
-    used = {"smf": 0, "smu": 0, "smi": 0, "gs": 0}
+    def emit(o, q):
+        call = o["q"][q][0]
+        if o["kind"] != "call":
+            call(q)
+            return
+        gate(q, o["r"], o["w"])
+        sem = ENG[q]
+        call(queue[q]).then_inc(T.sem[sem], 1)
+        count[sem] = count.get(sem, 0) + 1
+        note((sem, count[sem], dict(known[q])), o["r"], o["w"])
+
+    def op(qs, r, w, lag=0.0, kind="call"):
+        ops.append({"q": qs, "r": list(r), "w": list(w), "lag": lag, "kind": kind})
+
+    used = {"smf": 0, "smu": 0, "smi": 0, "gx": 0, "gyf": 0, "gyb": 0}
 
     def small(n, buf="smf"):
         a = -(-used[buf] // 32) * 32
         used[buf] = a + n
         return T[buf][:, a:a + n], (buf, a), a
 
-    def V(call, r=(), w=()):
-        do("v", call, r, w)
+    def V(call, n, r=(), w=()):
+        op({"v": (call, max(64, n) * CYC)}, r, w)
 
-    def S(call, r=(), w=()):
-        do("s", call, r, w)
+    def G(call, n, r=(), w=()):
+        op({"g": (call, 150 + 2 * n * CYC)}, r, w)
 
-    def ts(out, in0, s1, s2, op0, op1, r, w):
+    def ts(out, in0, s1, s2, op0, op1, r, w, n=32):
         if op1 is None:
-            V(lambda e: e.tensor_scalar(out, in0, s1, s2, op0), r, w)
+            V(lambda e: e.tensor_scalar(out, in0, s1, s2, op0), n, r, w)
         else:
-            V(lambda e: e.tensor_scalar(out, in0, s1, s2, op0, op1), r, w)
+            V(lambda e: e.tensor_scalar(out, in0, s1, s2, op0, op1), n, r, w)
 
-    def tt(out, a, b, op, r, w):
-        V(lambda e: e.tensor_tensor(out, a, b, op), r, w)
+    def tt(out, a, b, o, r, w, n=64):
+        V(lambda e: e.tensor_tensor(out, a, b, o), n, r, w)
 
-    def gs_pick(win, wkeys, off, okey):
-        i = used["gs"]
-        used["gs"] = i + 1
-        tt(T.gx[:, 256 * i:256 * i + 256], win.indirect(off), T.mask[:], OP.mult, list(wkeys) + [okey, "mask"], [("gx", i)])
-        return i
+    def copy(out, in_, n, r, w, gather):
+        c = (50 + 1.56 * n * CYC, 65 + 1.56 * n * CYC) if gather else (max(64, n) * CYC, max(64, n) * CYC)
+        op({"v": (lambda e: e.tensor_copy(out, in_), c[0]), "s": (lambda e: e.activation(out, in_, AF.Copy), c[1])}, r, w)
 
-    def gs_scan(i):
-        V(lambda e: e.tensor_tensor_scan(T.gy[:, 256 * i:256 * i + 256], T.nmask[:], T.gx[:, 256 * i:256 * i + 256], 0.0, OP.mult, OP.add),
-          [("gx", i), "nmask"], [("gy", i)])
-        return T.gy[:, 256 * i + 15:256 * i + 256:16], [("gy", i)]
+    def pick(win, wkeys, off, okey):
+        i = used["gx"]
+        used["gx"] = i + 1
+        out = T.gx[:, 256 * i:256 * i + 256]
+        copy(out, win.indirect(off), 256, list(wkeys) + [okey], [("gx", i)], True)
+        return out, [("gx", i)]
 
-    def gs(win, wkeys, off, okey):
-        return gs_scan(gs_pick(win, wkeys, off, okey))
-
-    def gs2(win, wkeys, o1, o2):
-        i = gs_pick(win, wkeys, *o1)
-        j = gs_pick(win, wkeys, *o2)
-        gs_scan(i)
-        gs_scan(j)
-        return T.gy[:, 256 * i + 15:256 * i + 512:16], [("gy", i), ("gy", j)]
+    def scan(rows, buf="gyf"):
+        first = used[buf]
+        col, n = (512, 256) if buf == "gyf" else (768, 128)
+        for row, keys in rows:
+            i = used[buf]
+            used[buf] = i + 1
+            V(lambda e, i=i, row=row: e.tensor_tensor_scan(T[buf][:, 256 * i:256 * i + 256], T.st[:, col:col + 256], row, 0.0, OP.add, OP.max),
+              n, keys + [("st", col)], [(buf, i)])
+        return T[buf][:, 256 * first + 15:256 * first + 256 * len(rows):16], [(buf, first + k) for k in range(len(rows))]
 
     L = T.Lst
     dmas("y", "lm", [(L[:, 0:32], T.m[:])], w=["m_"])
-    dmas("s", "lm", [(L[:, 32:80], T.la[:])], w=["la_"])
-    dmas("y", "lm", [(L[:, 80:128], T.lb[:])], w=["lists"])
+    dmas("s", "lm", [(L[:, 80:128], T.lb[:])], w=["lb_"])
+    dmas("y", "lm", [(L[:, 32:80], T.la[:])], w=["lists"])
     writer["lists"] = ("lm", 48, {})
-    dmas("s", "lx", [(T.X0[:], T.x[:])], w=["X0"])
-    dmas("y", "ll", [(L[:, 128:176], T.ld[:])], w=["ld_"])
+    dmas("s", "ll", [(L[:, 128:176], T.ld[:])], w=["ld_"])
+    dmas("y", "lx", [(T.X0[:], T.x[:])], w=["X0"])
     dmas("y", "lu", [(T.uin[:], T.u[:])], w=["uin"])
     dmas("y", "lw", [(T.wq[:].bitcast(dt.uint8), T.wc[:]), (T.wqs[:], T.ws[:])], w=["wq"])
     dmas("y", "lv", [(T.vin[:], T.v[:])], w=["vin"])
+    ready = {"lists": 2500.0, "ld_": 2600.0, "X0": 5000.0, "uin": 5600.0, "wq": 7200.0, "vin": 7800.0}
 
     pI, kpI, _ = small(32, "smi")
     kI, kkI, _ = small(32, "smi")
-    do("g", lambda e: e.iota(T.vI[:], [[-1, 256]], 512, 1), w=["vI"])
-    do("g", lambda e: e.iota(pI, [[0, 32]], 0, 1), w=[kpI])
-    do("g", lambda e: e.iota(kI, [[16, 32]], 0, 0), w=[kkI])
-    do("g", lambda e: e.iota(T.idw[:], [[1, 512]], -256, 0, allow_small_or_imprecise_dtypes=True), w=["idw"])
-    do("g", lambda e: e.iota(T.jr1[:], [[1, 256]], 1, 0, allow_small_or_imprecise_dtypes=True), w=["jr1"])
+    G(lambda e: e.iota(T.vI[:], [[-1, 256]], 512, 1), 256, w=["vI"])
+    G(lambda e: e.iota(pI, [[0, 32]], 0, 1), 32, w=[kpI])
+    G(lambda e: e.iota(T.idw[:], [[1, 512]], -256, 0, allow_small_or_imprecise_dtypes=True), 512, w=["idw"])
+    G(lambda e: e.iota(kI, [[16, 32]], 0, 0), 32, w=[kkI])
+    G(lambda e: e.iota(T.jr1[:], [[1, 256]], 1, 0, allow_small_or_imprecise_dtypes=True), 256, w=["jr1"])
     eps, keps, _ = small(1)
-    V(lambda e: e.memset(T.Dd[:], 0.0), w=["D0", "D2"])
-    V(lambda e: e.memset(eps, 1e-37), w=[keps])
-    ts(T.vJ[:], T.vI[:], 15, None, OP.bitwise_and, None, ["vI"], ["vJ"])
-    ts(T.mask[:], T.vJ[:], 0, None, OP.is_equal, None, ["vJ"], ["mask"])
-    S(lambda e: e.activation(T.nmask[:], T.mask[:], AF.Identity, bias=1.0, scale=-1.0), ["mask"], ["nmask"])
-    V(lambda e: e.memset(T.ones[:], 1.0), w=["ones"])
-    do("g", lambda e: e.affine_select(T.ez[:], T.ones[:], [[-1, 520]], OP.is_equal, 0.0, 4, 4), ["ones"], ["ez"])
-    V(lambda e: e.memset(T.Cc[:], -1024.0), w=["C0", "C1"])
     for t in range(R):
-        V(lambda e, t=t: e.memset(T.sgw[:, 272 * t:272 * t + 1], -1.0), w=[("pad", t)])
-    p15, kp15, _ = small(32, "smi")
-    p7, kp7, _ = small(32, "smi")
-    pg, kpg, _ = small(32, "smi")
-    idf, kidf, _ = small(32)
-    id16, kid16, _ = small(32, "smu")
+        V(lambda e, t=t: e.memset(T.Dd[:, 512 * t:512 * t + 512], 0.0), 256, w=["D%d" % t])
+        V(lambda e, t=t: e.memset(T.sgw[:, 272 * t:272 * t + 1], -1.0), 1, w=[("pad", t)])
+    V(lambda e: e.memset(eps, 1e-37), 1, w=[keps])
+    ts(T.vJ[:], T.vI[:], 15, None, OP.bitwise_and, None, ["vI"], ["vJ"], 256)
+    ts(T.st[:, 0:256], T.vJ[:], 15, LIFT, OP.is_equal, OP.mult, ["vJ"], [("st", 0)], 256)
+    ts(T.st[:, 256:512], T.vJ[:], 0, -2 * LIFT, OP.is_equal, OP.mult, ["vJ"], [("st", 256)], 256)
+    tt(T.st[:, 512:768], T.st[:, 0:256], T.st[:, 256:512], OP.add, [("st", 0), ("st", 256)], [("st", 512)], 512)
+    ts(T.st[:, 768:1024], T.st[:, 512:768], BASE / LIFT, None, OP.mult, None, [("st", 512)], [("st", 768)], 128)
+    p15, kp15, ap15 = small(32, "smi")
+    p7, kp7, ap7 = small(32, "smi")
+    pg, kpg, apg = small(32, "smi")
+    lift, klift, _ = small(1)
+    last, klast, _ = small(1)
+    ts(p15, pI, 15, None, OP.bitwise_and, None, [kpI], [kp15])
+    ts(lift, T.smi[:, ap15:ap15 + 1], 15, LIFT, OP.is_lt, OP.mult, [kp15], [klift])
+    ts(last, T.smi[:, ap15:ap15 + 1], 15, BASE, OP.is_equal, OP.mult, [kp15], [klast])
+    down = []
+    for p in range(4):
+        down.append(small(1))
+        ts(down[p][0], lift, -4.0, float(1024 + p), OP.mult, OP.add, [klift], [down[p][1]])
+    slot = []
+    for t in range(R):
+        slot.append(small(1))
+        ts(slot[t][0], lift, -1.0, float(BASE + 511 + 256 * t), OP.mult, OP.add, [klift], [slot[t][1]])
+    V(lambda e: e.memset(T.ones[:], 1.0), 260, w=["ones"])
+    G(lambda e: e.affine_select(T.ez[:], T.ones[:], [[-1, 520]], OP.is_equal, 0.0, 4, 4), 520, ["ones"], ["ez"])
+    idl, kidl, _ = small(32)
+    idt, kidt, _ = small(32)
     fr8, kfr8, _ = small(32)
-    gfr, kgfr, _ = small(32)
+    gfr, kgfr, _ = small(1)
     U16, kU16, u0 = small(16, "smu")
     ts(p7, pI, 7, None, OP.bitwise_and, None, [kpI], [kp7])
-    ts(p15, pI, 15, None, OP.bitwise_and, None, [kpI], [kp15])
     ts(pg, pI, 4, None, OP.arith_shift_right, None, [kpI], [kpg])
-    tt(idf, p15, kI, OP.add, [kp15, kkI], [kidf])
     ts(fr8, p7, 0.125, None, OP.mult, None, [kp7], [kfr8])
-    ts(gfr, pg, 0.125, None, OP.mult, None, [kpg], [kgfr])
-    V(lambda e: e.tensor_copy(id16, idf), [kidf], [kid16])
-    V(lambda e: e.tensor_copy(T.smu[:, u0:u0 + 8], T.smi[:, 32:40]), [kkI], [(kU16, 0)])
-    ts(T.smu[:, u0 + 8:u0 + 16], T.smi[:, kp7[1]:kp7[1] + 8], 16, None, OP.mult, None, [kp7], [(kU16, 1)])
+    ts(gfr, T.smi[:, apg:apg + 1], 0.125, None, OP.mult, None, [kpg], [kgfr])
+    tt(idt, p15, kI, OP.add, [kp15, kkI], [kidt])
+    ts(idl, idt, float(BASE), None, OP.add, None, [kidt], [kidl])
+    V(lambda e: e.tensor_copy(T.smu[:, u0:u0 + 8], T.smi[:, 32:40]), 8, [kkI], [(kU16, 0)])
+    ts(T.smu[:, u0 + 8:u0 + 16], T.smi[:, ap7:ap7 + 8], 16, None, OP.mult, None, [kp7], [(kU16, 1)])
 
     L16, kL16, l0 = small(128, "smu")
     D16, kD16, d0 = small(48, "smu")
     Lf, kLf, lf = small(128)
-    V(lambda e: e.tensor_copy(L16, L[:, 0:128]), ["lists"], [kL16])
+    mf, kmf, amf = small(32)
+    V(lambda e: e.tensor_copy(L16, L[:, 0:128]), 128, ["lists"], [kL16])
 
     def la16(t):
         return T.smu[:, l0 + 32 + 16 * t:l0 + 48 + 16 * t], kL16
@@ -208,79 +282,91 @@ def rank_program(g, core, T, topo):
     def lb16(t):
         return T.smu[:, l0 + 80 + 16 * t:l0 + 96 + 16 * t], kL16
 
-    idh = [(T.smu[:, kid16[1] + 16 * h:kid16[1] + 16 * h + 16], kid16) for h in range(2)]
-    V(lambda e: e.tensor_copy(T.m0r[:], T.idw[:].indirect(T.smu[:, l0:l0 + 32])), ["idw", kL16], ["m0r"])
+    def inverse(t):
+        V(lambda e: e.tensor_copy(T.Dd[:, 512 * t:512 * t + 512].indirect(T.smu[:, d0 + 16 * t:d0 + 16 * t + 16]), T.jr1[:]), 1000, ["jr1", kD16], ["D%d" % t])
 
-    zl = [small(128, "smu")[2] for _ in range(R + 1)]
-
-    def lists(t, half, src, keys, add):
+    copy(T.m0r[:], T.idw[:].indirect(T.smu[:, l0:l0 + 32]), 512, ["idw", kL16], ["m0r"], True)
+    rows0 = [pick(T.m0r[:], ["m0r"], *la16(0)), pick(T.m0r[:], ["m0r"], *lb16(0))]
+    V(lambda e: e.tensor_copy(D16, L[:, 128:176]), 48, ["ld_"], [kD16])
+    zl0 = small(128, "smu")[2]
+    zl = [None] + [small(32, "smu")[2] for _ in range(R)]
+    for half in range(2):
+        y, ky = scan([rows0[half]])
         for p in range(4):
-            a = zl[t] + 64 * half + 16 * p
-            ts(T.smu[:, a:a + 16], src, 4.0, float(4 * add + p), OP.mult, OP.add, keys, [("zl", t, half, p)])
-
-    def zoff(t, half, p, k):
-        a = zl[t] + 64 * half + 16 * p + 8 * k
-        return T.smu[:, a:a + 8]
-
-    for half, fn in ((0, la16), (1, lb16)):
-        y, ky = gs(T.m0r[:], ["m0r"], *fn(0))
-        lists(0, half, y, ky, 256)
+            a = zl0 + 64 * half + 16 * p
+            ts(T.smu[:, a:a + 16], y, 4.0, down[p][0], OP.mult, OP.add, ky + [down[p][1]], [("zl", 0, half, p)])
     m4 = []
     for p in range(4):
-        o, ko, _ = small(32, "smu")
-        ts(o, L[:, 0:32], 4, p, OP.mult, OP.add, ["lists"], [ko])
-        m4.append((o, ko))
+        m4.append(small(32, "smu"))
+        ts(m4[p][0], L[:, 0:32], 4, p, OP.mult, OP.add, ["lists"], [m4[p][1]])
+    ts(Lf, L[:, 0:128], float(BASE), None, OP.add, None, ["lists"], [kLf], 128)
+    ab2, kab2, aa = small(32)
+    V(lambda e: e.tensor_copy(T.smf[:, aa:aa + 16], T.smf[:, lf + 64:lf + 80]), 16, [kLf], [(kab2, 0)])
+    V(lambda e: e.tensor_copy(T.smf[:, aa + 16:aa + 32], T.smf[:, lf + 112:lf + 128]), 16, [kLf], [(kab2, 1)])
+    kab = [(kab2, 0), (kab2, 1)]
 
-    def fkeys(t):
-        return [("Fx", p) for p in range(4)] + [("Fn", s, h, b) for s in range(t) for h in range(2) for b in range(4)]
+    def zoff(t, half, p, k):
+        a = zl[t] + 16 * half + 8 * k if t else zl0 + 64 * half + 16 * p + 8 * k
+        return T.smu[:, a:a + 8], ("zl", t, half, p if t == 0 else 0)
 
-    def operands(t):
-        win, wk = (T.X0[:], ["X0"]) if t == 0 else (T.F[:, 0:2048 + 1024 * t], fkeys(t))
-        for h in range(2):
-            for p in range(4):
-                S(lambda e, h=h, p=p: e.activation(T.Ag[:, 256 * p + 128 * h:256 * p + 128 * h + 128], win.indirect(zoff(t, 0, p, h)), AF.Copy),
-                  wk + [("zl", t, 0, p)], [("A", h, p)])
-        for h in range(2):
-            for p in range(4):
-                tt(T.Z[:, 512 * h + p:512 * h + 512:4], win.indirect(zoff(t, 1, p, h)), T.Ag[:, 256 * p + 128 * h:256 * p + 128 * h + 128],
-                   OP.add, wk + [("zl", t, 1, p), ("A", h, p)], [("Z", h, p)])
-            qz, qs = T["qz%d" % t], T["qzs%d" % t]
-            lo, hi = 128 * h, 128 * h + 128
-            V(lambda e: e.quantize_mx(qz[:, lo:hi], qs[:, lo:hi], T.Z[:, 4 * lo:4 * hi]), [("Z", h, p) for p in range(4)], [("qz", t, h)])
+    def window(t, p):
+        if t == 0:
+            return T.X0[:], ["X0"]
+        return T.F[:, SL * p:SL * p + 512 + 256 * t], [("Fx", p)] + [("Fn", s, h, p) for s in range(t) for h in range(2)]
+
+    def send(t, h):
+        qz, qs = T["qz%d" % t], T["qzs%d" % t]
+        lo, hi = 128 * h, 128 * h + 128
+
+        def call(q):
             dst = T.cores[rank ^ STEP[t]]
             rid, pid = topo.addr(dst)[:2]
             eng = topo.engines(core, dst)
-            arr = T.sem["arr%d%d" % (t, h)]
+            name = "arr%d%d" % (t, h)
             gate("g", [("qz", t, h)], [])
             m0, m1 = sum(1 << e for e in eng[0::2]), sum(1 << e for e in eng[1::2])
-            g.remote_dma(T["lz%d" % t][:, lo:hi].bitcast(dt.uint8), qz[:, lo:hi].bitcast(dt.uint8), arr, T.sem.sent, pid, rid, m0)
-            g.remote_dma(T["lzs%d" % t][:, lo:hi], qs[:, lo:hi], arr, T.sem.sent, pid, rid, m1)
+            g.remote_dma(T["lz%d" % t][:, lo:hi].bitcast(dt.uint8), qz[:, lo:hi].bitcast(dt.uint8), T.sem[name], T.sem.sent, pid, rid, m0)
+            g.remote_dma(T["lzs%d" % t][:, lo:hi], qs[:, lo:hi], T.sem[name], T.sem.sent, pid, rid, m1)
             count["sent"] = count.get("sent", 0) + len(eng)
-            count["arr%d%d" % (t, h)] = len(eng)
-            writer[("lz", t, h)] = ("arr%d%d" % (t, h), len(eng), {})
+            count[name] = len(eng)
+            writer[("lz", t, h)] = (name, len(eng), {})
+        op({"g": (call, SEND + (FIRST if t + h == 0 else 0.0))}, [("qz", t, h)], [("lz", t, h)], FLY, "send")
 
-    def bank(k, n=128):
-        return T.ps[:, 512 * k:512 * k + n]
+    def operands(t):
+        for h in range(2):
+            for p in range(4):
+                (win, wk), (off, ko) = window(t, p), zoff(t, 0, p, h)
+                a = 1024 * t + 256 * p + 128 * h
+                copy(T.Ag[:, a:a + 128], win.indirect(off), 128, wk + [ko], [("A", t, h, p)], True)
+        for h in range(2):
+            lo, hi, z = 128 * h, 128 * h + 128, 1024 * t + 512 * h
+            for p in range(4):
+                (win, wk), (off, ko) = window(t, p), zoff(t, 1, p, h)
+                a = 1024 * t + 256 * p + 128 * h
+                tt(T.Z[:, z + p:z + 512:4], win.indirect(off), T.Ag[:, a:a + 128], OP.add, wk + [ko, ("A", t, h, p)], [("Z", t, h, p)], 260)
+            V(lambda e, lo=lo, hi=hi, z=z: e.quantize_mx(T["qz%d" % t][:, lo:hi], T["qzs%d" % t][:, lo:hi], T.Z[:, z:z + 512]), 150,
+              [("Z", t, h, p) for p in range(4)], [("qz", t, h)])
+            send(t, h)
 
-    def mm(k, lq, ls, rq, rs, r, n=128):
-        do("t", lambda e: e.matmul_mx(bank(k, n), lq, ls, rq, rs, True, True), r, [("bk", k)])
+    def bank(k):
+        return T.ps[:, 512 * k:512 * k + 128]
 
-    s1, s2 = [], []
-    for t in range(R):
-        s1.append([small(1) for _ in range(2)])
-        s2.append([small(1) for _ in range(2)])
+    def mm(k, lq, ls, rq, rs, r):
+        op({"t": (lambda e: e.matmul_mx(bank(k), lq, ls, rq, rs, True, True), 170.0)}, r, [("bk", k)])
+
+    s1 = [[small(1) for _ in range(2)] for _ in range(R)]
+    s2 = [[small(1) for _ in range(2)] for _ in range(R)]
+    own = [[small(1) for _ in range(2)] for _ in range(R)]
 
     def layer(t, h):
-        lo, hi = 128 * h, 128 * h + 128
-        for b in (0, 1, 2, 3):
+        lo, hi, z = 128 * h, 128 * h + 128, 1024 * t + 512 * h
+        for b in range(4):
             mm(b, T.wq[:, 128 * b:128 * b + 128], T.wqs[:, 128 * b:128 * b + 128], T["lz%d" % t][:, lo:hi], T["lzs%d" % t][:, lo:hi], ["wq", ("lz", t, h)])
-        for b in (0, 1, 2, 3):
-            out = T.Hb[:, 4 * lo + b:4 * hi:4]
-            if b % 2:
-                S(lambda e: e.activation(out, bank(b), AF.Relu, scale=0.015625), [("bk", b)], [("H", h, b)])
-            else:
-                ts(out, bank(b), 0.0, 0.015625, OP.max, OP.mult, [("bk", b)], [("H", h, b)])
-        V(lambda e: e.quantize_mx(T["qh%d" % t][:, lo:hi], T["qhs%d" % t][:, lo:hi], T.Hb[:, 4 * lo:4 * hi]), [("H", h, b) for b in range(4)], [("qh", t, h)])
+        for b in range(4):
+            out = T.Hb[:, z + b:z + 512:4]
+            op({"v": (lambda e, b=b, out=out: e.tensor_scalar(out, bank(b), 0.0, 0.015625, OP.max, OP.mult), 128 * CYC),
+                "s": (lambda e, b=b, out=out: e.activation(out, bank(b), AF.Relu, scale=0.015625), 128 * CYC)}, [("bk", b)], [("H", t, h, b)])
+        V(lambda e: e.quantize_mx(T["qh%d" % t][:, lo:hi], T["qhs%d" % t][:, lo:hi], T.Hb[:, z:z + 512]), 150, [("H", t, h, b) for b in range(4)], [("qh", t, h)])
 
     def scores(t, h):
         lo, hi = 128 * h, 128 * h + 128
@@ -288,220 +374,164 @@ def rank_program(g, core, T, topo):
         bs, bd = ((4, 5), (6, 7, 4, 5)) if h == 0 else ((6, 7), (0, 1, 2, 3))
         for i in range(2):
             mm(bs[i], T.up[:, 128 * i:128 * i + 128], T.ups[:, 128 * i:128 * i + 128], q, s, ["up", "ups", ("qh", t, h)])
-        out1 = T.sgw[:, 272 * t + 1 + lo:272 * t + 1 + hi]
-        out2 = T.sg2[:, 256 * t + lo:256 * t + hi]
-        S(lambda e: e.activation(out1, bank(bs[0]), AF.Sign, bias=eps, accum_out=s1[t][h][0]), [("bk", bs[0]), keps], [("sg", t, h), s1[t][h][1]])
-        S(lambda e: e.activation(out2, bank(bs[1]), AF.Sign, bias=eps, accum_out=s2[t][h][0]), [("bk", bs[1]), keps], [("sg2", t, h), s2[t][h][1]])
+            out = T.sgw[:, 272 * t + 1 + lo:272 * t + 1 + hi] if i == 0 else T.sg2[:, 256 * t + lo:256 * t + hi]
+            sm = (s1, s2)[i][t][h]
+            op({"s": (lambda e, i=i, out=out, sm=sm: e.activation(out, bank(bs[i]), AF.Sign, bias=eps, accum_out=sm[0]), 150.0)},
+               [("bk", bs[i]), keps], [("sg%d" % i, t, h), sm[1]])
         for b in range(4):
             mm(bd[b], T.eq[:, 128 * b:128 * b + 128], T.eqs[:, 128 * b:128 * b + 128], q, s, [("eq", b), ("qh", t, h)])
-            base = 2048 + 1024 * t + 4 * lo
-            S(lambda e: e.activation(T.F[:, base + b:base + 512:4], bank(bd[b]), AF.Copy), [("bk", bd[b])], [("Fn", t, h, b)])
+            a = SL * b + 512 + 256 * t + lo
+            copy(T.F[:, a:a + 128], bank(bd[b]), 128, [("bk", bd[b])], [("Fn", t, h, b)], False)
+        add, kadd = (gfr, kgfr) if h == 0 else own[t][0][:2]
+        ts(own[t][h][0], s1[t][h][0], add, None, OP.add, None, [s1[t][h][1], kadd], [own[t][h][1]])
 
-    def value(t, h):
-        a = 256 * t + 128 * h
-        ts(T.vs[:, a:a + 128], T.sgw[:, 272 * t + 1 + 128 * h:272 * t + 129 + 128 * h], 1024.0, None, OP.mult, None, [("sg", t, h)], [("vs", t, h)])
-        tt(T.val[:, a:a + 128], T.vs[:, a:a + 128], T.jr1[:, 128 * h:128 * h + 128], OP.min, [("vs", t, h), "jr1"], [("val", t, h)])
-
-    def scatter(win, src, t, r, w):
-        V(lambda e: e.tensor_copy(win.indirect(T.smu[:, d0 + 16 * t:d0 + 16 * t + 16]), src), r + [kD16], [w])
-
-    def inverse(t, win, wk, o1, o2):
-        y, ky = gs2(win, wk, o1, o2)
-        n, kn, _ = small(32)
+    def where(t, rows):
+        y, ky = scan(rows)
+        n, kn, na = small(32)
+        ts(n, y, slot[t][0], None, OP.add, None, ky + [slot[t][1]], [kn])
         o, ko, oa = small(32, "smu")
-        ts(n, y, float(511 + 256 * t), None, OP.add, None, ky, [kn])
-        ts(o, n, float(-511 - 256 * t), None, OP.add, None, [kn], [ko])
-        return n, kn, oa, ko
+        ts(o, n, float(-BASE - 511 - 256 * t), None, OP.add, None, [kn], [ko])
+        return {"n": n, "kn": kn, "na": na, "oa": oa, "ko": ko}
 
-    own = [small(1) for _ in range(R)]
+    def ident(t):
+        return [(T.Dd[:, 512 * t + 256 * k:512 * t + 256 * k + 256], ["D%d" % t]) for k in range(2)]
 
-    def own_half(t):
-        ts(own[t][0], s1[t][0][0], T.smf[:, kgfr[1]:kgfr[1] + 1], None, OP.add, None, [s1[t][0][1], kgfr], [own[t][1]])
+    def find(t, l):
+        return [pick(T.Dd[:, 512 * t:512 * t + 512], ["D%d" % t], *l2) for l2 in (la16(l), lb16(l))]
 
-    keep = [small(1) for _ in range(R)]
+    def signs(t, w):
+        win, wk = T.sgw[:, 272 * t:272 * t + 257], [("pad", t), ("sg0", t, 0), ("sg0", t, 1), klast, w["ko"]]
+        rows = []
+        for k in range(2):
+            i = used["gx"]
+            used["gx"] = i + 1
+            out, in_ = T.gx[:, 256 * i:256 * i + 256], win.indirect(T.smu[:, w["oa"] + 16 * k:w["oa"] + 16 * k + 16])
+            op({"v": (lambda e, out=out, in_=in_: e.tensor_scalar(out, in_, 2048.0, last, OP.mult, OP.add), 450 * CYC),
+                "s": (lambda e, out=out, in_=in_: e.activation(out, in_, AF.Identity, bias=last, scale=2048.0), 465 * CYC)}, wk, [("gx", i)])
+            rows.append((out, [("gx", i)]))
+        return rows
 
-    def keep_steps(t):
+    lim = [small(1) for _ in range(R)]
+    nlim, knlim, _ = small(1)
+
+    def limit(t):
         kb, kkb, _ = small(32)
         kt, kkt, ka = small(32)
         c8, kc8, _ = small(8)
-        cn, kcn, _ = small(1)
-        return [
-            lambda: ts(kb, fr8, s2[t][0][0], s2[t][1][0], OP.add, OP.add, [kfr8, s2[t][0][1], s2[t][1][1]], [kkb]),
-            lambda: V(lambda e: e.transpose(kt, kb), [kkb], [kkt]),
-            lambda: ts(c8, T.smf[:, ka:ka + 8], own[t][0], s1[t][1][0], OP.subtract, OP.is_lt, [kkt, own[t][1], s1[t][1][1]], [kc8]),
-            lambda: V(lambda e: e.tensor_reduce(cn, c8, AxisListType.X, OP.add), [kc8], [kcn]),
-            lambda: ts(keep[t][0], cn, 2.0, None, OP.is_ge, None, [kcn], [keep[t][1]]),
-        ]
+        ts(kb, fr8, s2[t][0][0], s2[t][1][0], OP.add, OP.add, [kfr8, s2[t][0][1], s2[t][1][1]], [kkb])
+        V(lambda e: e.transpose(kt, kb), 32, [kkb], [kkt])
+        ts(c8, T.smf[:, ka:ka + 8], own[t][1][0], float(BASE), OP.is_lt, OP.mult, [kkt, own[t][1][1]], [kc8])
+        V(lambda e: e.tensor_reduce(lim[t][0], c8, AxisListType.X, OP.add), 8, [kc8], [lim[t][1]])
+        if t == 2:
+            V(lambda e: e.tensor_reduce(nlim, c8, AxisListType.X, OP.add, negate=True), 8, [kc8], [knlim])
 
-    def bymax(a, ka, b, kb):
-        o, ko, _ = small(16)
-        tt(o, a, b, OP.max, ka + kb, [ko])
-        return o, [ko]
+    def cut(t, w, rows, first, floor, width=32):
+        outs = []
+        for k in range(32 // width):
+            y, ky = scan(rows if width == 32 else [rows[k]], "gyb")
+            sl = lambda v: T.smf[:, v[2] + width * k:v[2] + width * k + width]
+            c, kc, _ = small(width)
+            d, kd, _ = small(width)
+            o, ko, oa = small(width)
+            tt(c, y, T.smf[:, w["na"] + width * k:w["na"] + width * k + width], OP.min, ky + [w["kn"]], [kc])
+            if first:
+                f, kf, _ = small(width)
+                tt(f, c, sl(first), OP.max, [kc, first[1]], [kf])
+                c, kc = f, kf
+            ts(d, c, lim[t][0], None, OP.min, None, [kc, lim[t][1]], [kd])
+            fl = floor[k] if isinstance(floor, list) else floor
+            tt(o, d, fl[0], OP.max, [kd] + fl[1], [ko])
+            outs.append((o, ko, oa))
+        return outs
 
+    def settle(t, w, rows, first, floor):
+        outs = cut(t, w, rows, first, floor, 16)
+        for half in range(2):
+            a = zl[t + 1] + 16 * half
+            ts(T.smu[:, a:a + 16], outs[half][0], float(-BASE), None, OP.add, None, [outs[half][1]], [("zl", t + 1, half, 0)])
+        return outs
+
+    def halves(a, keys):
+        return [(T.smf[:, a:a + 16], keys), (T.smf[:, a + 16:a + 32], keys)]
+
+    inverse(0)
     operands(0)
-    V(lambda e: e.tensor_copy(D16, L[:, 128:176]), ["ld_"], [kD16])
-    V(lambda e: e.quantize_mx(T.uq[:], T.uqs[:], T.uin[:]), ["uin"], ["uq"])
-    V(lambda e: e.tensor_copy(T.up[:].bitcast(dt.uint32), T.uq[:].bitcast(dt.uint32).indirect(U16)), ["uq", (kU16, 0), (kU16, 1)], ["up"])
+    w01 = where(0, find(0, 1))
     for p in range(4):
-        S(lambda e, p=p: e.activation(T.F[:, p:2048:4], T.X0[:].indirect(m4[p][0]), AF.Copy), ["X0", m4[p][1]], [("Fx", p)])
-    S(lambda e: e.activation(T.ups[:], T.uqs[:].indirect(U16), AF.Copy), ["uq", (kU16, 0), (kU16, 1)], ["ups"])
-    scatter(T.Dd[:, 0:512], T.jr1[:], 0, ["jr1", "D0"], "D0")
+        copy(T.F[:, SL * p:SL * p + 512], T.X0[:].indirect(m4[p][0]), 512, ["X0", m4[p][1]], [("Fx", p)], True)
+    V(lambda e: e.quantize_mx(T.uq[:], T.uqs[:], T.uin[:]), 150, ["uin"], ["uq"])
+    V(lambda e: e.tensor_copy(T.up[:].bitcast(dt.uint32), T.uq[:].bitcast(dt.uint32).indirect(U16)), 450, ["uq", (kU16, 0), (kU16, 1)], ["up"])
+    copy(T.ups[:], T.uqs[:].indirect(U16), 256, ["uq", (kU16, 0), (kU16, 1)], ["ups"], True)
     for b in range(4):
-        V(lambda e, b=b: e.quantize_mx(T.eq[:, 128 * b:128 * b + 128], T.eqs[:, 128 * b:128 * b + 128], T.ez[:, 4 - b:516 - b]), ["ez"], [("eq", b)])
+        V(lambda e, b=b: e.quantize_mx(T.eq[:, 128 * b:128 * b + 128], T.eqs[:, 128 * b:128 * b + 128], T.ez[:, 4 - b:516 - b]), 150, ["ez"], [("eq", b)])
     layer(0, 0)
-    np0, knp0, j0, kj0 = inverse(0, T.Dd[:, 0:512], ["D0"], la16(1), lb16(1))
     scores(0, 0)
-    V(lambda e: e.tensor_copy(Lf, L[:, 0:128]), ["lists"], [kLf])
-    own_half(0)
     layer(0, 1)
     scores(0, 1)
-
-    def finish_j(t, np_, knp, ja, kj, base, kbase, after_keep):
-        npk, knpk, na = small(32)
-        win, wk = T.sgw[:, 272 * t:272 * t + 257], [("pad", t), ("sg", t, 0), ("sg", t, 1)]
-        st = keep_steps(t)
-        i = gs_pick(win, wk, T.smu[:, ja:ja + 16], kj)
-        st[0]()
-        st[1]()
-        y, ky = gs_scan(i)
-        for f in st[2:]:
-            f()
-        ts(npk, np_, keep[t][0], None, OP.mult, None, [knp, keep[t][1]], [knpk])
-        after_keep()
-        offs = []
-        for half in range(2):
-            if half:
-                y, ky = gs(win, wk, T.smu[:, ja + 16:ja + 32], kj)
-            tmp, ktmp, _ = small(16)
-            tt(tmp, y, T.smf[:, na + 16 * half:na + 16 * half + 16], OP.mult, ky + [knpk], [ktmp])
-            o, ko = bymax(tmp, [ktmp], base[half], kbase)
-            lists(t + 1, half, o, ko, 0)
-            offs.append((o, ko))
-        return offs
-
-    finish_j(0, np0, knp0, j0, kj0, [T.smf[:, lf + 48:lf + 64], T.smf[:, lf + 96:lf + 112]], [kLf], lambda: None)
-
-    def kplus(t):
-        k, kk, _ = small(1)
-        ts(k, keep[t][0], float(2511 + 256 * t), -2000.0, OP.mult, OP.add, [keep[t][1]], [kk])
-        return k, kk
+    limit(0)
+    settle(0, w01, signs(0, w01), None, [(T.smf[:, lf + 48:lf + 64], [kLf]), (T.smf[:, lf + 96:lf + 112], [kLf])])
 
     operands(1)
-    kp0, kkp0 = kplus(0)
-    value(0, 0)
-    value(0, 1)
-    scatter(T.Cc[:, 0:512], T.val[:, 0:256], 0, [("val", 0, 0), ("val", 0, 1), "C0"], "C0")
-    y, ky = gs2(T.Cc[:, 0:512], ["C0"], la16(2), lb16(2))
-    ab2, kab2, aa = small(32)
-    V(lambda e: e.tensor_copy(T.smf[:, aa:aa + 16], T.smf[:, lf + 64:lf + 80]), [kLf], [(kab2, 0)])
-    V(lambda e: e.tensor_copy(T.smf[:, aa + 16:aa + 32], T.smf[:, lf + 112:lf + 128]), [kLf], [(kab2, 1)])
-    c0, kc0, _ = small(32)
-    p1, kp1, _ = small(32)
-    ts(c0, y, kp0, None, OP.add, None, ky + [kkp0], [kc0])
-    tt(p1, c0, ab2, OP.max, [kc0, (kab2, 0), (kab2, 1)], [kp1])
+    inverse(1)
+    w12, w02 = where(1, find(1, 2)), where(0, find(0, 2))
     layer(1, 0)
     scores(1, 0)
-    y, ky = gs2(T.Cc[:, 0:512], ["C0"], idh[0], idh[1])
-    c1, kc1, _ = small(32)
-    g1, kg1, _ = small(32)
-    ts(c1, y, kp0, None, OP.add, None, ky + [kkp0], [kc1])
-    tt(g1, c1, idf, OP.max, [kc1, kidf], [kg1])
-    value(1, 0)
-    own_half(1)
+    p1 = cut(0, w02, signs(0, w02), None, (ab2, kab))[0]
     layer(1, 1)
     scores(1, 1)
-    st = keep_steps(1)
-    value(1, 1)
-    scatter(T.Cc[:, 512:1024], T.val[:, 256:512], 1, [("val", 1, 0), ("val", 1, 1), "C1"], "C1")
-    i = gs_pick(T.Cc[:, 512:1024], ["C1"], *la16(2))
-    st[0]()
-    st[1]()
-    y, ky = gs_scan(i)
-    for fn in st[2:]:
-        fn()
-    kp1_, kkp1 = kplus(1)
-    pk, kpk, _ = small(32)
-    base, kbase, ba = small(32)
-    ts(pk, p1, keep[1][0], None, OP.mult, None, [kp1, keep[1][1]], [kpk])
-    tt(base, pk, ab2, OP.max, [kpk, (kab2, 0), (kab2, 1)], [kbase])
-    for half in range(2):
-        if half:
-            y, ky = gs(T.Cc[:, 512:1024], ["C1"], *lb16(2))
-        tmp, ktmp, _ = small(16)
-        ts(tmp, y, kp1_, None, OP.add, None, ky + [kkp1], [ktmp])
-        o, ko = bymax(tmp, [ktmp], T.smf[:, ba + 16 * half:ba + 16 * half + 16], [kbase])
-        lists(2, half, o, ko, 0)
+    limit(1)
+    settle(1, w12, signs(1, w12), p1, halves(aa, kab))
 
     operands(2)
-    scatter(T.Dd[:, 512:1024], T.jr1[:], 2, ["jr1", "D2"], "D2")
-    np2, knp2, j2, kj2 = inverse(2, T.Dd[:, 512:1024], ["D2"], idh[0], idh[1])
+    inverse(2)
+    w0, w1, w2 = [where(t, ident(t)) for t in range(R)]
+    g1 = cut(0, w0, signs(0, w0), None, (idl, [kidl]))[0]
+    g2 = cut(1, w1, signs(1, w1), g1, (idl, [kidl]))[0]
+    gm, kgm, _ = small(32)
+    ts(gm, g1[0], float(-3 * BASE), None, OP.add, None, [g1[1]], [kgm])
+    V(lambda e: e.quantize_mx(T.vq[:], T.vqs[:], T.vin[:]), 150, ["vin"], ["vq"])
     layer(2, 0)
     scores(2, 0)
-    y, ky = gs2(T.Cc[:, 512:1024], ["C1"], idh[0], idh[1])
-    c2, kc2, _ = small(32)
-    g2, kg2, _ = small(32)
-    ts(c2, y, kp1_, None, OP.add, None, ky + [kkp1], [kc2])
-    tt(g2, c2, g1, OP.max, [kc2, kg1], [kg2])
-    g3, kg3, _ = small(32)
-    g4, kg4, _ = small(32)
-    ts(g3, g2, keep[1][0], None, OP.mult, None, [kg2, keep[1][1]], [kg3])
-    tt(g4, g3, idf, OP.max, [kg3, kidf], [kg4])
-    df, kdf, _ = small(32)
-    tt(df, g4, g1, OP.subtract, [kg4, kg1], [kdf])
-    V(lambda e: e.quantize_mx(T.vq[:], T.vqs[:], T.vin[:]), ["vin"], ["vq"])
-    own_half(2)
     layer(2, 1)
     scores(2, 1)
-    d1, kd1, _ = small(32)
+    limit(2)
     fb, kfb, fa = small(32)
+    ts(fb, gm, nlim, float(3 * BASE), OP.min, OP.add, [kgm, knlim], [kfb])
+    offs = settle(2, w2, signs(2, w2), g2, halves(fa, [kfb]))
 
-    def final_base():
-        ts(d1, df, keep[2][0], None, OP.mult, None, [kdf, keep[2][1]], [kd1])
-        tt(fb, d1, g1, OP.add, [kd1, kg1], [kfb])
-
-    offs = finish_j(2, np2, knp2, j2, kj2, [T.smf[:, fa:fa + 16], T.smf[:, fa + 16:fa + 32]], [kfb], final_base)
-
-    win, wk = T.F[:], fkeys(3)
-
-    def gather_t(c, p, on_scalar):
-        out, off = T.Tt[:, 512 * c + p:512 * c + 512:4], zoff(3, c // 2, p, c % 2)
-        r, w = wk + [("zl", 3, c // 2, p)], [("T", c, p)]
-        if on_scalar:
-            S(lambda e: e.activation(out, win.indirect(off), AF.Copy), r, w)
-        else:
-            V(lambda e: e.tensor_copy(out, win.indirect(off)), r, w)
-
-    def om_out():
-        pl, kpl, pa = small(32)
-        ot, kot, oa = small(32)
-        for half in range(2):
-            o, ko = offs[half]
-            a, ka, _ = small(16)
-            b, kb, _ = small(16)
-            ts(a, o, 512.0, None, OP.is_ge, None, ko, [ka])
-            tt(b, a, o, OP.mult, ko + [ka], [kb])
-            tt(T.smf[:, pa + 16 * half:pa + 16 * half + 16], b, T.smf[:, lf + 16 * half:lf + 16 * half + 16], OP.max, [kb, kLf], [(kpl, half)])
-        V(lambda e: e.transpose(ot, pl), [(kpl, 0), (kpl, 1)], [kot])
-        dmas("y", "som", [(T.om[q:q + 1, :], T.smf[32 * (q // 2):32 * (q // 2) + 32, oa + 16 * (q % 2):oa + 16 * (q % 2) + 16]) for q in range(8)], [kot], ["om"])
-
-    def evac_y(c):
-        k = 4 + c
-        S(lambda e: e.activation(T.yo[:, 128 * c:128 * c + 128], bank(k), AF.Copy), [("bk", k)], [("yo", c)])
-        dmas("y", "sy%d" % c, [(T.y[:, 128 * c:128 * c + 128], T.yo[:, 128 * c:128 * c + 128])], [("yo", c)], [("y", c)])
+    def store(q, sem, pairs, r, w):
+        op({q: (lambda q: dmas(q, sem, pairs, r, w), 60.0 * len(pairs))}, r, w, 2500.0, "dma")
 
     for c in range(4):
-        for p in range(4):
-            gather_t(c, p, p < (3 if c == 0 else 2))
         lo, hi = 128 * c, 128 * c + 128
-        V(lambda e: e.quantize_mx(T.oq[:, lo:hi], T.oqs[:, lo:hi], T.Tt[:, 4 * lo:4 * hi]), [("T", c, p) for p in range(4)], [("oq", c)])
+        for p in range(4):
+            (win, wk), (off, ko) = window(3, p), zoff(3, c // 2, p, c % 2)
+            copy(T.Tt[:, 512 * c + p:512 * c + 512:4], win.indirect(off), 128, wk + [ko], [("T", c, p)], True)
+        V(lambda e, lo=lo, hi=hi: e.quantize_mx(T.oq[:, lo:hi], T.oqs[:, lo:hi], T.Tt[:, 4 * lo:4 * hi]), 150, [("T", c, p) for p in range(4)], [("oq", c)])
         mm(4 + c, T.vq[:], T.vqs[:], T.oq[:, lo:hi], T.oqs[:, lo:hi], ["vq", ("oq", c)])
-        if c:
-            evac_y(c - 1)
-        dmas("y", "so%d" % c, [(T.oc[:, 4 * lo:4 * hi], T.oq[:, lo:hi].bitcast(dt.uint8))], [("oq", c)], [("oc", c)])
-        if c == 1:
-            om_out()
-    evac_y(3)
-    dmas("s", "sos", [(T.osc[4 * k:4 * k + 4, :], T.oqs[32 * k:32 * k + 4, :]) for k in range(4)], [("oq", c) for c in range(4)], ["osc"])
+        copy(T.yo[:, lo:hi], bank(4 + c), 128, [("bk", 4 + c)], [("yo", c)], False)
+        store("y", "so%d" % c, [(T.oc[:, 4 * lo:4 * hi], T.oq[:, lo:hi].bitcast(dt.uint8))], [("oq", c)], [("oc", c)])
+        store("y", "sy%d" % c, [(T.y[:, lo:hi], T.yo[:, lo:hi])], [("yo", c)], [("y", c)])
+    store("s", "sos", [(T.osc[4 * k:4 * k + 4, :], T.oqs[32 * k:32 * k + 4, :]) for k in range(4)], [("oq", c) for c in range(4)], ["osc"])
+    pl, kpl, pa = small(32)
+    ot, kot, oa = small(32)
+    V(lambda e: e.tensor_copy(mf, L[:, 0:32]), 32, ["lists"], [kmf])
+    for half in range(2):
+        o, ko, _ = offs[half]
+        a, ka, _ = small(16)
+        b, kb, _ = small(16)
+        c, kc, _ = small(16)
+        ts(b, o, float(-BASE), None, OP.add, None, [ko], [kb])
+        ts(a, b, 512.0, None, OP.is_ge, None, [kb], [ka])
+        tt(c, a, b, OP.mult, [kb, ka], [kc])
+        tt(T.smf[:, pa + 16 * half:pa + 16 * half + 16], c, T.smf[:, amf + 16 * half:amf + 16 * half + 16], OP.max, [kc, kmf], [(kpl, half)])
+    V(lambda e: e.transpose(ot, pl), 32, [(kpl, 0), (kpl, 1)], [kot])
+    store("y", "som", [(T.om[q:q + 1, :], T.smf[32 * (q // 2):32 * (q // 2) + 32, oa + 16 * (q % 2):oa + 16 * (q % 2) + 16]) for q in range(8)], [kot], ["om"])
+
+    if "order" not in PLAN:
+        PLAN["order"] = make_plan(ops, ready)
+    for i, q in PLAN["order"]:
+        emit(ops[i], q)
     for s in SEMAPHORES:
         if known["g"].get(s, 0) < count.get(s, 0):
             g.wait_ge(T.sem[s], count[s])

@@ -9,7 +9,8 @@ STEP = [1, 2, 4]
 LIFT = 2048
 BASE = 8192
 SL = 1280
-CYC, WAKE, NEAR, SEND, FLY, FIRST = 1.0, 130.0, 60.0, 600.0, 2200.0, 1000.0
+CYC, WAKE, NEAR, SEND, FLY, FIRST = 1.0, 280.0, 120.0, 300.0, 2200.0, 800.0
+GATH, SHY, EARLY = 1.5, 60.0, 300.0
 PLAN = {}
 
 SCRATCH = {
@@ -80,7 +81,7 @@ def make_plan(ops, ready):
     rank = [0.0] * n
     for i in range(n - 1, -1, -1):
         o = ops[i]
-        rank[i] = min(c for _, c in o["q"].values()) + o["lag"] + max([WAKE + rank[j] for j in succ[i]] + [0.0])
+        rank[i] = min(c for _, c in o["q"].values()) + o["lag"] + max([WAKE + rank[j] for j in succ[i]] + [0.0]) + o.get("early", 0.0)
     free, fin, start, where, left = {}, [0.0] * n, [0.0] * n, [""] * n, [len(p) for p in pred]
     cand = [i for i in range(n) if not left[i]]
     for _ in range(n):
@@ -93,13 +94,12 @@ def make_plan(ops, ready):
                 t = max(t0, free.get(q, 0.0))
                 for j, raw in pred[i]:
                     t = max(t, fin[j] + WAKE if raw or where[j] != q else start[j])
-                opt.append((t + o["q"][q][1], t, q))
+                opt.append((t + o["q"][q][1] + (SHY if q == "v" and len(o["q"]) > 1 else 0.0), t, q))
             best.append((min(opt), i))
         soon = min(b[0][1] for b in best)
-        pick = max((b for b in best if b[0][1] <= soon + NEAR), key=lambda b: (rank[b[1]], -b[1]))
-        (end, t, q), i = pick
-        start[i], fin[i], where[i] = t, end + ops[i]["lag"], q
-        free[q] = end
+        (_, t, q), i = max((b for b in best if b[0][1] <= soon + NEAR), key=lambda b: (rank[b[1]], -b[1]))
+        free[q] = t + ops[i]["q"][q][1]
+        start[i], fin[i], where[i] = t, free[q] + ops[i]["lag"], q
         cand.remove(i)
         for j in succ[i]:
             left[j] -= 1
@@ -189,7 +189,7 @@ def rank_program(g, core, T, topo):
         V(lambda e: e.tensor_tensor(out, a, b, o), n, r, w)
 
     def copy(out, in_, n, r, w, gather):
-        c = (50 + 1.56 * n * CYC, 65 + 1.56 * n * CYC) if gather else (max(64, n) * CYC, max(64, n) * CYC)
+        c = (50 + GATH * n * CYC, 65 + GATH * n * CYC) if gather else (max(64, n) * CYC, max(64, n) * CYC)
         op({"v": (lambda e: e.tensor_copy(out, in_), c[0]), "s": (lambda e: e.activation(out, in_, AF.Copy), c[1])}, r, w)
 
     def pick(win, wkeys, off, okey):
@@ -343,7 +343,7 @@ def rank_program(g, core, T, topo):
             for p in range(4):
                 (win, wk), (off, ko) = window(t, p), zoff(t, 1, p, h)
                 a = 1024 * t + 256 * p + 128 * h
-                tt(T.Z[:, z + p:z + 512:4], win.indirect(off), T.Ag[:, a:a + 128], OP.add, wk + [ko, ("A", t, h, p)], [("Z", t, h, p)], 260)
+                tt(T.Z[:, z + p:z + 512:4], win.indirect(off), T.Ag[:, a:a + 128], OP.add, wk + [ko, ("A", t, h, p)], [("Z", t, h, p)], 50 + 128 * GATH)
             V(lambda e, lo=lo, hi=hi, z=z: e.quantize_mx(T["qz%d" % t][:, lo:hi], T["qzs%d" % t][:, lo:hi], T.Z[:, z:z + 512]), 150,
               [("Z", t, h, p) for p in range(4)], [("qz", t, h)])
             send(t, h)
@@ -406,8 +406,8 @@ def rank_program(g, core, T, topo):
             i = used["gx"]
             used["gx"] = i + 1
             out, in_ = T.gx[:, 256 * i:256 * i + 256], win.indirect(T.smu[:, w["oa"] + 16 * k:w["oa"] + 16 * k + 16])
-            op({"v": (lambda e, out=out, in_=in_: e.tensor_scalar(out, in_, 2048.0, last, OP.mult, OP.add), 450 * CYC),
-                "s": (lambda e, out=out, in_=in_: e.activation(out, in_, AF.Identity, bias=last, scale=2048.0), 465 * CYC)}, wk, [("gx", i)])
+            op({"v": (lambda e, out=out, in_=in_: e.tensor_scalar(out, in_, 2048.0, last, OP.mult, OP.add), 50 + 256 * GATH * CYC),
+                "s": (lambda e, out=out, in_=in_: e.activation(out, in_, AF.Identity, bias=last, scale=2048.0), 65 + 256 * GATH * CYC)}, wk, [("gx", i)])
             rows.append((out, [("gx", i)]))
         return rows
 
@@ -429,14 +429,13 @@ def rank_program(g, core, T, topo):
         outs = []
         for k in range(32 // width):
             y, ky = scan(rows if width == 32 else [rows[k]], "gyb")
-            sl = lambda v: T.smf[:, v[2] + width * k:v[2] + width * k + width]
             c, kc, _ = small(width)
             d, kd, _ = small(width)
             o, ko, oa = small(width)
             tt(c, y, T.smf[:, w["na"] + width * k:w["na"] + width * k + width], OP.min, ky + [w["kn"]], [kc])
             if first:
                 f, kf, _ = small(width)
-                tt(f, c, sl(first), OP.max, [kc, first[1]], [kf])
+                tt(f, c, T.smf[:, first[2] + width * k:first[2] + width * k + width], OP.max, [kc, first[1]], [kf])
                 c, kc = f, kf
             ts(d, c, lim[t][0], None, OP.min, None, [kc, lim[t][1]], [kd])
             fl = floor[k] if isinstance(floor, list) else floor
@@ -508,6 +507,7 @@ def rank_program(g, core, T, topo):
             (win, wk), (off, ko) = window(3, p), zoff(3, c // 2, p, c % 2)
             copy(T.Tt[:, 512 * c + p:512 * c + 512:4], win.indirect(off), 128, wk + [ko], [("T", c, p)], True)
         V(lambda e, lo=lo, hi=hi: e.quantize_mx(T.oq[:, lo:hi], T.oqs[:, lo:hi], T.Tt[:, 4 * lo:4 * hi]), 150, [("T", c, p) for p in range(4)], [("oq", c)])
+        ops[-1]["early"] = EARLY * (3 - c)
         mm(4 + c, T.vq[:], T.vqs[:], T.oq[:, lo:hi], T.oqs[:, lo:hi], ["vq", ("oq", c)])
         copy(T.yo[:, lo:hi], bank(4 + c), 128, [("bk", 4 + c)], [("yo", c)], False)
         store("y", "so%d" % c, [(T.oc[:, 4 * lo:4 * hi], T.oq[:, lo:hi].bitcast(dt.uint8))], [("oq", c)], [("oc", c)])

@@ -1,3 +1,4 @@
+import math
 import numpy as np
 from concourse.bass import DstId, RemoteDMATransfer
 from concourse.mybir import dt, AluOpType, AxisListType, ActivationFunctionType
@@ -6,11 +7,14 @@ OP = AluOpType
 AF = ActivationFunctionType
 R = 3
 STEP = [1, 2, 4]
-LIFT = 2048
-BASE = 8192
+LIFT = 1024
 SL = 1280
-CYC, WAKE, NEAR, SEND, FLY, FIRST = 1.0, 280.0, 120.0, 300.0, 2200.0, 800.0
-GATH, SHY, EARLY = 1.5, 60.0, 300.0
+UNIT = 2048.0
+HALF = "float16"
+SPLIT = (0, 3, 5)
+COSTS = [(1.0, 160.0, 1.5, 3.5, 1900.0, 140.0), (1.0, 280.0, 1.3, 3.0, 2200.0, 190.0), (1.2, 120.0, 1.8, 4.5, 1800.0, 170.0),
+         (0.85, 220.0, 1.5, 3.5, 2500.0, 220.0)]
+TRIES, HEAT = 16000, 12.0
 PLAN = {}
 
 SCRATCH = {
@@ -25,20 +29,22 @@ SCRATCH = {
     "vin": ("sbuf", [128, 512], "bfloat16"),
     "ones": ("sbuf", [128, 520], "bfloat16"),
     "ez": ("sbuf", [128, 520], "bfloat16"),
-    "vI": ("sbuf", [128, 256], "int32"),
-    "vJ": ("sbuf", [128, 256], "int32"),
-    "st": ("sbuf", [128, 1024], "bfloat16"),
+    "sw": ("sbuf", [128, 32], "bfloat16"),
+    "st": ("sbuf", [128, 512], "bfloat16"),
     "idw": ("sbuf", [128, 512], "bfloat16"),
     "m0r": ("sbuf", [128, 512], "bfloat16"),
     "jr1": ("sbuf", [128, 256], "bfloat16"),
     "Dd": ("sbuf", [128, 1536], "bfloat16"),
     "sgw": ("sbuf", [128, 3 * 272], "bfloat16"),
+    "sg1": ("sbuf", [128, 3 * 256], "bfloat16"),
     "sg2": ("sbuf", [128, 3 * 256], "bfloat16"),
     "gx": ("sbuf", [128, 256 * 24], "bfloat16"),
-    "gyf": ("sbuf", [128, 256 * 16], "float32"),
-    "gyb": ("sbuf", [128, 256 * 12], "bfloat16"),
-    "smi": ("sbuf", [128, 256], "int32"),
-    "smf": ("sbuf", [128, 4096], "float32"),
+    "gy": ("sbuf", [128, 256 * 14], HALF),
+    "d1": ("sbuf", [128, 12 * 768 + 64], HALF),
+    "d0": ("sbuf", [128, 6 * 96], "float32"),
+    "rs": ("sbuf", [128, 6 * 96], "float32"),
+    "smi": ("sbuf", [128, 320], "int32"),
+    "smf": ("sbuf", [128, 2560], "float32"),
     "smu": ("sbuf", [128, 1280], "uint16"),
     "yo": ("sbuf", [128, 512], "float32"),
     "ps": ("psum", [128, 4096], "float32"),
@@ -57,6 +63,12 @@ ENG = {"v": "ve", "s": "ac", "t": "pe", "g": "gp"}
 LOADS = ["lm", "lx", "ll", "lu", "lw", "lv"]
 STORES = ["so0", "so1", "so2", "so3", "sy0", "sy1", "sy2", "sy3", "som", "sos"]
 SEMAPHORES = ["ve", "ac", "pe", "gp", "sent"] + ["arr%d%d" % (t, h) for t in range(R) for h in range(2)] + LOADS + STORES
+MAIN = ("zl", "Fn", "A", "Z", "qz", "lz", "H", "qh", "flag", "lim", "T", "oq", "yo")
+
+
+def price(o, q, c):
+    fix, cyc, gat, sca = o["q"][q][1]
+    return c[5] if q == "t" else fix + c[0] * (cyc + c[2] * gat + c[3] * sca)
 
 
 def make_plan(ops, ready):
@@ -78,34 +90,128 @@ def make_plan(ops, ready):
         pred[i] = sorted(p.items())
         for j in p:
             succ[j].append(i)
+    first = [max([ready.get(k, 0.0) for k in o["r"]] + [0.0]) for o in ops]
+    lag = [[c[4] if o["kind"] == "send" else 1700.0 if o["kind"] == "dma" else 0.0 for o in ops] for c in COSTS]
+    cost = [[{q: price(o, q, c) for q in o["q"]} for o in ops] for c in COSTS]
+    busy = [o.get("busy", 0.0) for o in ops]
+    weight = [0.3 / n if o["w"][0][0] in MAIN else 0.0 for o in ops]
     rank = [0.0] * n
     for i in range(n - 1, -1, -1):
-        o = ops[i]
-        rank[i] = min(c for _, c in o["q"].values()) + o["lag"] + max([WAKE + rank[j] for j in succ[i]] + [0.0]) + o.get("early", 0.0)
-    free, fin, start, where, left = {}, [0.0] * n, [0.0] * n, [""] * n, [len(p) for p in pred]
-    cand = [i for i in range(n) if not left[i]]
-    for _ in range(n):
-        best = []
-        for i in cand:
-            o = ops[i]
-            t0 = max([ready.get(k, 0.0) for k in o["r"]] + [0.0])
-            opt = []
-            for q in o["q"]:
-                t = max(t0, free.get(q, 0.0))
+        rank[i] = min(cost[0][i].values()) + lag[0][i] + max([COSTS[0][1] + rank[j] for j in succ[i]] + [0.0])
+
+    def greedy():
+        free, fin, start, where, left = {}, [0.0] * n, [0.0] * n, [""] * n, [len(p) for p in pred]
+        cand = [i for i in range(n) if not left[i]]
+        for _ in range(n):
+            best = []
+            for i in cand:
+                opt = []
+                for q in ops[i]["q"]:
+                    t = max(first[i], free.get(q, 0.0))
+                    for j, raw in pred[i]:
+                        t = max(t, fin[j] + COSTS[0][1] if raw or where[j] != q else start[j])
+                    opt.append((t + cost[0][i][q] + (60.0 if q == "v" and len(ops[i]["q"]) > 1 else 0.0), t, q))
+                best.append((min(opt), i))
+            soon = min(b[0][1] for b in best)
+            (_, t, q), i = max((b for b in best if b[0][1] <= soon + 120.0), key=lambda b: (rank[b[1]], -b[1]))
+            start[i], where[i] = t, q
+            free[q] = t + cost[0][i][q]
+            fin[i] = free[q] + lag[0][i]
+            cand.remove(i)
+            for j in succ[i]:
+                left[j] -= 1
+                if not left[j]:
+                    cand.append(j)
+        return sorted(range(n), key=lambda i: (start[i], i)), where
+
+    free, start, fin = [None] * len(COSTS), [None] * len(COSTS), [None] * len(COSTS)
+
+    def span(seq, where, a):
+        total = 0.0
+        for k, c in enumerate(COSTS):
+            wake, ck, lk, snap, sk, fk = c[1], cost[k], lag[k], free[k][:a + 1], start[k], fin[k]
+            f5, end, late = snap[a]
+            f5 = dict(f5)
+            for i in seq[a:]:
+                q = where[i]
+                t = first[i]
+                f = f5[q]
+                if f > t:
+                    t = f
                 for j, raw in pred[i]:
-                    t = max(t, fin[j] + WAKE if raw or where[j] != q else start[j])
-                opt.append((t + o["q"][q][1] + (SHY if q == "v" and len(o["q"]) > 1 else 0.0), t, q))
-            best.append((min(opt), i))
-        soon = min(b[0][1] for b in best)
-        (_, t, q), i = max((b for b in best if b[0][1] <= soon + NEAR), key=lambda b: (rank[b[1]], -b[1]))
-        free[q] = t + ops[i]["q"][q][1]
-        start[i], fin[i], where[i] = t, free[q] + ops[i]["lag"], q
-        cand.remove(i)
-        for j in succ[i]:
-            left[j] -= 1
-            if not left[j]:
-                cand.append(j)
-    return [(i, where[i]) for i in sorted(range(n), key=lambda i: (start[i], i))]
+                    f = fk[j] + wake if raw or where[j] != q else sk[j]
+                    if f > t:
+                        t = f
+                sk[i] = t
+                f = t + ck[i][q]
+                f5[q] = f
+                if busy[i]:
+                    f = max(f + lk[i], f5["e"]) + busy[i]
+                    f5["e"] = f
+                    f += 500.0
+                else:
+                    f += lk[i]
+                fk[i] = f
+                late += f * weight[i]
+                if f > end:
+                    end = f
+                snap.append((dict(f5), end, late))
+            free[k] = snap
+            total += end + late
+        return total
+
+    for k in range(len(COSTS)):
+        free[k], start[k], fin[k] = [({"v": 0.0, "s": 0.0, "t": 0.0, "g": 0.0, "y": 0.0, "e": 0.0}, 0.0, 0.0)], [0.0] * n, [0.0] * n
+    seq, where = greedy()
+    seed = [12345]
+
+    def draw(m):
+        seed[0] = (seed[0] * 1103515245 + 12345) % 2147483648
+        return (seed[0] >> 8) % m
+
+    now = span(seq, where, 0)
+    kept = (now, list(seq), list(where))
+    pos = [0] * n
+    for k, i in enumerate(seq):
+        pos[i] = k
+    both = [i for i in range(n) if len(ops[i]["q"]) > 1]
+    for it in range(TRIES):
+        heat = HEAT * (1.0 - it / TRIES) + 0.1
+        flip = draw(6) == 0
+        i = both[draw(len(both))] if flip else draw(n)
+        a = b = pos[i]
+        if not flip:
+            lo = max([pos[j] for j, _ in pred[i]] + [-1]) + 1
+            hi = min([pos[j] for j in succ[i]] + [n]) - 1
+            if hi <= lo:
+                continue
+            if draw(3):
+                d = 1 if draw(2) else -1
+                b = a + d
+                while lo <= b <= hi and where[seq[b]] != where[i]:
+                    b += d
+            else:
+                b = max(lo, a - 60) + draw(min(hi, a + 60) - max(lo, a - 60) + 1)
+            if b == a or b < lo or b > hi:
+                continue
+        old = (where[i], list(free), [list(s) for s in start], [list(s) for s in fin])
+        if flip:
+            where[i] = [q for q in sorted(ops[i]["q"]) if q != where[i]][0]
+        else:
+            seq.insert(b, seq.pop(a))
+        new = span(seq, where, min(a, b))
+        if new <= now or draw(10000) < 10000 * math.exp((now - new) / heat):
+            now = new
+            for k in range(min(a, b), max(a, b) + 1):
+                pos[seq[k]] = k
+            if now < kept[0]:
+                kept = (now, list(seq), list(where))
+        else:
+            where[i] = old[0]
+            seq.insert(a, seq.pop(b))
+            for k in range(len(COSTS)):
+                free[k], start[k], fin[k] = old[1][k], old[2][k], old[3][k]
+    return [(i, kept[2][i]) for i in kept[1]]
 
 
 def rank_program(g, core, T, topo):
@@ -163,21 +269,21 @@ def rank_program(g, core, T, topo):
         count[sem] = count.get(sem, 0) + 1
         note((sem, count[sem], dict(known[q])), o["r"], o["w"])
 
-    def op(qs, r, w, lag=0.0, kind="call"):
-        ops.append({"q": qs, "r": list(r), "w": list(w), "lag": lag, "kind": kind})
+    def op(qs, r, w, kind="call"):
+        ops.append({"q": qs, "r": list(r), "w": list(w), "kind": kind})
 
-    used = {"smf": 0, "smu": 0, "smi": 0, "gx": 0, "gyf": 0, "gyb": 0}
+    used = {"smf": 0, "smu": 0, "smi": 0, "gx": 0, "gy": 0}
 
     def small(n, buf="smf"):
-        a = -(-used[buf] // 32) * 32
+        a = -(-used[buf] // (32 if n > 8 else 8)) * (32 if n > 8 else 8)
         used[buf] = a + n
         return T[buf][:, a:a + n], (buf, a), a
 
     def V(call, n, r=(), w=()):
-        op({"v": (call, max(64, n) * CYC)}, r, w)
+        op({"v": (call, (0.0, max(64, n), 0, 0))}, r, w)
 
     def G(call, n, r=(), w=()):
-        op({"g": (call, 150 + 2 * n * CYC)}, r, w)
+        op({"g": (call, (150.0, 2 * n, 0, 0))}, r, w)
 
     def ts(out, in0, s1, s2, op0, op1, r, w, n=32):
         if op1 is None:
@@ -189,8 +295,16 @@ def rank_program(g, core, T, topo):
         V(lambda e: e.tensor_tensor(out, a, b, o), n, r, w)
 
     def copy(out, in_, n, r, w, gather):
-        c = (50 + GATH * n * CYC, 65 + GATH * n * CYC) if gather else (max(64, n) * CYC, max(64, n) * CYC)
+        c = ((50.0, 0, n, 0), (65.0, 0, n, 0)) if gather else ((0.0, max(64, n), 0, 0), (0.0, max(64, n), 0, 0))
         op({"v": (lambda e: e.tensor_copy(out, in_), c[0]), "s": (lambda e: e.activation(out, in_, AF.Copy), c[1])}, r, w)
+
+    def affine(out, in_, scale, bias, r, w, n=32):
+        op({"v": (lambda e: e.tensor_scalar(out, in_, scale, bias, OP.mult, OP.add), (0.0, max(64, n), 0, 0)),
+            "s": (lambda e: e.activation(out, in_, AF.Copy, bias=bias, scale=scale), (0.0, max(64, n), 0, 0))}, r, w)
+
+    def fill(out, v, n, cycles, key):
+        op({"v": (lambda e: e.memset(out, float(v)), (0.0, cycles, 0, 0)),
+            "g": (lambda e: e.iota(out, [[0, n]], v, 0, allow_small_or_imprecise_dtypes=True), (150.0, 2 * n, 0, 0))}, [], [key])
 
     def pick(win, wkeys, off, okey):
         i = used["gx"]
@@ -199,15 +313,14 @@ def rank_program(g, core, T, topo):
         copy(out, win.indirect(off), 256, list(wkeys) + [okey], [("gx", i)], True)
         return out, [("gx", i)]
 
-    def scan(rows, buf="gyf"):
-        first = used[buf]
-        col, n = (512, 256) if buf == "gyf" else (768, 128)
+    def scan(rows):
+        first = used["gy"]
         for row, keys in rows:
-            i = used[buf]
-            used[buf] = i + 1
-            V(lambda e, i=i, row=row: e.tensor_tensor_scan(T[buf][:, 256 * i:256 * i + 256], T.st[:, col:col + 256], row, 0.0, OP.add, OP.max),
-              n, keys + [("st", col)], [(buf, i)])
-        return T[buf][:, 256 * first + 15:256 * first + 256 * len(rows):16], [(buf, first + k) for k in range(len(rows))]
+            i = used["gy"]
+            used["gy"] = i + 1
+            V(lambda e, i=i, row=row: e.tensor_tensor_scan(T.gy[:, 256 * i:256 * i + 256], T.st[:, 0:256], row, 0.0, OP.add, OP.max),
+              128, keys + [("st", 0)], [("gy", i)])
+        return T.gy[:, 256 * first + 15:256 * first + 256 * len(rows):16], [("gy", first + k) for k in range(len(rows))]
 
     L = T.Lst
     dmas("y", "lm", [(L[:, 0:32], T.m[:])], w=["m_"])
@@ -219,74 +332,95 @@ def rank_program(g, core, T, topo):
     dmas("y", "lu", [(T.uin[:], T.u[:])], w=["uin"])
     dmas("y", "lw", [(T.wq[:].bitcast(dt.uint8), T.wc[:]), (T.wqs[:], T.ws[:])], w=["wq"])
     dmas("y", "lv", [(T.vin[:], T.v[:])], w=["vin"])
-    ready = {"lists": 2500.0, "ld_": 2600.0, "X0": 5000.0, "uin": 5600.0, "wq": 7200.0, "vin": 7800.0}
+    ready = {"lists": 2300.0, "ld_": 2350.0, "X0": 4600.0, "uin": 5200.0, "wq": 6800.0, "vin": 7300.0}
 
+    vI, kvI, _ = small(32, "smi")
     pI, kpI, _ = small(32, "smi")
-    kI, kkI, _ = small(32, "smi")
-    G(lambda e: e.iota(T.vI[:], [[-1, 256]], 512, 1), 256, w=["vI"])
+    kI, kkI, akI = small(32, "smi")
+    G(lambda e: e.iota(vI, [[-1, 32]], 512, 1), 32, w=[kvI])
     G(lambda e: e.iota(pI, [[0, 32]], 0, 1), 32, w=[kpI])
     G(lambda e: e.iota(T.idw[:], [[1, 512]], -256, 0, allow_small_or_imprecise_dtypes=True), 512, w=["idw"])
     G(lambda e: e.iota(kI, [[16, 32]], 0, 0), 32, w=[kkI])
     G(lambda e: e.iota(T.jr1[:], [[1, 256]], 1, 0, allow_small_or_imprecise_dtypes=True), 256, w=["jr1"])
     eps, keps, _ = small(1)
+    zero, kzero, _ = small(32)
+    low, klow, _ = small(96)
+    fill(T.d0[:], -16, 576, 576, "d0")
+    V(lambda e: e.memset(low, -1.0), 96, w=[klow])
+    V(lambda e: e.memset(zero, 0.0), 32, w=[kzero])
     for t in range(R):
-        V(lambda e, t=t: e.memset(T.Dd[:, 512 * t:512 * t + 512], 0.0), 256, w=["D%d" % t])
-        V(lambda e, t=t: e.memset(T.sgw[:, 272 * t:272 * t + 1], -1.0), 1, w=[("pad", t)])
+        fill(T.Dd[:, 512 * t:512 * t + 512], 0, 512, 256, "D%d" % t)
+        V(lambda e, t=t: e.memset(T.sgw[:, 272 * t:272 * t + 1], 0.0), 1, w=[("pad", t)])
     V(lambda e: e.memset(eps, 1e-37), 1, w=[keps])
-    ts(T.vJ[:], T.vI[:], 15, None, OP.bitwise_and, None, ["vI"], ["vJ"], 256)
-    ts(T.st[:, 0:256], T.vJ[:], 15, LIFT, OP.is_equal, OP.mult, ["vJ"], [("st", 0)], 256)
-    ts(T.st[:, 256:512], T.vJ[:], 0, -2 * LIFT, OP.is_equal, OP.mult, ["vJ"], [("st", 256)], 256)
-    tt(T.st[:, 512:768], T.st[:, 0:256], T.st[:, 256:512], OP.add, [("st", 0), ("st", 256)], [("st", 512)], 512)
-    ts(T.st[:, 768:1024], T.st[:, 512:768], BASE / LIFT, None, OP.mult, None, [("st", 512)], [("st", 768)], 128)
+    vJ, kvJ, _ = small(32, "smi")
     p15, kp15, ap15 = small(32, "smi")
     p7, kp7, ap7 = small(32, "smi")
+    p31, kp31, _ = small(32, "smi")
     pg, kpg, apg = small(32, "smi")
+    s_a, ks_a, _ = small(32)
+    s_b, ks_b, _ = small(32)
+    r16, kr16, _ = small(16, "smu")
+    ts(vJ, vI, 15, None, OP.bitwise_and, None, [kvI], [kvJ])
+    ts(p15, pI, 15, None, OP.bitwise_and, None, [kpI], [kp15])
+    ts(s_a, vJ, 15, LIFT, OP.is_equal, OP.mult, [kvJ], [ks_a])
+    ts(s_b, vJ, 0, -2 * LIFT, OP.is_equal, OP.mult, [kvJ], [ks_b])
+    V(lambda e: e.tensor_copy(r16, T.smi[:, ap15:ap15 + 16]), 16, [kp15], [kr16])
+    tt(T.sw[:], s_a, s_b, OP.add, [ks_a, ks_b], ["sw"])
+    copy(T.st[:, 0:256], T.sw[:].indirect(r16), 256, ["sw", kr16], [("st", 0)], True)
+    op({"s": (lambda e: e.activation(T.st[:, 256:512], T.sw[:].indirect(r16), AF.Copy, scale=1.0 / LIFT), (65.0, 0, 256, 0))}, ["sw", kr16], [("st", 256)])
     lift, klift, _ = small(1)
     last, klast, _ = small(1)
-    ts(p15, pI, 15, None, OP.bitwise_and, None, [kpI], [kp15])
     ts(lift, T.smi[:, ap15:ap15 + 1], 15, LIFT, OP.is_lt, OP.mult, [kp15], [klift])
-    ts(last, T.smi[:, ap15:ap15 + 1], 15, BASE, OP.is_equal, OP.mult, [kp15], [klast])
+    ts(last, T.smi[:, ap15:ap15 + 1], 15, 2.0, OP.is_equal, OP.subtract, [kp15], [klast])
     down = []
     for p in range(4):
         down.append(small(1))
         ts(down[p][0], lift, -4.0, float(1024 + p), OP.mult, OP.add, [klift], [down[p][1]])
+    mlift, kmlift, _ = small(1)
+    ts(mlift, lift, -1.0, None, OP.mult, None, [klift], [kmlift])
     slot = []
     for t in range(R):
         slot.append(small(1))
-        ts(slot[t][0], lift, -1.0, float(BASE + 511 + 256 * t), OP.mult, OP.add, [klift], [slot[t][1]])
-    V(lambda e: e.memset(T.ones[:], 1.0), 260, w=["ones"])
+        ts(slot[t][0], lift, -1.0, float(511 + 256 * t - SL), OP.mult, OP.add, [klift], [slot[t][1]])
+    fill(T.ones[:], 1, 520, 260, "ones")
     G(lambda e: e.affine_select(T.ez[:], T.ones[:], [[-1, 520]], OP.is_equal, 0.0, 4, 4), 520, ["ones"], ["ez"])
-    idl, kidl, _ = small(32)
     idt, kidt, _ = small(32)
+    f_a, kf_a, _ = small(32)
+    f_b, kf_b, _ = small(32)
     fr8, kfr8, _ = small(32)
     gfr, kgfr, _ = small(1)
     U16, kU16, u0 = small(16, "smu")
     ts(p7, pI, 7, None, OP.bitwise_and, None, [kpI], [kp7])
+    ts(p31, pI, 31, None, OP.bitwise_and, None, [kpI], [kp31])
     ts(pg, pI, 4, None, OP.arith_shift_right, None, [kpI], [kpg])
-    ts(fr8, p7, 0.125, None, OP.mult, None, [kp7], [kfr8])
+    ts(f_a, p31, 0.125, None, OP.mult, None, [kp31], [kf_a])
+    ts(f_b, p31, 8, -8192.0, OP.is_ge, OP.mult, [kp31], [kf_b])
+    tt(fr8, f_a, f_b, OP.add, [kf_a, kf_b], [kfr8])
     ts(gfr, T.smi[:, apg:apg + 1], 0.125, None, OP.mult, None, [kpg], [kgfr])
     tt(idt, p15, kI, OP.add, [kp15, kkI], [kidt])
-    ts(idl, idt, float(BASE), None, OP.add, None, [kidt], [kidl])
-    V(lambda e: e.tensor_copy(T.smu[:, u0:u0 + 8], T.smi[:, 32:40]), 8, [kkI], [(kU16, 0)])
+    V(lambda e: e.tensor_copy(T.smu[:, u0:u0 + 8], T.smi[:, akI:akI + 8]), 8, [kkI], [(kU16, 0)])
     ts(T.smu[:, u0 + 8:u0 + 16], T.smi[:, ap7:ap7 + 8], 16, None, OP.mult, None, [kp7], [(kU16, 1)])
 
     L16, kL16, l0 = small(128, "smu")
     D16, kD16, d0 = small(48, "smu")
-    Lf, kLf, lf = small(128)
     mf, kmf, amf = small(32)
-    V(lambda e: e.tensor_copy(L16, L[:, 0:128]), 128, ["lists"], [kL16])
+    V(lambda e: e.tensor_copy(T.smu[:, l0:l0 + 32], L[:, 0:32]), 32, ["lists"], [(kL16, 0)])
+    V(lambda e: e.tensor_copy(T.smu[:, l0 + 32:l0 + 128], L[:, 32:128]), 96, ["lists"], [(kL16, 1)])
 
     def la16(t):
-        return T.smu[:, l0 + 32 + 16 * t:l0 + 48 + 16 * t], kL16
+        return T.smu[:, l0 + 32 + 16 * t:l0 + 48 + 16 * t], (kL16, 1)
 
     def lb16(t):
-        return T.smu[:, l0 + 80 + 16 * t:l0 + 96 + 16 * t], kL16
+        return T.smu[:, l0 + 80 + 16 * t:l0 + 96 + 16 * t], (kL16, 1)
 
     def inverse(t):
-        V(lambda e: e.tensor_copy(T.Dd[:, 512 * t:512 * t + 512].indirect(T.smu[:, d0 + 16 * t:d0 + 16 * t + 16]), T.jr1[:]), 1000, ["jr1", kD16], ["D%d" % t])
+        op({"v": (lambda e: e.tensor_copy(T.Dd[:, 512 * t:512 * t + 512].indirect(T.smu[:, d0 + 16 * t:d0 + 16 * t + 16]), T.jr1[:]), (50.0, 0, 0, 256))},
+           ["jr1", kD16], ["D%d" % t])
 
-    copy(T.m0r[:], T.idw[:].indirect(T.smu[:, l0:l0 + 32]), 512, ["idw", kL16], ["m0r"], True)
-    rows0 = [pick(T.m0r[:], ["m0r"], *la16(0)), pick(T.m0r[:], ["m0r"], *lb16(0))]
+    for k in range(2):
+        copy(T.m0r[:, 256 * k:256 * k + 256], T.idw[:].indirect(T.smu[:, l0 + 16 * k:l0 + 16 * k + 16]), 256, ["idw", (kL16, 0)], [("m0r", k)], True)
+    km0r = [("m0r", 0), ("m0r", 1)]
+    rows0 = [pick(T.m0r[:], km0r, *la16(0)), pick(T.m0r[:], km0r, *lb16(0))]
     V(lambda e: e.tensor_copy(D16, L[:, 128:176]), 48, ["ld_"], [kD16])
     zl0 = small(128, "smu")[2]
     zl = [None] + [small(32, "smu")[2] for _ in range(R)]
@@ -299,11 +433,6 @@ def rank_program(g, core, T, topo):
     for p in range(4):
         m4.append(small(32, "smu"))
         ts(m4[p][0], L[:, 0:32], 4, p, OP.mult, OP.add, ["lists"], [m4[p][1]])
-    ts(Lf, L[:, 0:128], float(BASE), None, OP.add, None, ["lists"], [kLf], 128)
-    ab2, kab2, aa = small(32)
-    V(lambda e: e.tensor_copy(T.smf[:, aa:aa + 16], T.smf[:, lf + 64:lf + 80]), 16, [kLf], [(kab2, 0)])
-    V(lambda e: e.tensor_copy(T.smf[:, aa + 16:aa + 32], T.smf[:, lf + 112:lf + 128]), 16, [kLf], [(kab2, 1)])
-    kab = [(kab2, 0), (kab2, 1)]
 
     def zoff(t, half, p, k):
         a = zl[t] + 16 * half + 8 * k if t else zl0 + 64 * half + 16 * p + 8 * k
@@ -330,7 +459,7 @@ def rank_program(g, core, T, topo):
             count["sent"] = count.get("sent", 0) + len(eng)
             count[name] = len(eng)
             writer[("lz", t, h)] = (name, len(eng), {})
-        op({"g": (call, SEND + (FIRST if t + h == 0 else 0.0))}, [("qz", t, h)], [("lz", t, h)], FLY, "send")
+        op({"g": (call, (300.0 + (800.0 if t + h == 0 else 0.0), 0, 0, 0))}, [("qz", t, h)], [("lz", t, h)], "send")
 
     def operands(t):
         for h in range(2):
@@ -343,7 +472,9 @@ def rank_program(g, core, T, topo):
             for p in range(4):
                 (win, wk), (off, ko) = window(t, p), zoff(t, 1, p, h)
                 a = 1024 * t + 256 * p + 128 * h
-                tt(T.Z[:, z + p:z + 512:4], win.indirect(off), T.Ag[:, a:a + 128], OP.add, wk + [ko, ("A", t, h, p)], [("Z", t, h, p)], 50 + 128 * GATH)
+                out, in_, ag = T.Z[:, z + p:z + 512:4], win.indirect(off), T.Ag[:, a:a + 128]
+                op({"v": (lambda e, out=out, in_=in_, ag=ag: e.tensor_tensor(out, in_, ag, OP.add), (50.0, 0, 128, 0))},
+                   wk + [ko, ("A", t, h, p)], [("Z", t, h, p)])
             V(lambda e, lo=lo, hi=hi, z=z: e.quantize_mx(T["qz%d" % t][:, lo:hi], T["qzs%d" % t][:, lo:hi], T.Z[:, z:z + 512]), 150,
               [("Z", t, h, p) for p in range(4)], [("qz", t, h)])
             send(t, h)
@@ -352,11 +483,10 @@ def rank_program(g, core, T, topo):
         return T.ps[:, 512 * k:512 * k + 128]
 
     def mm(k, lq, ls, rq, rs, r):
-        op({"t": (lambda e: e.matmul_mx(bank(k), lq, ls, rq, rs, True, True), 170.0)}, r, [("bk", k)])
+        op({"t": (lambda e: e.matmul_mx(bank(k), lq, ls, rq, rs, True, True), (0.0, 150, 0, 0))}, r, [("bk", k)])
 
     s1 = [[small(1) for _ in range(2)] for _ in range(R)]
     s2 = [[small(1) for _ in range(2)] for _ in range(R)]
-    own = [[small(1) for _ in range(2)] for _ in range(R)]
 
     def layer(t, h):
         lo, hi, z = 128 * h, 128 * h + 128, 1024 * t + 512 * h
@@ -364,34 +494,54 @@ def rank_program(g, core, T, topo):
             mm(b, T.wq[:, 128 * b:128 * b + 128], T.wqs[:, 128 * b:128 * b + 128], T["lz%d" % t][:, lo:hi], T["lzs%d" % t][:, lo:hi], ["wq", ("lz", t, h)])
         for b in range(4):
             out = T.Hb[:, z + b:z + 512:4]
-            op({"v": (lambda e, b=b, out=out: e.tensor_scalar(out, bank(b), 0.0, 0.015625, OP.max, OP.mult), 128 * CYC),
-                "s": (lambda e, b=b, out=out: e.activation(out, bank(b), AF.Relu, scale=0.015625), 128 * CYC)}, [("bk", b)], [("H", t, h, b)])
+            op({"v": (lambda e, b=b, out=out: e.tensor_scalar(out, bank(b), 0.0, 0.015625, OP.max, OP.mult), (0.0, 128, 0, 0)),
+                "s": (lambda e, b=b, out=out: e.activation(out, bank(b), AF.Relu, scale=0.015625), (0.0, 128, 0, 0))}, [("bk", b)], [("H", t, h, b)])
         V(lambda e: e.quantize_mx(T["qh%d" % t][:, lo:hi], T["qhs%d" % t][:, lo:hi], T.Hb[:, z:z + 512]), 150, [("H", t, h, b) for b in range(4)], [("qh", t, h)])
 
     def scores(t, h):
         lo, hi = 128 * h, 128 * h + 128
         q, s = T["qh%d" % t][:, lo:hi], T["qhs%d" % t][:, lo:hi]
-        bs, bd = ((4, 5), (6, 7, 4, 5)) if h == 0 else ((6, 7), (0, 1, 2, 3))
-        for i in range(2):
-            mm(bs[i], T.up[:, 128 * i:128 * i + 128], T.ups[:, 128 * i:128 * i + 128], q, s, ["up", "ups", ("qh", t, h)])
-            out = T.sgw[:, 272 * t + 1 + lo:272 * t + 1 + hi] if i == 0 else T.sg2[:, 256 * t + lo:256 * t + hi]
-            sm = (s1, s2)[i][t][h]
-            op({"s": (lambda e, i=i, out=out, sm=sm: e.activation(out, bank(bs[i]), AF.Sign, bias=eps, accum_out=sm[0]), 150.0)},
-               [("bk", bs[i]), keps], [("sg%d" % i, t, h), sm[1]])
+        bs, bd = ((4, 5, 6), (7, 4, 5, 6)) if h == 0 else ((7, 4, 5), (0, 1, 2, 3))
+        for k, i in enumerate((1, 0, 0)):
+            mm(bs[k], T.up[:, 128 * i:128 * i + 128], T.ups[:, 128 * i:128 * i + 128], q, s, ["up", "ups", ("qh", t, h)])
+        for k, (name, sm) in ((0, ("sg2", s2[t][h])), (2, ("sg1", s1[t][h]))):
+            out = T[name][:, 256 * t + lo:256 * t + hi]
+            op({"s": (lambda e, k=k, out=out, sm=sm: e.activation(out, bank(bs[k]), AF.Sign, bias=eps, accum_out=sm[0]), (20.0, 128, 0, 0))},
+               [("bk", bs[k]), keps], [(name, t, h), sm[1]])
+        ts(T.sgw[:, 272 * t + 1 + lo:272 * t + 1 + hi], bank(bs[1]), 0.0, None, OP.is_ge, None, [("bk", bs[1])], [("sgw", t, h)], 128)
         for b in range(4):
             mm(bd[b], T.eq[:, 128 * b:128 * b + 128], T.eqs[:, 128 * b:128 * b + 128], q, s, [("eq", b), ("qh", t, h)])
             a = SL * b + 512 + 256 * t + lo
             copy(T.F[:, a:a + 128], bank(bd[b]), 128, [("bk", bd[b])], [("Fn", t, h, b)], False)
-        add, kadd = (gfr, kgfr) if h == 0 else own[t][0][:2]
-        ts(own[t][h][0], s1[t][h][0], add, None, OP.add, None, [s1[t][h][1], kadd], [own[t][h][1]])
 
-    def where(t, rows):
+    def older(c, n=32, k=0):
+        a = 1536 * c + 768 * k + 61
+        return T.d1[:, a:a + 48 * n - 47:48]
+
+    def backed(c, n=32, k=0):
+        a = 1536 * c + 768 * k + 77
+        return T.d1[:, a:a + 48 * n - 47:48]
+
+    def result(c, k=None):
+        return T.rs[:, 96 * c + 2:96 * c + 96:3] if k is None else T.rs[:, 96 * c + 48 * k + 2:96 * c + 48 * k + 48:3]
+
+    def kres(c):
+        return [("rs", c, 0), ("rs", c, 1)]
+
+    V(lambda e: e.tensor_copy(older(0, 96), low), 96, [klow], [("old", 0), ("old", 1), ("old", 2)])
+    for c, t in ((0, 1), (1, 2), (3, 2)):
+        for k in range(2):
+            a = 32 + 48 * k + 16 * t
+            ts(backed(c, 16, k), L[:, a:a + 16], float(-SL), 1.0 / UNIT, OP.add, OP.mult, ["lists"], [("bak", c, k)])
+    for c in (2, 4):
+        ts(backed(c), idt, float(-SL), 1.0 / UNIT, OP.add, OP.mult, [kidt], [("bak", c, 0), ("bak", c, 1)])
+
+    def where(c, t, rows):
         y, ky = scan(rows)
-        n, kn, na = small(32)
-        ts(n, y, slot[t][0], None, OP.add, None, ky + [slot[t][1]], [kn])
         o, ko, oa = small(32, "smu")
-        ts(o, n, float(-BASE - 511 - 256 * t), None, OP.add, None, [kn], [ko])
-        return {"n": n, "kn": kn, "na": na, "oa": oa, "ko": ko}
+        ts(o, y, mlift, None, OP.add, None, ky + [kmlift], [ko])
+        ts(T.d0[:, 96 * c + 1:96 * c + 96:3], y, slot[t][0], 1.0 / UNIT, OP.add, OP.mult, ky + [slot[t][1], "d0"], [("n", c)])
+        return oa, ko
 
     def ident(t):
         return [(T.Dd[:, 512 * t + 256 * k:512 * t + 256 * k + 256], ["D%d" % t]) for k in range(2)]
@@ -399,67 +549,59 @@ def rank_program(g, core, T, topo):
     def find(t, l):
         return [pick(T.Dd[:, 512 * t:512 * t + 512], ["D%d" % t], *l2) for l2 in (la16(l), lb16(l))]
 
-    def signs(t, w):
-        win, wk = T.sgw[:, 272 * t:272 * t + 257], [("pad", t), ("sg0", t, 0), ("sg0", t, 1), klast, w["ko"]]
-        rows = []
-        for k in range(2):
-            i = used["gx"]
-            used["gx"] = i + 1
-            out, in_ = T.gx[:, 256 * i:256 * i + 256], win.indirect(T.smu[:, w["oa"] + 16 * k:w["oa"] + 16 * k + 16])
-            op({"v": (lambda e, out=out, in_=in_: e.tensor_scalar(out, in_, 2048.0, last, OP.mult, OP.add), 50 + 256 * GATH * CYC),
-                "s": (lambda e, out=out, in_=in_: e.activation(out, in_, AF.Identity, bias=last, scale=2048.0), 65 + 256 * GATH * CYC)}, wk, [("gx", i)])
-            rows.append((out, [("gx", i)]))
-        return rows
-
-    lim = [small(1) for _ in range(R)]
-    nlim, knlim, _ = small(1)
+    rk = [small(1) for _ in range(R)]
 
     def limit(t):
         kb, kkb, _ = small(32)
         kt, kkt, ka = small(32)
-        c8, kc8, _ = small(8)
+        c8, kc8, _ = small(12)
+        own, kown, _ = small(1)
         ts(kb, fr8, s2[t][0][0], s2[t][1][0], OP.add, OP.add, [kfr8, s2[t][0][1], s2[t][1][1]], [kkb])
         V(lambda e: e.transpose(kt, kb), 32, [kkb], [kkt])
-        ts(c8, T.smf[:, ka:ka + 8], own[t][1][0], float(BASE), OP.is_lt, OP.mult, [kkt, own[t][1][1]], [kc8])
-        V(lambda e: e.tensor_reduce(lim[t][0], c8, AxisListType.X, OP.add), 8, [kc8], [lim[t][1]])
-        if t == 2:
-            V(lambda e: e.tensor_reduce(nlim, c8, AxisListType.X, OP.add, negate=True), 8, [kc8], [knlim])
+        ts(own, gfr, s1[t][0][0], s1[t][1][0], OP.add, OP.add, [kgfr, s1[t][0][1], s1[t][1][1]], [kown])
+        op({"s": (lambda e: e.activation(c8, T.smf[:, ka:ka + 12], AF.Sign, bias=own, scale=-1.0, accum_out=rk[t][0]), (20.0, 64, 0, 0))},
+           [kkt, kown], [kc8, rk[t][1]])
 
-    def cut(t, w, rows, first, floor, width=32):
-        outs = []
-        for k in range(32 // width):
-            y, ky = scan(rows if width == 32 else [rows[k]], "gyb")
-            c, kc, _ = small(width)
-            d, kd, _ = small(width)
-            o, ko, oa = small(width)
-            tt(c, y, T.smf[:, w["na"] + width * k:w["na"] + width * k + width], OP.min, ky + [w["kn"]], [kc])
-            if first:
-                f, kf, _ = small(width)
-                tt(f, c, T.smf[:, first[2] + width * k:first[2] + width * k + width], OP.max, [kc, first[1]], [kf])
-                c, kc = f, kf
-            ts(d, c, lim[t][0], None, OP.min, None, [kc, lim[t][1]], [kd])
-            fl = floor[k] if isinstance(floor, list) else floor
-            tt(o, d, fl[0], OP.max, [kd] + fl[1], [ko])
-            outs.append((o, ko, oa))
-        return outs
+    def merge(c, t, off):
+        oa, ko = off
+        win, wk = T.sgw[:, 272 * t:272 * t + 257], [("pad", t), ("sgw", t, 0), ("sgw", t, 1), klast, ko]
+        ts(T.d0[:, 96 * c + 2:96 * c + 96:3], zero, rk[t][0], None, OP.add, None, [kzero, rk[t][1], "d0"], [("lim", c)])
+        parts = 2 if c in SPLIT else 1
+        w = 256 // parts
+        for k in range(2):
+            i = used["gx"]
+            used["gx"] = i + 1
+            row = T.gx[:, 256 * i:256 * i + 256]
+            for d in range(parts):
+                o = oa + 16 * k + 8 * d
+                out, in_ = T.gx[:, 256 * i + w * d:256 * i + w * d + w], win.indirect(T.smu[:, o:o + 16 // parts])
+                op({"v": (lambda e, out=out, in_=in_: e.tensor_scalar(out, in_, last, None, OP.add), (50.0, 0, w, 0)),
+                    "s": (lambda e, out=out, in_=in_: e.activation(out, in_, AF.Identity, bias=last), (65.0, 0, w, 0))}, wk, [("gx", i, d)])
+            a = 1536 * c + 768 * k
+            V(lambda e, a=a, row=row: e.tensor_tensor_scan(T.d1[:, a:a + 768:3], T.st[:, 256:512], row, 0.0, OP.add, OP.max),
+              128, [("gx", i, d) for d in range(parts)] + [("st", 256)], [("flag", c, k)])
+        for k in range(2):
+            a, b = 1536 * c + 768 * k + 45, 96 * c + 48 * k
+            V(lambda e, a=a, b=b: e.tensor_tensor_scan(T.rs[:, b:b + 48], T.d0[:, b:b + 48], T.d1[:, a:a + 753:16], 0.0, OP.min, OP.max),
+              48, [("flag", c, k), ("old", c), ("bak", c, k), ("n", c), ("lim", c), "d0"], [("rs", c, k)])
 
-    def settle(t, w, rows, first, floor):
-        outs = cut(t, w, rows, first, floor, 16)
+    def settle(c, t, off):
+        merge(c, t, off)
         for half in range(2):
             a = zl[t + 1] + 16 * half
-            ts(T.smu[:, a:a + 16], outs[half][0], float(-BASE), None, OP.add, None, [outs[half][1]], [("zl", t + 1, half, 0)])
-        return outs
+            ts(T.smu[:, a:a + 16], result(c, half), UNIT, float(SL), OP.mult, OP.add, [("rs", c, half)], [("zl", t + 1, half, 0)])
 
-    def halves(a, keys):
-        return [(T.smf[:, a:a + 16], keys), (T.smf[:, a + 16:a + 32], keys)]
+    def before(c, b):
+        V(lambda e: e.tensor_copy(older(c), result(b)), 32, kres(b), [("old", c)])
 
     inverse(0)
     operands(0)
-    w01 = where(0, find(0, 1))
+    w01 = where(0, 0, find(0, 1))
     for p in range(4):
         copy(T.F[:, SL * p:SL * p + 512], T.X0[:].indirect(m4[p][0]), 512, ["X0", m4[p][1]], [("Fx", p)], True)
     V(lambda e: e.quantize_mx(T.uq[:], T.uqs[:], T.uin[:]), 150, ["uin"], ["uq"])
-    V(lambda e: e.tensor_copy(T.up[:].bitcast(dt.uint32), T.uq[:].bitcast(dt.uint32).indirect(U16)), 450, ["uq", (kU16, 0), (kU16, 1)], ["up"])
+    op({"v": (lambda e: e.tensor_copy(T.up[:].bitcast(dt.uint32), T.uq[:].bitcast(dt.uint32).indirect(U16)), (50.0, 0, 256, 0))},
+       ["uq", (kU16, 0), (kU16, 1)], ["up"])
     copy(T.ups[:], T.uqs[:].indirect(U16), 256, ["uq", (kU16, 0), (kU16, 1)], ["ups"], True)
     for b in range(4):
         V(lambda e, b=b: e.quantize_mx(T.eq[:, 128 * b:128 * b + 128], T.eqs[:, 128 * b:128 * b + 128], T.ez[:, 4 - b:516 - b]), 150, ["ez"], [("eq", b)])
@@ -468,38 +610,41 @@ def rank_program(g, core, T, topo):
     layer(0, 1)
     scores(0, 1)
     limit(0)
-    settle(0, w01, signs(0, w01), None, [(T.smf[:, lf + 48:lf + 64], [kLf]), (T.smf[:, lf + 96:lf + 112], [kLf])])
+    settle(0, 0, w01)
 
     operands(1)
     inverse(1)
-    w12, w02 = where(1, find(1, 2)), where(0, find(0, 2))
+    w12, w02 = where(3, 1, find(1, 2)), where(1, 0, find(0, 2))
     layer(1, 0)
     scores(1, 0)
-    p1 = cut(0, w02, signs(0, w02), None, (ab2, kab))[0]
+    merge(1, 0, w02)
+    before(3, 1)
     layer(1, 1)
     scores(1, 1)
     limit(1)
-    settle(1, w12, signs(1, w12), p1, halves(aa, kab))
+    settle(3, 1, w12)
 
     operands(2)
     inverse(2)
-    w0, w1, w2 = [where(t, ident(t)) for t in range(R)]
-    g1 = cut(0, w0, signs(0, w0), None, (idl, [kidl]))[0]
-    g2 = cut(1, w1, signs(1, w1), g1, (idl, [kidl]))[0]
+    w0, w1, w2 = [where(c, t, ident(t)) for c, t in ((2, 0), (4, 1), (5, 2))]
+    merge(2, 0, w0)
+    before(4, 2)
+    merge(4, 1, w1)
+    before(5, 4)
     gm, kgm, _ = small(32)
-    ts(gm, g1[0], float(-3 * BASE), None, OP.add, None, [g1[1]], [kgm])
+    affine(gm, result(2), -1.0, 0.0, kres(2), [kgm])
     V(lambda e: e.quantize_mx(T.vq[:], T.vqs[:], T.vin[:]), 150, ["vin"], ["vq"])
     layer(2, 0)
     scores(2, 0)
     layer(2, 1)
     scores(2, 1)
     limit(2)
-    fb, kfb, fa = small(32)
-    ts(fb, gm, nlim, float(3 * BASE), OP.min, OP.add, [kgm, knlim], [kfb])
-    offs = settle(2, w2, signs(2, w2), g2, halves(fa, [kfb]))
+    ts(backed(5), gm, rk[2][0], -1.0, OP.max, OP.mult, [kgm, rk[2][1]], [("bak", 5, 0), ("bak", 5, 1)])
+    settle(5, 2, w2)
 
     def store(q, sem, pairs, r, w):
-        op({q: (lambda q: dmas(q, sem, pairs, r, w), 60.0 * len(pairs))}, r, w, 2500.0, "dma")
+        op({q: (lambda q: dmas(q, sem, pairs, r, w), (60.0 * len(pairs), 0, 0, 0))}, r, w, "dma")
+        ops[-1]["busy"] = 320.0 if len(pairs) == 1 else 150.0
 
     for c in range(4):
         lo, hi = 128 * c, 128 * c + 128
@@ -507,26 +652,23 @@ def rank_program(g, core, T, topo):
             (win, wk), (off, ko) = window(3, p), zoff(3, c // 2, p, c % 2)
             copy(T.Tt[:, 512 * c + p:512 * c + 512:4], win.indirect(off), 128, wk + [ko], [("T", c, p)], True)
         V(lambda e, lo=lo, hi=hi: e.quantize_mx(T.oq[:, lo:hi], T.oqs[:, lo:hi], T.Tt[:, 4 * lo:4 * hi]), 150, [("T", c, p) for p in range(4)], [("oq", c)])
-        ops[-1]["early"] = EARLY * (3 - c)
         mm(4 + c, T.vq[:], T.vqs[:], T.oq[:, lo:hi], T.oqs[:, lo:hi], ["vq", ("oq", c)])
         copy(T.yo[:, lo:hi], bank(4 + c), 128, [("bk", 4 + c)], [("yo", c)], False)
         store("y", "so%d" % c, [(T.oc[:, 4 * lo:4 * hi], T.oq[:, lo:hi].bitcast(dt.uint8))], [("oq", c)], [("oc", c)])
         store("y", "sy%d" % c, [(T.y[:, lo:hi], T.yo[:, lo:hi])], [("yo", c)], [("y", c)])
     store("s", "sos", [(T.osc[4 * k:4 * k + 4, :], T.oqs[32 * k:32 * k + 4, :]) for k in range(4)], [("oq", c) for c in range(4)], ["osc"])
-    pl, kpl, pa = small(32)
+    z1, kz1, _ = small(32)
+    z2, kz2, _ = small(32)
+    z3, kz3, _ = small(32)
+    pl, kpl, _ = small(32)
     ot, kot, oa = small(32)
     V(lambda e: e.tensor_copy(mf, L[:, 0:32]), 32, ["lists"], [kmf])
-    for half in range(2):
-        o, ko, _ = offs[half]
-        a, ka, _ = small(16)
-        b, kb, _ = small(16)
-        c, kc, _ = small(16)
-        ts(b, o, float(-BASE), None, OP.add, None, [ko], [kb])
-        ts(a, b, 512.0, None, OP.is_ge, None, [kb], [ka])
-        tt(c, a, b, OP.mult, [kb, ka], [kc])
-        tt(T.smf[:, pa + 16 * half:pa + 16 * half + 16], c, T.smf[:, amf + 16 * half:amf + 16 * half + 16], OP.max, [kc, kmf], [(kpl, half)])
-    V(lambda e: e.transpose(ot, pl), 32, [(kpl, 0), (kpl, 1)], [kot])
-    store("y", "som", [(T.om[q:q + 1, :], T.smf[32 * (q // 2):32 * (q // 2) + 32, oa + 16 * (q % 2):oa + 16 * (q % 2) + 16]) for q in range(8)], [kot], ["om"])
+    affine(z1, result(5), 4096.0 * UNIT, 4096.0 * (SL - 511.5), kres(5), [kz1])
+    affine(z2, result(5), UNIT, float(SL), kres(5), [kz2])
+    tt(z3, z1, z2, OP.min, [kz1, kz2], [kz3])
+    tt(pl, z3, mf, OP.max, [kz3, kmf], [kpl])
+    V(lambda e: e.transpose(ot, pl), 32, [kpl], [kot])
+    store("y", "som", [(T.om[k:8:2, :], T.smf[:, oa + 16 * k:oa + 16 * k + 16]) for k in range(2)], [kot], ["om"])
 
     if "order" not in PLAN:
         PLAN["order"] = make_plan(ops, ready)

@@ -36,10 +36,10 @@ SCRATCH = {
     "jr1": ("sbuf", [128, 256], "bfloat16"),
     "Dd": ("sbuf", [128, 1536], "bfloat16"),
     "sgw": ("sbuf", [128, 3 * 272], "bfloat16"),
-    "sg1": ("sbuf", [128, 3 * 256], "bfloat16"),
+    "val": ("sbuf", [128, 272], "bfloat16"),
     "sg2": ("sbuf", [128, 3 * 256], "bfloat16"),
     "gx": ("sbuf", [128, 256 * 24], "bfloat16"),
-    "gy": ("sbuf", [128, 256 * 14], HALF),
+    "gy": ("sbuf", [128, 256 * 20], HALF),
     "d1": ("sbuf", [128, 12 * 768 + 64], HALF),
     "d0": ("sbuf", [128, 6 * 96], "float32"),
     "rs": ("sbuf", [128, 6 * 96], "float32"),
@@ -350,7 +350,8 @@ def rank_program(g, core, T, topo):
     V(lambda e: e.memset(zero, 0.0), 32, w=[kzero])
     for t in range(R):
         fill(T.Dd[:, 512 * t:512 * t + 512], 0, 512, 256, "D%d" % t)
-        V(lambda e, t=t: e.memset(T.sgw[:, 272 * t:272 * t + 1], 0.0), 1, w=[("pad", t)])
+        V(lambda e, t=t: e.memset(T.sgw[:, 272 * t:272 * t + 1], -1.0), 1, w=[("pad", t)])
+    V(lambda e: e.memset(T.val[:, 0:1], -256.0), 1, w=[("pad", R)])
     V(lambda e: e.memset(eps, 1e-37), 1, w=[keps])
     vJ, kvJ, _ = small(32, "smi")
     p15, kp15, ap15 = small(32, "smi")
@@ -372,6 +373,10 @@ def rank_program(g, core, T, topo):
     last, klast, _ = small(1)
     ts(lift, T.smi[:, ap15:ap15 + 1], 15, LIFT, OP.is_lt, OP.mult, [kp15], [klift])
     ts(last, T.smi[:, ap15:ap15 + 1], 15, 2.0, OP.is_equal, OP.subtract, [kp15], [klast])
+    half1, khalf1, _ = small(1)
+    ts(half1, last, 0.5, None, OP.add, None, [klast], [khalf1])
+    mcol, kmcol, _ = small(1)
+    ts(mcol, lift, -1.0, float(256 - SL), OP.mult, OP.add, [klift], [kmcol])
     down = []
     for p in range(4):
         down.append(small(1))
@@ -384,7 +389,6 @@ def rank_program(g, core, T, topo):
         ts(slot[t][0], lift, -1.0, float(511 + 256 * t - SL), OP.mult, OP.add, [klift], [slot[t][1]])
     fill(T.ones[:], 1, 520, 260, "ones")
     G(lambda e: e.affine_select(T.ez[:], T.ones[:], [[-1, 520]], OP.is_equal, 0.0, 4, 4), 520, ["ones"], ["ez"])
-    idt, kidt, _ = small(32)
     f_a, kf_a, _ = small(32)
     f_b, kf_b, _ = small(32)
     fr8, kfr8, _ = small(32)
@@ -397,13 +401,11 @@ def rank_program(g, core, T, topo):
     ts(f_b, p31, 8, -8192.0, OP.is_ge, OP.mult, [kp31], [kf_b])
     tt(fr8, f_a, f_b, OP.add, [kf_a, kf_b], [kfr8])
     ts(gfr, T.smi[:, apg:apg + 1], 0.125, None, OP.mult, None, [kpg], [kgfr])
-    tt(idt, p15, kI, OP.add, [kp15, kkI], [kidt])
     V(lambda e: e.tensor_copy(T.smu[:, u0:u0 + 8], T.smi[:, akI:akI + 8]), 8, [kkI], [(kU16, 0)])
     ts(T.smu[:, u0 + 8:u0 + 16], T.smi[:, ap7:ap7 + 8], 16, None, OP.mult, None, [kp7], [(kU16, 1)])
 
     L16, kL16, l0 = small(128, "smu")
     D16, kD16, d0 = small(48, "smu")
-    mf, kmf, amf = small(32)
     V(lambda e: e.tensor_copy(T.smu[:, l0:l0 + 32], L[:, 0:32]), 32, ["lists"], [(kL16, 0)])
     V(lambda e: e.tensor_copy(T.smu[:, l0 + 32:l0 + 128], L[:, 32:128]), 96, ["lists"], [(kL16, 1)])
 
@@ -429,10 +431,6 @@ def rank_program(g, core, T, topo):
         for p in range(4):
             a = zl0 + 64 * half + 16 * p
             ts(T.smu[:, a:a + 16], y, 4.0, down[p][0], OP.mult, OP.add, ky + [down[p][1]], [("zl", 0, half, p)])
-    m4 = []
-    for p in range(4):
-        m4.append(small(32, "smu"))
-        ts(m4[p][0], L[:, 0:32], 4, p, OP.mult, OP.add, ["lists"], [m4[p][1]])
 
     def zoff(t, half, p, k):
         a = zl[t] + 16 * half + 8 * k if t else zl0 + 64 * half + 16 * p + 8 * k
@@ -450,15 +448,14 @@ def rank_program(g, core, T, topo):
         def call(q):
             dst = T.cores[rank ^ STEP[t]]
             rid, pid = topo.addr(dst)[:2]
-            eng = topo.engines(core, dst)
+            every, n = topo.mask(core, dst), 2 * len(topo.engines(core, dst))
             name = "arr%d%d" % (t, h)
             gate("g", [("qz", t, h)], [])
-            m0, m1 = sum(1 << e for e in eng[0::2]), sum(1 << e for e in eng[1::2])
-            g.remote_dma(T["lz%d" % t][:, lo:hi].bitcast(dt.uint8), qz[:, lo:hi].bitcast(dt.uint8), T.sem[name], T.sem.sent, pid, rid, m0)
-            g.remote_dma(T["lzs%d" % t][:, lo:hi], qs[:, lo:hi], T.sem[name], T.sem.sent, pid, rid, m1)
-            count["sent"] = count.get("sent", 0) + len(eng)
-            count[name] = len(eng)
-            writer[("lz", t, h)] = (name, len(eng), {})
+            g.remote_dma(T["lz%d" % t][:, lo:hi].bitcast(dt.uint8), qz[:, lo:hi].bitcast(dt.uint8), T.sem[name], T.sem.sent, pid, rid, every)
+            g.remote_dma(T["lzs%d" % t][:, lo:hi], qs[:, lo:hi], T.sem[name], T.sem.sent, pid, rid, every)
+            count["sent"] = count.get("sent", 0) + n
+            count[name] = n
+            writer[("lz", t, h)] = (name, n, {})
         op({"g": (call, (300.0 + (800.0 if t + h == 0 else 0.0), 0, 0, 0))}, [("qz", t, h)], [("lz", t, h)], "send")
 
     def operands(t):
@@ -501,26 +498,26 @@ def rank_program(g, core, T, topo):
     def scores(t, h):
         lo, hi = 128 * h, 128 * h + 128
         q, s = T["qh%d" % t][:, lo:hi], T["qhs%d" % t][:, lo:hi]
-        bs, bd = ((4, 5, 6), (7, 4, 5, 6)) if h == 0 else ((7, 4, 5), (0, 1, 2, 3))
-        for k, i in enumerate((1, 0, 0)):
-            mm(bs[k], T.up[:, 128 * i:128 * i + 128], T.ups[:, 128 * i:128 * i + 128], q, s, ["up", "ups", ("qh", t, h)])
-        for k, (name, sm) in ((0, ("sg2", s2[t][h])), (2, ("sg1", s1[t][h]))):
-            out = T[name][:, 256 * t + lo:256 * t + hi]
+        bs, bd = ((4, 5), (6, 7, 4, 5)) if h == 0 else ((0, 1), (2, 3, 6, 7))
+        for k in range(2):
+            mm(bs[k], T.up[:, 128 * k:128 * k + 128], T.ups[:, 128 * k:128 * k + 128], q, s, ["up", "ups", ("qh", t, h)])
+        for k, name, out, sm in ((0, "sgw", T.sgw[:, 272 * t + 1 + lo:272 * t + 1 + hi], s1[t][h]), (1, "sg2", T.sg2[:, 256 * t + lo:256 * t + hi], s2[t][h])):
             op({"s": (lambda e, k=k, out=out, sm=sm: e.activation(out, bank(bs[k]), AF.Sign, bias=eps, accum_out=sm[0]), (20.0, 128, 0, 0))},
                [("bk", bs[k]), keps], [(name, t, h), sm[1]])
-        ts(T.sgw[:, 272 * t + 1 + lo:272 * t + 1 + hi], bank(bs[1]), 0.0, None, OP.is_ge, None, [("bk", bs[1])], [("sgw", t, h)], 128)
         for b in range(4):
             mm(bd[b], T.eq[:, 128 * b:128 * b + 128], T.eqs[:, 128 * b:128 * b + 128], q, s, [("eq", b), ("qh", t, h)])
             a = SL * b + 512 + 256 * t + lo
             copy(T.F[:, a:a + 128], bank(bd[b]), 128, [("bk", bd[b])], [("Fn", t, h, b)], False)
 
-    def older(c, n=32, k=0):
-        a = 1536 * c + 768 * k + 61
+    def flags(c):
+        return T.d1[:, 1536 * c + 45:1536 * c + 1534:48]
+
+    def older(c, n=32):
+        a = 1536 * c + 61
         return T.d1[:, a:a + 48 * n - 47:48]
 
-    def backed(c, n=32, k=0):
-        a = 1536 * c + 768 * k + 77
-        return T.d1[:, a:a + 48 * n - 47:48]
+    def backed(c):
+        return T.d1[:, 1536 * c + 77:1536 * c + 1566:48]
 
     def result(c, k=None):
         return T.rs[:, 96 * c + 2:96 * c + 96:3] if k is None else T.rs[:, 96 * c + 48 * k + 2:96 * c + 48 * k + 48:3]
@@ -529,18 +526,22 @@ def rank_program(g, core, T, topo):
         return [("rs", c, 0), ("rs", c, 1)]
 
     V(lambda e: e.tensor_copy(older(0, 96), low), 96, [klow], [("old", 0), ("old", 1), ("old", 2)])
-    for c, t in ((0, 1), (1, 2), (3, 2)):
-        for k in range(2):
-            a = 32 + 48 * k + 16 * t
-            ts(backed(c, 16, k), L[:, a:a + 16], float(-SL), 1.0 / UNIT, OP.add, OP.mult, ["lists"], [("bak", c, k)])
+    for t, cs in ((1, (0,)), (2, (1, 3))):
+        y, ky = scan([pick(T.m0r[:], km0r, *l) for l in (la16(t), lb16(t))])
+        for c in cs:
+            ts(backed(c), y, mcol, 1.0 / UNIT, OP.add, OP.mult, ky + [kmcol], [("bak", c, 0), ("bak", c, 1)])
     for c in (2, 4):
-        ts(backed(c), idt, float(-SL), 1.0 / UNIT, OP.add, OP.mult, [kidt], [("bak", c, 0), ("bak", c, 1)])
+        ts(backed(c), L[:, 0:32], float(-SL), 1.0 / UNIT, OP.add, OP.mult, ["lists"], [("bak", c, 0), ("bak", c, 1)])
+
+    def new(c, t, y, ky):
+        ts(T.d0[:, 96 * c + 1:96 * c + 96:3], y, slot[t][0], 1.0 / UNIT, OP.add, OP.mult, ky + [slot[t][1], "d0"], [("n", c)])
 
     def where(c, t, rows):
         y, ky = scan(rows)
         o, ko, oa = small(32, "smu")
         ts(o, y, mlift, None, OP.add, None, ky + [kmlift], [ko])
-        ts(T.d0[:, 96 * c + 1:96 * c + 96:3], y, slot[t][0], 1.0 / UNIT, OP.add, OP.mult, ky + [slot[t][1], "d0"], [("n", c)])
+        if c is not None:
+            new(c, t, y, ky)
         return oa, ko
 
     def ident(t):
@@ -562,10 +563,15 @@ def rank_program(g, core, T, topo):
         op({"s": (lambda e: e.activation(c8, T.smf[:, ka:ka + 12], AF.Sign, bias=own, scale=-1.0, accum_out=rk[t][0]), (20.0, 64, 0, 0))},
            [kkt, kown], [kc8, rk[t][1]])
 
+    def limits(c, t):
+        out, col = T.d0[:, 96 * c + 2:96 * c + 96:3], rk[t][0]
+        op({"v": (lambda e: e.tensor_scalar(out, zero, col, None, OP.add), (0.0, 64, 0, 0)),
+            "s": (lambda e: e.activation(out, zero, AF.Identity, bias=col), (0.0, 64, 0, 0))}, [kzero, rk[t][1], "d0"], [("lim", c)])
+
     def merge(c, t, off):
         oa, ko = off
-        win, wk = T.sgw[:, 272 * t:272 * t + 257], [("pad", t), ("sgw", t, 0), ("sgw", t, 1), klast, ko]
-        ts(T.d0[:, 96 * c + 2:96 * c + 96:3], zero, rk[t][0], None, OP.add, None, [kzero, rk[t][1], "d0"], [("lim", c)])
+        win, wk = T.sgw[:, 272 * t:272 * t + 257], [("pad", t), ("sgw", t, 0), ("sgw", t, 1), khalf1, ko]
+        limits(c, t)
         parts = 2 if c in SPLIT else 1
         w = 256 // parts
         for k in range(2):
@@ -575,8 +581,8 @@ def rank_program(g, core, T, topo):
             for d in range(parts):
                 o = oa + 16 * k + 8 * d
                 out, in_ = T.gx[:, 256 * i + w * d:256 * i + w * d + w], win.indirect(T.smu[:, o:o + 16 // parts])
-                op({"v": (lambda e, out=out, in_=in_: e.tensor_scalar(out, in_, last, None, OP.add), (50.0, 0, w, 0)),
-                    "s": (lambda e, out=out, in_=in_: e.activation(out, in_, AF.Identity, bias=last), (65.0, 0, w, 0))}, wk, [("gx", i, d)])
+                op({"v": (lambda e, out=out, in_=in_: e.tensor_scalar(out, in_, 0.5, half1, OP.mult, OP.add), (50.0, 0, w, 0)),
+                    "s": (lambda e, out=out, in_=in_: e.activation(out, in_, AF.Identity, bias=half1, scale=0.5), (65.0, 0, w, 0))}, wk, [("gx", i, d)])
             a = 1536 * c + 768 * k
             V(lambda e, a=a, row=row: e.tensor_tensor_scan(T.d1[:, a:a + 768:3], T.st[:, 256:512], row, 0.0, OP.add, OP.max),
               128, [("gx", i, d) for d in range(parts)] + [("st", 256)], [("flag", c, k)])
@@ -584,6 +590,15 @@ def rank_program(g, core, T, topo):
             a, b = 1536 * c + 768 * k + 45, 96 * c + 48 * k
             V(lambda e, a=a, b=b: e.tensor_tensor_scan(T.rs[:, b:b + 48], T.d0[:, b:b + 48], T.d1[:, a:a + 753:16], 0.0, OP.min, OP.max),
               48, [("flag", c, k), ("old", c), ("bak", c, k), ("n", c), ("lim", c), "d0"], [("rs", c, k)])
+
+    def merge_rows(c, t, rows):
+        y, ky = scan(rows)
+        limits(c, t)
+        new(c, t, y, ky)
+        ts(flags(c), y, mlift, None, OP.add, None, ky + [kmlift], [("flag", c, 0), ("flag", c, 1)])
+        a, b = 1536 * c + 45, 96 * c
+        V(lambda e: e.tensor_tensor_scan(T.rs[:, b:b + 96], T.d0[:, b:b + 96], T.d1[:, a:a + 1521:16], 0.0, OP.min, OP.max),
+          96, [("flag", c, 0), ("flag", c, 1), ("old", c), ("bak", c, 0), ("bak", c, 1), ("n", c), ("lim", c), "d0"], kres(c))
 
     def settle(c, t, off):
         merge(c, t, off)
@@ -598,7 +613,9 @@ def rank_program(g, core, T, topo):
     operands(0)
     w01 = where(0, 0, find(0, 1))
     for p in range(4):
-        copy(T.F[:, SL * p:SL * p + 512], T.X0[:].indirect(m4[p][0]), 512, ["X0", m4[p][1]], [("Fx", p)], True)
+        out, in_ = T.F[:, SL * p:SL * p + 512], T.X0[:, p:2048:4]
+        op({"g": (lambda e, out=out, in_=in_: e.affine_select(out, in_, [[0, 512]], OP.is_equal, 0.0, 0, 0), (170.0, 1024, 0, 0)),
+            "v": (lambda e, out=out, in_=in_: e.tensor_copy(out, in_), (0.0, 256, 0, 0))}, ["X0"], [("Fx", p)])
     V(lambda e: e.quantize_mx(T.uq[:], T.uqs[:], T.uin[:]), 150, ["uin"], ["uq"])
     op({"v": (lambda e: e.tensor_copy(T.up[:].bitcast(dt.uint32), T.uq[:].bitcast(dt.uint32).indirect(U16)), (50.0, 0, 256, 0))},
        ["uq", (kU16, 0), (kU16, 1)], ["up"])
@@ -614,10 +631,13 @@ def rank_program(g, core, T, topo):
 
     operands(1)
     inverse(1)
-    w12, w02 = where(3, 1, find(1, 2)), where(1, 0, find(0, 2))
+    w12, w0 = where(3, 1, find(1, 2)), where(None, 0, ident(0))
     layer(1, 0)
     scores(1, 0)
-    merge(1, 0, w02)
+    tt(T.val[:, 1:257], T.sgw[:, 1:257], T.jr1[:], OP.mult, [("sgw", 0, 0), ("sgw", 0, 1), "jr1"], ["val"], 256)
+    regs = [pick(T.val[:, 0:257], ["val", ("pad", R)], T.smu[:, w0[0] + 16 * k:w0[0] + 16 * k + 16], w0[1]) for k in range(2)]
+    g0 = 256 * regs[0][1][0][1]
+    merge_rows(1, 0, [pick(T.gx[:, g0:g0 + 512], regs[0][1] + regs[1][1], *l) for l in (la16(2), lb16(2))])
     before(3, 1)
     layer(1, 1)
     scores(1, 1)
@@ -626,8 +646,8 @@ def rank_program(g, core, T, topo):
 
     operands(2)
     inverse(2)
-    w0, w1, w2 = [where(c, t, ident(t)) for c, t in ((2, 0), (4, 1), (5, 2))]
-    merge(2, 0, w0)
+    w1, w2 = [where(c, t, ident(t)) for c, t in ((4, 1), (5, 2))]
+    merge_rows(2, 0, regs)
     before(4, 2)
     merge(4, 1, w1)
     before(5, 4)
@@ -657,16 +677,9 @@ def rank_program(g, core, T, topo):
         store("y", "so%d" % c, [(T.oc[:, 4 * lo:4 * hi], T.oq[:, lo:hi].bitcast(dt.uint8))], [("oq", c)], [("oc", c)])
         store("y", "sy%d" % c, [(T.y[:, lo:hi], T.yo[:, lo:hi])], [("yo", c)], [("y", c)])
     store("s", "sos", [(T.osc[4 * k:4 * k + 4, :], T.oqs[32 * k:32 * k + 4, :]) for k in range(4)], [("oq", c) for c in range(4)], ["osc"])
-    z1, kz1, _ = small(32)
-    z2, kz2, _ = small(32)
-    z3, kz3, _ = small(32)
     pl, kpl, _ = small(32)
     ot, kot, oa = small(32)
-    V(lambda e: e.tensor_copy(mf, L[:, 0:32]), 32, ["lists"], [kmf])
-    affine(z1, result(5), 4096.0 * UNIT, 4096.0 * (SL - 511.5), kres(5), [kz1])
-    affine(z2, result(5), UNIT, float(SL), kres(5), [kz2])
-    tt(z3, z1, z2, OP.min, [kz1, kz2], [kz3])
-    tt(pl, z3, mf, OP.max, [kz3, kmf], [kpl])
+    affine(pl, result(5), UNIT, float(SL), kres(5), [kpl])
     V(lambda e: e.transpose(ot, pl), 32, [kpl], [kot])
     store("y", "som", [(T.om[k:8:2, :], T.smf[:, oa + 16 * k:oa + 16 * k + 16]) for k in range(2)], [kot], ["om"])
 

import math
import numpy as np
from concourse.bass import DstId, RemoteDMATransfer
from concourse.mybir import dt, AluOpType, AxisListType, ActivationFunctionType

OP = AluOpType
AF = ActivationFunctionType
R = 3
STEP = [1, 2, 4]
LIFT = 1024
SL = 1280
UNIT = 2048.0
HALF = "float16"
SPLIT = (0, 3, 5)
COSTS = [(1.0, 160.0, 1.5, 3.5, 1900.0, 140.0), (1.0, 280.0, 1.3, 3.0, 2200.0, 190.0), (1.2, 120.0, 1.8, 4.5, 1800.0, 170.0),
         (0.85, 220.0, 1.5, 3.5, 2500.0, 220.0)]
TRIES, HEAT = 16000, 12.0
PLAN = {}

SCRATCH = {
    "Lst": ("sbuf", [128, 176], "int32"),
    "X0": ("sbuf", [128, 2048], "bfloat16"),
    "F": ("sbuf", [128, 4 * SL], "bfloat16"),
    "Ag": ("sbuf", [128, 3072], "bfloat16"),
    "Z": ("sbuf", [128, 3072], "bfloat16"),
    "Hb": ("sbuf", [128, 3072], "bfloat16"),
    "Tt": ("sbuf", [128, 2048], "bfloat16"),
    "uin": ("sbuf", [128, 512], "bfloat16"),
    "vin": ("sbuf", [128, 512], "bfloat16"),
    "ones": ("sbuf", [128, 520], "bfloat16"),
    "ez": ("sbuf", [128, 520], "bfloat16"),
    "sw": ("sbuf", [128, 32], "bfloat16"),
    "st": ("sbuf", [128, 512], "bfloat16"),
    "idw": ("sbuf", [128, 512], "bfloat16"),
    "m0r": ("sbuf", [128, 512], "bfloat16"),
    "jr1": ("sbuf", [128, 256], "bfloat16"),
    "Dd": ("sbuf", [128, 1536], "bfloat16"),
    "sgw": ("sbuf", [128, 3 * 272], "bfloat16"),
    "val": ("sbuf", [128, 272], "bfloat16"),
    "sg2": ("sbuf", [128, 3 * 256], "bfloat16"),
    "gx": ("sbuf", [128, 256 * 24], "bfloat16"),
    "gy": ("sbuf", [128, 256 * 20], HALF),
    "d1": ("sbuf", [128, 12 * 768 + 64], HALF),
    "d0": ("sbuf", [128, 6 * 96], "float32"),
    "rs": ("sbuf", [128, 6 * 96], "float32"),
    "smi": ("sbuf", [128, 320], "int32"),
    "smf": ("sbuf", [128, 2560], "float32"),
    "smu": ("sbuf", [128, 1280], "uint16"),
    "yo": ("sbuf", [128, 512], "float32"),
    "ps": ("psum", [128, 4096], "float32"),
    "wq": ("sbuf", [128, 512], "float8_e4m3fn_x4"), "wqs": ("sbuf", [128, 512], "uint8"),
    "uq": ("sbuf", [128, 128], "float8_e4m3fn_x4"), "uqs": ("sbuf", [128, 128], "uint8"),
    "up": ("sbuf", [128, 256], "float8_e4m3fn_x4"), "ups": ("sbuf", [128, 256], "uint8"),
    "vq": ("sbuf", [128, 128], "float8_e4m3fn_x4"), "vqs": ("sbuf", [128, 128], "uint8"),
    "eq": ("sbuf", [128, 512], "float8_e4m3fn_x4"), "eqs": ("sbuf", [128, 512], "uint8"),
    "oq": ("sbuf", [128, 512], "float8_e4m3fn_x4"), "oqs": ("sbuf", [128, 512], "uint8"),
}
for _t in range(R):
    for _n in ("qz", "lz", "qh"):
        SCRATCH["%s%d" % (_n, _t)] = ("sbuf", [128, 256], "float8_e4m3fn_x4")
        SCRATCH["%ss%d" % (_n, _t)] = ("sbuf", [128, 256], "uint8")
ENG = {"v": "ve", "s": "ac", "t": "pe", "g": "gp"}
LOADS = ["lm", "lx", "ll", "lu", "lw", "lv"]
STORES = ["so0", "so1", "so2", "so3", "sy0", "sy1", "sy2", "sy3", "som", "sos"]
SEMAPHORES = ["ve", "ac", "pe", "gp", "sent"] + ["arr%d%d" % (t, h) for t in range(R) for h in range(2)] + LOADS + STORES
MAIN = ("zl", "Fn", "A", "Z", "qz", "lz", "H", "qh", "flag", "lim", "T", "oq", "yo")


def price(o, q, c):
    fix, cyc, gat, sca = o["q"][q][1]
    return c[5] if q == "t" else fix + c[0] * (cyc + c[2] * gat + c[3] * sca)


def make_plan(ops, ready):
    n = len(ops)
    pred, succ, wrote, read = [[] for _ in ops], [[] for _ in ops], {}, {}
    for i, o in enumerate(ops):
        p = {}
        for k in o["w"]:
            for j in read.get(k, []) + ([wrote[k]] if k in wrote else []):
                p[j] = False
        for k in o["r"]:
            if k in wrote:
                p[wrote[k]] = True
        for k in o["r"]:
            read.setdefault(k, []).append(i)
        for k in o["w"]:
            wrote[k], read[k] = i, []
        p.pop(i, None)
        pred[i] = sorted(p.items())
        for j in p:
            succ[j].append(i)
    first = [max([ready.get(k, 0.0) for k in o["r"]] + [0.0]) for o in ops]
    lag = [[c[4] if o["kind"] == "send" else 1700.0 if o["kind"] == "dma" else 0.0 for o in ops] for c in COSTS]
    cost = [[{q: price(o, q, c) for q in o["q"]} for o in ops] for c in COSTS]
    busy = [o.get("busy", 0.0) for o in ops]
    weight = [0.3 / n if o["w"][0][0] in MAIN else 0.0 for o in ops]
    rank = [0.0] * n
    for i in range(n - 1, -1, -1):
        rank[i] = min(cost[0][i].values()) + lag[0][i] + max([COSTS[0][1] + rank[j] for j in succ[i]] + [0.0])

    def greedy():
        free, fin, start, where, left = {}, [0.0] * n, [0.0] * n, [""] * n, [len(p) for p in pred]
        cand = [i for i in range(n) if not left[i]]
        for _ in range(n):
            best = []
            for i in cand:
                opt = []
                for q in ops[i]["q"]:
                    t = max(first[i], free.get(q, 0.0))
                    for j, raw in pred[i]:
                        t = max(t, fin[j] + COSTS[0][1] if raw or where[j] != q else start[j])
                    opt.append((t + cost[0][i][q] + (60.0 if q == "v" and len(ops[i]["q"]) > 1 else 0.0), t, q))
                best.append((min(opt), i))
            soon = min(b[0][1] for b in best)
            (_, t, q), i = max((b for b in best if b[0][1] <= soon + 120.0), key=lambda b: (rank[b[1]], -b[1]))
            start[i], where[i] = t, q
            free[q] = t + cost[0][i][q]
            fin[i] = free[q] + lag[0][i]
            cand.remove(i)
            for j in succ[i]:
                left[j] -= 1
                if not left[j]:
                    cand.append(j)
        return sorted(range(n), key=lambda i: (start[i], i)), where

    free, start, fin = [None] * len(COSTS), [None] * len(COSTS), [None] * len(COSTS)

    def span(seq, where, a):
        total = 0.0
        for k, c in enumerate(COSTS):
            wake, ck, lk, snap, sk, fk = c[1], cost[k], lag[k], free[k][:a + 1], start[k], fin[k]
            f5, end, late = snap[a]
            f5 = dict(f5)
            for i in seq[a:]:
                q = where[i]
                t = first[i]
                f = f5[q]
                if f > t:
                    t = f
                for j, raw in pred[i]:
                    f = fk[j] + wake if raw or where[j] != q else sk[j]
                    if f > t:
                        t = f
                sk[i] = t
                f = t + ck[i][q]
                f5[q] = f
                if busy[i]:
                    f = max(f + lk[i], f5["e"]) + busy[i]
                    f5["e"] = f
                    f += 500.0
                else:
                    f += lk[i]
                fk[i] = f
                late += f * weight[i]
                if f > end:
                    end = f
                snap.append((dict(f5), end, late))
            free[k] = snap
            total += end + late
        return total

    for k in range(len(COSTS)):
        free[k], start[k], fin[k] = [({"v": 0.0, "s": 0.0, "t": 0.0, "g": 0.0, "y": 0.0, "e": 0.0}, 0.0, 0.0)], [0.0] * n, [0.0] * n
    seq, where = greedy()
    seed = [12345]

    def draw(m):
        seed[0] = (seed[0] * 1103515245 + 12345) % 2147483648
        return (seed[0] >> 8) % m

    now = span(seq, where, 0)
    kept = (now, list(seq), list(where))
    pos = [0] * n
    for k, i in enumerate(seq):
        pos[i] = k
    both = [i for i in range(n) if len(ops[i]["q"]) > 1]
    for it in range(TRIES):
        heat = HEAT * (1.0 - it / TRIES) + 0.1
        flip = draw(6) == 0
        i = both[draw(len(both))] if flip else draw(n)
        a = b = pos[i]
        if not flip:
            lo = max([pos[j] for j, _ in pred[i]] + [-1]) + 1
            hi = min([pos[j] for j in succ[i]] + [n]) - 1
            if hi <= lo:
                continue
            if draw(3):
                d = 1 if draw(2) else -1
                b = a + d
                while lo <= b <= hi and where[seq[b]] != where[i]:
                    b += d
            else:
                b = max(lo, a - 60) + draw(min(hi, a + 60) - max(lo, a - 60) + 1)
            if b == a or b < lo or b > hi:
                continue
        old = (where[i], list(free), [list(s) for s in start], [list(s) for s in fin])
        if flip:
            where[i] = [q for q in sorted(ops[i]["q"]) if q != where[i]][0]
        else:
            seq.insert(b, seq.pop(a))
        new = span(seq, where, min(a, b))
        if new <= now or draw(10000) < 10000 * math.exp((now - new) / heat):
            now = new
            for k in range(min(a, b), max(a, b) + 1):
                pos[seq[k]] = k
            if now < kept[0]:
                kept = (now, list(seq), list(where))
        else:
            where[i] = old[0]
            seq.insert(a, seq.pop(b))
            for k in range(len(COSTS)):
                free[k], start[k], fin[k] = old[1][k], old[2][k], old[3][k]
    return [(i, kept[2][i]) for i in kept[1]]


def rank_program(g, core, T, topo):
    rank = T.rank_of(core)
    if rank is None:
        return
    queue = {"v": g.vector, "s": g.scalar, "t": g.tensor, "g": g, "y": g.sync}
    count = {}
    known = {q: {} for q in queue}
    writer, readers = {}, {}
    ops = []

    def need(q, ev):
        sem, val, snap = ev
        k = known[q]
        if k.get(sem, 0) < val:
            queue[q].wait_ge(T.sem[sem], val)
            k[sem] = val
        for s in snap:
            if k.get(s, 0) < snap[s]:
                k[s] = snap[s]

    def gate(q, r, w):
        own = ENG.get(q)
        evs = [writer[k] for k in r]
        for k in w:
            if k in writer and writer[k][0] != own:
                evs.append(writer[k])
            evs += [e for e in readers.get(k, {}).values() if e[0] != own]
        for e in sorted(evs, key=lambda e: -e[1]):
            need(q, e)

    def note(ev, r, w):
        for k in w:
            writer[k] = ev
            readers[k] = {}
        for k in r:
            readers.setdefault(k, {})[ev[0]] = ev

    def dmas(q, sem, pairs, r=(), w=()):
        gate(q, r, w)
        for out, in_ in pairs:
            queue[q].dma_start(out, in_).then_inc(T.sem[sem], 16)
            count[sem] = count.get(sem, 0) + 16
        note((sem, count[sem], dict(known[q])), r, w)

    def emit(o, q):
        call = o["q"][q][0]
        if o["kind"] != "call":
            call(q)
            return
        gate(q, o["r"], o["w"])
        sem = ENG[q]
        call(queue[q]).then_inc(T.sem[sem], 1)
        count[sem] = count.get(sem, 0) + 1
        note((sem, count[sem], dict(known[q])), o["r"], o["w"])

    def op(qs, r, w, kind="call"):
        ops.append({"q": qs, "r": list(r), "w": list(w), "kind": kind})

    used = {"smf": 0, "smu": 0, "smi": 0, "gx": 0, "gy": 0}

    def small(n, buf="smf"):
        a = -(-used[buf] // (32 if n > 8 else 8)) * (32 if n > 8 else 8)
        used[buf] = a + n
        return T[buf][:, a:a + n], (buf, a), a

    def V(call, n, r=(), w=()):
        op({"v": (call, (0.0, max(64, n), 0, 0))}, r, w)

    def G(call, n, r=(), w=()):
        op({"g": (call, (150.0, 2 * n, 0, 0))}, r, w)

    def ts(out, in0, s1, s2, op0, op1, r, w, n=32):
        if op1 is None:
            V(lambda e: e.tensor_scalar(out, in0, s1, s2, op0), n, r, w)
        else:
            V(lambda e: e.tensor_scalar(out, in0, s1, s2, op0, op1), n, r, w)

    def tt(out, a, b, o, r, w, n=64):
        V(lambda e: e.tensor_tensor(out, a, b, o), n, r, w)

    def copy(out, in_, n, r, w, gather):
        c = ((50.0, 0, n, 0), (65.0, 0, n, 0)) if gather else ((0.0, max(64, n), 0, 0), (0.0, max(64, n), 0, 0))
        op({"v": (lambda e: e.tensor_copy(out, in_), c[0]), "s": (lambda e: e.activation(out, in_, AF.Copy), c[1])}, r, w)

    def affine(out, in_, scale, bias, r, w, n=32):
        op({"v": (lambda e: e.tensor_scalar(out, in_, scale, bias, OP.mult, OP.add), (0.0, max(64, n), 0, 0)),
            "s": (lambda e: e.activation(out, in_, AF.Copy, bias=bias, scale=scale), (0.0, max(64, n), 0, 0))}, r, w)

    def fill(out, v, n, cycles, key):
        op({"v": (lambda e: e.memset(out, float(v)), (0.0, cycles, 0, 0)),
            "g": (lambda e: e.iota(out, [[0, n]], v, 0, allow_small_or_imprecise_dtypes=True), (150.0, 2 * n, 0, 0))}, [], [key])

    def pick(win, wkeys, off, okey):
        i = used["gx"]
        used["gx"] = i + 1
        out = T.gx[:, 256 * i:256 * i + 256]
        copy(out, win.indirect(off), 256, list(wkeys) + [okey], [("gx", i)], True)
        return out, [("gx", i)]

    def scan(rows):
        first = used["gy"]
        for row, keys in rows:
            i = used["gy"]
            used["gy"] = i + 1
            V(lambda e, i=i, row=row: e.tensor_tensor_scan(T.gy[:, 256 * i:256 * i + 256], T.st[:, 0:256], row, 0.0, OP.add, OP.max),
              128, keys + [("st", 0)], [("gy", i)])
        return T.gy[:, 256 * first + 15:256 * first + 256 * len(rows):16], [("gy", first + k) for k in range(len(rows))]

    L = T.Lst
    dmas("y", "lm", [(L[:, 0:32], T.m[:])], w=["m_"])
    dmas("s", "lm", [(L[:, 80:128], T.lb[:])], w=["lb_"])
    dmas("y", "lm", [(L[:, 32:80], T.la[:])], w=["lists"])
    writer["lists"] = ("lm", 48, {})
    dmas("s", "ll", [(L[:, 128:176], T.ld[:])], w=["ld_"])
    dmas("y", "lx", [(T.X0[:], T.x[:])], w=["X0"])
    dmas("y", "lu", [(T.uin[:], T.u[:])], w=["uin"])
    dmas("y", "lw", [(T.wq[:].bitcast(dt.uint8), T.wc[:]), (T.wqs[:], T.ws[:])], w=["wq"])
    dmas("y", "lv", [(T.vin[:], T.v[:])], w=["vin"])
    ready = {"lists": 2300.0, "ld_": 2350.0, "X0": 4600.0, "uin": 5200.0, "wq": 6800.0, "vin": 7300.0}

    vI, kvI, _ = small(32, "smi")
    pI, kpI, _ = small(32, "smi")
    kI, kkI, akI = small(32, "smi")
    G(lambda e: e.iota(vI, [[-1, 32]], 512, 1), 32, w=[kvI])
    G(lambda e: e.iota(pI, [[0, 32]], 0, 1), 32, w=[kpI])
    G(lambda e: e.iota(T.idw[:], [[1, 512]], -256, 0, allow_small_or_imprecise_dtypes=True), 512, w=["idw"])
    G(lambda e: e.iota(kI, [[16, 32]], 0, 0), 32, w=[kkI])
    G(lambda e: e.iota(T.jr1[:], [[1, 256]], 1, 0, allow_small_or_imprecise_dtypes=True), 256, w=["jr1"])
    eps, keps, _ = small(1)
    zero, kzero, _ = small(32)
    low, klow, _ = small(96)
    fill(T.d0[:], -16, 576, 576, "d0")
    V(lambda e: e.memset(low, -1.0), 96, w=[klow])
    V(lambda e: e.memset(zero, 0.0), 32, w=[kzero])
    for t in range(R):
        fill(T.Dd[:, 512 * t:512 * t + 512], 0, 512, 256, "D%d" % t)
        V(lambda e, t=t: e.memset(T.sgw[:, 272 * t:272 * t + 1], -1.0), 1, w=[("pad", t)])
    V(lambda e: e.memset(T.val[:, 0:1], -256.0), 1, w=[("pad", R)])
    V(lambda e: e.memset(eps, 1e-37), 1, w=[keps])
    vJ, kvJ, _ = small(32, "smi")
    p15, kp15, ap15 = small(32, "smi")
    p7, kp7, ap7 = small(32, "smi")
    p31, kp31, _ = small(32, "smi")
    pg, kpg, apg = small(32, "smi")
    s_a, ks_a, _ = small(32)
    s_b, ks_b, _ = small(32)
    r16, kr16, _ = small(16, "smu")
    ts(vJ, vI, 15, None, OP.bitwise_and, None, [kvI], [kvJ])
    ts(p15, pI, 15, None, OP.bitwise_and, None, [kpI], [kp15])
    ts(s_a, vJ, 15, LIFT, OP.is_equal, OP.mult, [kvJ], [ks_a])
    ts(s_b, vJ, 0, -2 * LIFT, OP.is_equal, OP.mult, [kvJ], [ks_b])
    V(lambda e: e.tensor_copy(r16, T.smi[:, ap15:ap15 + 16]), 16, [kp15], [kr16])
    tt(T.sw[:], s_a, s_b, OP.add, [ks_a, ks_b], ["sw"])
    copy(T.st[:, 0:256], T.sw[:].indirect(r16), 256, ["sw", kr16], [("st", 0)], True)
    op({"s": (lambda e: e.activation(T.st[:, 256:512], T.sw[:].indirect(r16), AF.Copy, scale=1.0 / LIFT), (65.0, 0, 256, 0))}, ["sw", kr16], [("st", 256)])
    lift, klift, _ = small(1)
    last, klast, _ = small(1)
    ts(lift, T.smi[:, ap15:ap15 + 1], 15, LIFT, OP.is_lt, OP.mult, [kp15], [klift])
    ts(last, T.smi[:, ap15:ap15 + 1], 15, 2.0, OP.is_equal, OP.subtract, [kp15], [klast])
    half1, khalf1, _ = small(1)
    ts(half1, last, 0.5, None, OP.add, None, [klast], [khalf1])
    mcol, kmcol, _ = small(1)
    ts(mcol, lift, -1.0, float(256 - SL), OP.mult, OP.add, [klift], [kmcol])
    down = []
    for p in range(4):
        down.append(small(1))
        ts(down[p][0], lift, -4.0, float(1024 + p), OP.mult, OP.add, [klift], [down[p][1]])
    mlift, kmlift, _ = small(1)
    ts(mlift, lift, -1.0, None, OP.mult, None, [klift], [kmlift])
    slot = []
    for t in range(R):
        slot.append(small(1))
        ts(slot[t][0], lift, -1.0, float(511 + 256 * t - SL), OP.mult, OP.add, [klift], [slot[t][1]])
    fill(T.ones[:], 1, 520, 260, "ones")
    G(lambda e: e.affine_select(T.ez[:], T.ones[:], [[-1, 520]], OP.is_equal, 0.0, 4, 4), 520, ["ones"], ["ez"])
    f_a, kf_a, _ = small(32)
    f_b, kf_b, _ = small(32)
    fr8, kfr8, _ = small(32)
    gfr, kgfr, _ = small(1)
    U16, kU16, u0 = small(16, "smu")
    ts(p7, pI, 7, None, OP.bitwise_and, None, [kpI], [kp7])
    ts(p31, pI, 31, None, OP.bitwise_and, None, [kpI], [kp31])
    ts(pg, pI, 4, None, OP.arith_shift_right, None, [kpI], [kpg])
    ts(f_a, p31, 0.125, None, OP.mult, None, [kp31], [kf_a])
    ts(f_b, p31, 8, -8192.0, OP.is_ge, OP.mult, [kp31], [kf_b])
    tt(fr8, f_a, f_b, OP.add, [kf_a, kf_b], [kfr8])
    ts(gfr, T.smi[:, apg:apg + 1], 0.125, None, OP.mult, None, [kpg], [kgfr])
    V(lambda e: e.tensor_copy(T.smu[:, u0:u0 + 8], T.smi[:, akI:akI + 8]), 8, [kkI], [(kU16, 0)])
    ts(T.smu[:, u0 + 8:u0 + 16], T.smi[:, ap7:ap7 + 8], 16, None, OP.mult, None, [kp7], [(kU16, 1)])

    L16, kL16, l0 = small(128, "smu")
    D16, kD16, d0 = small(48, "smu")
    V(lambda e: e.tensor_copy(T.smu[:, l0:l0 + 32], L[:, 0:32]), 32, ["lists"], [(kL16, 0)])
    V(lambda e: e.tensor_copy(T.smu[:, l0 + 32:l0 + 128], L[:, 32:128]), 96, ["lists"], [(kL16, 1)])

    def la16(t):
        return T.smu[:, l0 + 32 + 16 * t:l0 + 48 + 16 * t], (kL16, 1)

    def lb16(t):
        return T.smu[:, l0 + 80 + 16 * t:l0 + 96 + 16 * t], (kL16, 1)

    def inverse(t):
        op({"v": (lambda e: e.tensor_copy(T.Dd[:, 512 * t:512 * t + 512].indirect(T.smu[:, d0 + 16 * t:d0 + 16 * t + 16]), T.jr1[:]), (50.0, 0, 0, 256))},
           ["jr1", kD16], ["D%d" % t])

    for k in range(2):
        copy(T.m0r[:, 256 * k:256 * k + 256], T.idw[:].indirect(T.smu[:, l0 + 16 * k:l0 + 16 * k + 16]), 256, ["idw", (kL16, 0)], [("m0r", k)], True)
    km0r = [("m0r", 0), ("m0r", 1)]
    rows0 = [pick(T.m0r[:], km0r, *la16(0)), pick(T.m0r[:], km0r, *lb16(0))]
    V(lambda e: e.tensor_copy(D16, L[:, 128:176]), 48, ["ld_"], [kD16])
    zl0 = small(128, "smu")[2]
    zl = [None] + [small(32, "smu")[2] for _ in range(R)]
    for half in range(2):
        y, ky = scan([rows0[half]])
        for p in range(4):
            a = zl0 + 64 * half + 16 * p
            ts(T.smu[:, a:a + 16], y, 4.0, down[p][0], OP.mult, OP.add, ky + [down[p][1]], [("zl", 0, half, p)])

    def zoff(t, half, p, k):
        a = zl[t] + 16 * half + 8 * k if t else zl0 + 64 * half + 16 * p + 8 * k
        return T.smu[:, a:a + 8], ("zl", t, half, p if t == 0 else 0)

    def window(t, p):
        if t == 0:
            return T.X0[:], ["X0"]
        return T.F[:, SL * p:SL * p + 512 + 256 * t], [("Fx", p)] + [("Fn", s, h, p) for s in range(t) for h in range(2)]

    def send(t, h):
        qz, qs = T["qz%d" % t], T["qzs%d" % t]
        lo, hi = 128 * h, 128 * h + 128

        def call(q):
            dst = T.cores[rank ^ STEP[t]]
            rid, pid = topo.addr(dst)[:2]
            every, n = topo.mask(core, dst), 2 * len(topo.engines(core, dst))
            name = "arr%d%d" % (t, h)
            gate("g", [("qz", t, h)], [])
            g.remote_dma(T["lz%d" % t][:, lo:hi].bitcast(dt.uint8), qz[:, lo:hi].bitcast(dt.uint8), T.sem[name], T.sem.sent, pid, rid, every)
            g.remote_dma(T["lzs%d" % t][:, lo:hi], qs[:, lo:hi], T.sem[name], T.sem.sent, pid, rid, every)
            count["sent"] = count.get("sent", 0) + n
            count[name] = n
            writer[("lz", t, h)] = (name, n, {})
        op({"g": (call, (300.0 + (800.0 if t + h == 0 else 0.0), 0, 0, 0))}, [("qz", t, h)], [("lz", t, h)], "send")

    def operands(t):
        for h in range(2):
            for p in range(4):
                (win, wk), (off, ko) = window(t, p), zoff(t, 0, p, h)
                a = 1024 * t + 256 * p + 128 * h
                copy(T.Ag[:, a:a + 128], win.indirect(off), 128, wk + [ko], [("A", t, h, p)], True)
        for h in range(2):
            lo, hi, z = 128 * h, 128 * h + 128, 1024 * t + 512 * h
            for p in range(4):
                (win, wk), (off, ko) = window(t, p), zoff(t, 1, p, h)
                a = 1024 * t + 256 * p + 128 * h
                out, in_, ag = T.Z[:, z + p:z + 512:4], win.indirect(off), T.Ag[:, a:a + 128]
                op({"v": (lambda e, out=out, in_=in_, ag=ag: e.tensor_tensor(out, in_, ag, OP.add), (50.0, 0, 128, 0))},
                   wk + [ko, ("A", t, h, p)], [("Z", t, h, p)])
            V(lambda e, lo=lo, hi=hi, z=z: e.quantize_mx(T["qz%d" % t][:, lo:hi], T["qzs%d" % t][:, lo:hi], T.Z[:, z:z + 512]), 150,
              [("Z", t, h, p) for p in range(4)], [("qz", t, h)])
            send(t, h)

    def bank(k):
        return T.ps[:, 512 * k:512 * k + 128]

    def mm(k, lq, ls, rq, rs, r):
        op({"t": (lambda e: e.matmul_mx(bank(k), lq, ls, rq, rs, True, True), (0.0, 150, 0, 0))}, r, [("bk", k)])

    s1 = [[small(1) for _ in range(2)] for _ in range(R)]
    s2 = [[small(1) for _ in range(2)] for _ in range(R)]

    def layer(t, h):
        lo, hi, z = 128 * h, 128 * h + 128, 1024 * t + 512 * h
        for b in range(4):
            mm(b, T.wq[:, 128 * b:128 * b + 128], T.wqs[:, 128 * b:128 * b + 128], T["lz%d" % t][:, lo:hi], T["lzs%d" % t][:, lo:hi], ["wq", ("lz", t, h)])
        for b in range(4):
            out = T.Hb[:, z + b:z + 512:4]
            op({"v": (lambda e, b=b, out=out: e.tensor_scalar(out, bank(b), 0.0, 0.015625, OP.max, OP.mult), (0.0, 128, 0, 0)),
                "s": (lambda e, b=b, out=out: e.activation(out, bank(b), AF.Relu, scale=0.015625), (0.0, 128, 0, 0))}, [("bk", b)], [("H", t, h, b)])
        V(lambda e: e.quantize_mx(T["qh%d" % t][:, lo:hi], T["qhs%d" % t][:, lo:hi], T.Hb[:, z:z + 512]), 150, [("H", t, h, b) for b in range(4)], [("qh", t, h)])

    def scores(t, h):
        lo, hi = 128 * h, 128 * h + 128
        q, s = T["qh%d" % t][:, lo:hi], T["qhs%d" % t][:, lo:hi]
        bs, bd = ((4, 5), (6, 7, 4, 5)) if h == 0 else ((0, 1), (2, 3, 6, 7))
        for k in range(2):
            mm(bs[k], T.up[:, 128 * k:128 * k + 128], T.ups[:, 128 * k:128 * k + 128], q, s, ["up", "ups", ("qh", t, h)])
        for k, name, out, sm in ((0, "sgw", T.sgw[:, 272 * t + 1 + lo:272 * t + 1 + hi], s1[t][h]), (1, "sg2", T.sg2[:, 256 * t + lo:256 * t + hi], s2[t][h])):
            op({"s": (lambda e, k=k, out=out, sm=sm: e.activation(out, bank(bs[k]), AF.Sign, bias=eps, accum_out=sm[0]), (20.0, 128, 0, 0))},
               [("bk", bs[k]), keps], [(name, t, h), sm[1]])
        for b in range(4):
            mm(bd[b], T.eq[:, 128 * b:128 * b + 128], T.eqs[:, 128 * b:128 * b + 128], q, s, [("eq", b), ("qh", t, h)])
            a = SL * b + 512 + 256 * t + lo
            copy(T.F[:, a:a + 128], bank(bd[b]), 128, [("bk", bd[b])], [("Fn", t, h, b)], False)

    def flags(c):
        return T.d1[:, 1536 * c + 45:1536 * c + 1534:48]

    def older(c, n=32):
        a = 1536 * c + 61
        return T.d1[:, a:a + 48 * n - 47:48]

    def backed(c):
        return T.d1[:, 1536 * c + 77:1536 * c + 1566:48]

    def result(c, k=None):
        return T.rs[:, 96 * c + 2:96 * c + 96:3] if k is None else T.rs[:, 96 * c + 48 * k + 2:96 * c + 48 * k + 48:3]

    def kres(c):
        return [("rs", c, 0), ("rs", c, 1)]

    V(lambda e: e.tensor_copy(older(0, 96), low), 96, [klow], [("old", 0), ("old", 1), ("old", 2)])
    for t, cs in ((1, (0,)), (2, (1, 3))):
        y, ky = scan([pick(T.m0r[:], km0r, *l) for l in (la16(t), lb16(t))])
        for c in cs:
            ts(backed(c), y, mcol, 1.0 / UNIT, OP.add, OP.mult, ky + [kmcol], [("bak", c, 0), ("bak", c, 1)])
    for c in (2, 4):
        ts(backed(c), L[:, 0:32], float(-SL), 1.0 / UNIT, OP.add, OP.mult, ["lists"], [("bak", c, 0), ("bak", c, 1)])

    def new(c, t, y, ky):
        ts(T.d0[:, 96 * c + 1:96 * c + 96:3], y, slot[t][0], 1.0 / UNIT, OP.add, OP.mult, ky + [slot[t][1], "d0"], [("n", c)])

    def where(c, t, rows):
        y, ky = scan(rows)
        o, ko, oa = small(32, "smu")
        ts(o, y, mlift, None, OP.add, None, ky + [kmlift], [ko])
        if c is not None:
            new(c, t, y, ky)
        return oa, ko

    def ident(t):
        return [(T.Dd[:, 512 * t + 256 * k:512 * t + 256 * k + 256], ["D%d" % t]) for k in range(2)]

    def find(t, l):
        return [pick(T.Dd[:, 512 * t:512 * t + 512], ["D%d" % t], *l2) for l2 in (la16(l), lb16(l))]

    rk = [small(1) for _ in range(R)]

    def limit(t):
        kb, kkb, _ = small(32)
        kt, kkt, ka = small(32)
        c8, kc8, _ = small(12)
        own, kown, _ = small(1)
        ts(kb, fr8, s2[t][0][0], s2[t][1][0], OP.add, OP.add, [kfr8, s2[t][0][1], s2[t][1][1]], [kkb])
        V(lambda e: e.transpose(kt, kb), 32, [kkb], [kkt])
        ts(own, gfr, s1[t][0][0], s1[t][1][0], OP.add, OP.add, [kgfr, s1[t][0][1], s1[t][1][1]], [kown])
        op({"s": (lambda e: e.activation(c8, T.smf[:, ka:ka + 12], AF.Sign, bias=own, scale=-1.0, accum_out=rk[t][0]), (20.0, 64, 0, 0))},
           [kkt, kown], [kc8, rk[t][1]])

    def limits(c, t):
        out, col = T.d0[:, 96 * c + 2:96 * c + 96:3], rk[t][0]
        op({"v": (lambda e: e.tensor_scalar(out, zero, col, None, OP.add), (0.0, 64, 0, 0)),
            "s": (lambda e: e.activation(out, zero, AF.Identity, bias=col), (0.0, 64, 0, 0))}, [kzero, rk[t][1], "d0"], [("lim", c)])

    def merge(c, t, off):
        oa, ko = off
        win, wk = T.sgw[:, 272 * t:272 * t + 257], [("pad", t), ("sgw", t, 0), ("sgw", t, 1), khalf1, ko]
        limits(c, t)
        parts = 2 if c in SPLIT else 1
        w = 256 // parts
        for k in range(2):
            i = used["gx"]
            used["gx"] = i + 1
            row = T.gx[:, 256 * i:256 * i + 256]
            for d in range(parts):
                o = oa + 16 * k + 8 * d
                out, in_ = T.gx[:, 256 * i + w * d:256 * i + w * d + w], win.indirect(T.smu[:, o:o + 16 // parts])
                op({"v": (lambda e, out=out, in_=in_: e.tensor_scalar(out, in_, 0.5, half1, OP.mult, OP.add), (50.0, 0, w, 0)),
                    "s": (lambda e, out=out, in_=in_: e.activation(out, in_, AF.Identity, bias=half1, scale=0.5), (65.0, 0, w, 0))}, wk, [("gx", i, d)])
            a = 1536 * c + 768 * k
            V(lambda e, a=a, row=row: e.tensor_tensor_scan(T.d1[:, a:a + 768:3], T.st[:, 256:512], row, 0.0, OP.add, OP.max),
              128, [("gx", i, d) for d in range(parts)] + [("st", 256)], [("flag", c, k)])
        for k in range(2):
            a, b = 1536 * c + 768 * k + 45, 96 * c + 48 * k
            V(lambda e, a=a, b=b: e.tensor_tensor_scan(T.rs[:, b:b + 48], T.d0[:, b:b + 48], T.d1[:, a:a + 753:16], 0.0, OP.min, OP.max),
              48, [("flag", c, k), ("old", c), ("bak", c, k), ("n", c), ("lim", c), "d0"], [("rs", c, k)])

    def merge_rows(c, t, rows):
        y, ky = scan(rows)
        limits(c, t)
        new(c, t, y, ky)
        ts(flags(c), y, mlift, None, OP.add, None, ky + [kmlift], [("flag", c, 0), ("flag", c, 1)])
        a, b = 1536 * c + 45, 96 * c
        V(lambda e: e.tensor_tensor_scan(T.rs[:, b:b + 96], T.d0[:, b:b + 96], T.d1[:, a:a + 1521:16], 0.0, OP.min, OP.max),
          96, [("flag", c, 0), ("flag", c, 1), ("old", c), ("bak", c, 0), ("bak", c, 1), ("n", c), ("lim", c), "d0"], kres(c))

    def settle(c, t, off):
        merge(c, t, off)
        for half in range(2):
            a = zl[t + 1] + 16 * half
            ts(T.smu[:, a:a + 16], result(c, half), UNIT, float(SL), OP.mult, OP.add, [("rs", c, half)], [("zl", t + 1, half, 0)])

    def before(c, b):
        V(lambda e: e.tensor_copy(older(c), result(b)), 32, kres(b), [("old", c)])

    inverse(0)
    operands(0)
    w01 = where(0, 0, find(0, 1))
    for p in range(4):
        out, in_ = T.F[:, SL * p:SL * p + 512], T.X0[:, p:2048:4]
        op({"g": (lambda e, out=out, in_=in_: e.affine_select(out, in_, [[0, 512]], OP.is_equal, 0.0, 0, 0), (170.0, 1024, 0, 0)),
            "v": (lambda e, out=out, in_=in_: e.tensor_copy(out, in_), (0.0, 256, 0, 0))}, ["X0"], [("Fx", p)])
    V(lambda e: e.quantize_mx(T.uq[:], T.uqs[:], T.uin[:]), 150, ["uin"], ["uq"])
    op({"v": (lambda e: e.tensor_copy(T.up[:].bitcast(dt.uint32), T.uq[:].bitcast(dt.uint32).indirect(U16)), (50.0, 0, 256, 0))},
       ["uq", (kU16, 0), (kU16, 1)], ["up"])
    copy(T.ups[:], T.uqs[:].indirect(U16), 256, ["uq", (kU16, 0), (kU16, 1)], ["ups"], True)
    for b in range(4):
        V(lambda e, b=b: e.quantize_mx(T.eq[:, 128 * b:128 * b + 128], T.eqs[:, 128 * b:128 * b + 128], T.ez[:, 4 - b:516 - b]), 150, ["ez"], [("eq", b)])
    layer(0, 0)
    scores(0, 0)
    layer(0, 1)
    scores(0, 1)
    limit(0)
    settle(0, 0, w01)

    operands(1)
    inverse(1)
    w12, w0 = where(3, 1, find(1, 2)), where(None, 0, ident(0))
    layer(1, 0)
    scores(1, 0)
    tt(T.val[:, 1:257], T.sgw[:, 1:257], T.jr1[:], OP.mult, [("sgw", 0, 0), ("sgw", 0, 1), "jr1"], ["val"], 256)
    regs = [pick(T.val[:, 0:257], ["val", ("pad", R)], T.smu[:, w0[0] + 16 * k:w0[0] + 16 * k + 16], w0[1]) for k in range(2)]
    g0 = 256 * regs[0][1][0][1]
    merge_rows(1, 0, [pick(T.gx[:, g0:g0 + 512], regs[0][1] + regs[1][1], *l) for l in (la16(2), lb16(2))])
    before(3, 1)
    layer(1, 1)
    scores(1, 1)
    limit(1)
    settle(3, 1, w12)

    operands(2)
    inverse(2)
    w1, w2 = [where(c, t, ident(t)) for c, t in ((4, 1), (5, 2))]
    merge_rows(2, 0, regs)
    before(4, 2)
    merge(4, 1, w1)
    before(5, 4)
    gm, kgm, _ = small(32)
    affine(gm, result(2), -1.0, 0.0, kres(2), [kgm])
    V(lambda e: e.quantize_mx(T.vq[:], T.vqs[:], T.vin[:]), 150, ["vin"], ["vq"])
    layer(2, 0)
    scores(2, 0)
    layer(2, 1)
    scores(2, 1)
    limit(2)
    ts(backed(5), gm, rk[2][0], -1.0, OP.max, OP.mult, [kgm, rk[2][1]], [("bak", 5, 0), ("bak", 5, 1)])
    settle(5, 2, w2)

    def store(q, sem, pairs, r, w):
        op({q: (lambda q: dmas(q, sem, pairs, r, w), (60.0 * len(pairs), 0, 0, 0))}, r, w, "dma")
        ops[-1]["busy"] = 320.0 if len(pairs) == 1 else 150.0

    for c in range(4):
        lo, hi = 128 * c, 128 * c + 128
        for p in range(4):
            (win, wk), (off, ko) = window(3, p), zoff(3, c // 2, p, c % 2)
            copy(T.Tt[:, 512 * c + p:512 * c + 512:4], win.indirect(off), 128, wk + [ko], [("T", c, p)], True)
        V(lambda e, lo=lo, hi=hi: e.quantize_mx(T.oq[:, lo:hi], T.oqs[:, lo:hi], T.Tt[:, 4 * lo:4 * hi]), 150, [("T", c, p) for p in range(4)], [("oq", c)])
        mm(4 + c, T.vq[:], T.vqs[:], T.oq[:, lo:hi], T.oqs[:, lo:hi], ["vq", ("oq", c)])
        copy(T.yo[:, lo:hi], bank(4 + c), 128, [("bk", 4 + c)], [("yo", c)], False)
        store("y", "so%d" % c, [(T.oc[:, 4 * lo:4 * hi], T.oq[:, lo:hi].bitcast(dt.uint8))], [("oq", c)], [("oc", c)])
        store("y", "sy%d" % c, [(T.y[:, lo:hi], T.yo[:, lo:hi])], [("yo", c)], [("y", c)])
    store("s", "sos", [(T.osc[4 * k:4 * k + 4, :], T.oqs[32 * k:32 * k + 4, :]) for k in range(4)], [("oq", c) for c in range(4)], ["osc"])
    pl, kpl, _ = small(32)
    ot, kot, oa = small(32)
    affine(pl, result(5), UNIT, float(SL), kres(5), [kpl])
    V(lambda e: e.transpose(ot, pl), 32, [kpl], [kot])
    store("y", "som", [(T.om[k:8:2, :], T.smf[:, oa + 16 * k:oa + 16 * k + 16]) for k in range(2)], [kot], ["om"])

    if "order" not in PLAN:
        PLAN["order"] = make_plan(ops, ready)
    for i, q in PLAN["order"]:
        emit(ops[i], q)
    for s in SEMAPHORES:
        if known["g"].get(s, 0) < count.get(s, 0):
            g.wait_ge(T.sem[s], count[s])
